import numpy as np
import ml_dtypes


def mxq(x, axis, fmt="e4m3"):
    dtype, down = {"e4m3": (ml_dtypes.float8_e4m3fn, 7), "e5m2": (ml_dtypes.float8_e5m2, 14)}[fmt]
    v = np.moveaxis(np.asarray(x, np.float32).astype(ml_dtypes.bfloat16).astype(np.float64), axis, -1)
    blocks = v.reshape(v.shape[:-1] + (-1, 32))
    amax = np.abs(blocks).max(-1, keepdims=True)
    byte = np.maximum(np.where(amax > 0, np.frexp(amax)[1] - 1 + 127, 0) - down, 1)
    scale = np.exp2(byte - 127.0)
    codes = (blocks / scale).astype(np.float32).astype(dtype).astype(np.float64)
    return np.moveaxis((codes * scale).reshape(v.shape), -1, axis)


WIDE = False


def mx_kscale(k):
    if not WIDE:
        return np.ones(k)
    levels = np.array([10, -10, 5, -5, 0])
    if k % 512:
        return np.exp2(np.random.permutation(np.resize(levels, k // 32))).repeat(32)
    a = np.empty((k // 512, 16))
    for p in range(k // 512):
        a[p, :8] = np.random.permutation(np.resize(levels, 8))
        for g in range(8):
            far = levels[np.abs(levels - a[p, g]) >= 10]
            a[p, g + 8] = far[np.random.randint(len(far))]
    return np.exp2(a.ravel()).repeat(32)


def f64(x):
    return np.asarray(x).astype(np.float64)


def striped(idx):
    return np.tile(idx.reshape(-1, 16).T, (8, 1)).astype(np.uint16)


def unstriped(offs):
    return offs[:16].T.reshape(-1).astype(np.int64)


E2M1 = np.array([0.0, 0.5, 1.0, 1.5, 2.0, 3.0, 4.0, 6.0, -0.0, -0.5, -1.0, -1.5, -2.0, -3.0, -4.0, -6.0])


def pack_weight(w, fmt):
    k, n = w.shape
    w = f64(np.asarray(w, np.float32).astype(ml_dtypes.bfloat16)).reshape(k // 32, 32, n)
    amax = np.abs(w).max(1)
    if fmt == "e4m3":
        byte = np.frexp(amax)[1] - 1 + 127 - 7
    else:
        mant, ex = np.frexp(amax / 6.0)
        byte = np.where(mant > 0.5, ex, ex - 1) + 127
    byte = np.clip(np.where(amax > 0, byte, 1), 1, 254)
    scaled = (w * np.exp2(127.0 - byte)[:, None, :]).reshape(k, n).astype(np.float32)
    by_word = np.ascontiguousarray(scaled.reshape(k // 512, 128, 4, n).transpose(0, 1, 3, 2))
    if fmt == "e4m3":
        words = by_word.astype(ml_dtypes.float8_e4m3fn).view(np.uint8)
    else:
        c = by_word.astype(ml_dtypes.float4_e2m1fn).view(np.uint8) & 0xF
        words = (c[..., 0::2] | (c[..., 1::2] << 4)).reshape(k // 512, 128, 2 * n)
    return np.ascontiguousarray(words), np.ascontiguousarray(byte.astype(np.uint8).reshape(k // 512, 16, n))


def unpack_weight(words, scales, fmt):
    g, _, n = scales.shape
    words = np.ascontiguousarray(words).reshape(g, 128, n, -1)
    if fmt == "e4m3":
        vals = words.view(ml_dtypes.float8_e4m3fn).astype(np.float64)
    else:
        nib = np.empty((g, 128, n, 4), np.uint8)
        nib[..., 0::2] = words & 0xF
        nib[..., 1::2] = words >> 4
        vals = E2M1[nib]
    vals = vals * np.repeat(np.exp2(scales.astype(np.float64) - 127.0), 8, axis=1)[..., None]
    return vals.transpose(0, 1, 3, 2).reshape(g * 512, n)


def relu(v):
    return np.maximum(v, 0.0)


K, T, E, C, N = 1024, 1024, 12, 256, 256
TOP = 3


def by_expert(wq, xq):
    return np.concatenate([wq[e].T @ xq[:, e * C:(e + 1) * C] for e in range(E)], axis=1)


def setup_inputs():
    n = np.random.standard_normal
    s = mx_kscale(K)[:, None]
    deal = np.repeat(np.arange(E), C).reshape(TOP, T)[:, np.random.permutation(T)]
    deal = np.take_along_axis(deal, np.argsort(np.random.rand(TOP, T), axis=0), axis=0)
    for _ in range(8):
        s_, t_ = np.random.permutation(T).reshape(2, -1); r = np.random.randint(TOP, size=T // 2); x, y = deal[r, s_].copy(), deal[r, t_].copy()
        ok = ~((deal[:, s_] == y).any(0) | (deal[:, t_] == x).any(0)); deal[r[ok], s_[ok]] = y[ok]; deal[r[ok], t_[ok]] = x[ok]
    order = np.lexsort((np.random.rand(TOP * T), deal.reshape(-1)))
    slot_token = order % T; pos = np.empty(TOP * T, np.int64); pos[order] = np.arange(TOP * T); pos = pos.reshape(TOP, T)
    g = np.random.uniform(0.5, 1.5, (TOP, T)); g = g / g.sum(0)
    w = [pack_weight(m, "e2m1") for m in n((E, K, N)) / np.sqrt(K) / s[None]]
    return {
        "xT": (n((K, T)) * s).astype(np.float32),
        "w_words": np.stack([m[0] for m in w]),
        "w_scales": np.stack([m[1] for m in w]),
        "b": (0.3 * n((N, E))).astype(np.float32),
        "gate": np.stack([np.tile(r, (N, 1)) for r in g]).astype(np.float32),
        "offs": striped(slot_token),
        "pos1": striped(pos[0]),
        "pos2": striped(pos[1]),
        "pos3": striped(pos[2]),
    }


def reference(xT, w_words, w_scales, b, gate, offs, pos1, pos2, pos3):
    idx = unstriped(offs)
    w = np.stack([unpack_weight(w_words[e], w_scales[e], "e2m1") for e in range(E)])
    xq = mxq(f64(xT)[:, idx], 0, "e4m3")
    y = by_expert(w, xq)
    y = relu(y + np.repeat(f64(b), C, axis=1))
    return sum(f64(gate[r]) * y[:, unstriped(p)] for r, p in enumerate((pos1, pos2, pos3)))

@@ -1,0 +1,222 @@
+from contextlib import ExitStack
+
+import concourse.mybir as mybir
+
+K, T, E, C, N = 1024, 1024, 12, 256, 256
+TOP = 3
+FLOPS = 2 * K * N * E * C
+
+F32 = mybir.dt.float32
+BF16 = mybir.dt.bfloat16
+I32 = mybir.dt.int32
+U32 = mybir.dt.uint32
+U16 = mybir.dt.uint16
+U8 = mybir.dt.uint8
+FP8X4 = mybir.dt.float8_e4m3fn_x4
+FP4X4 = mybir.dt.float4_e2m1fn_x4
+MULT, ADD, MAX = mybir.AluOpType.mult, mybir.AluOpType.add, mybir.AluOpType.max
+COPY = mybir.ActivationFunctionType.Copy
+RELU = mybir.ActivationFunctionType.Relu
+
+P = 128
+PASSES = K // 512
+SLOTS = E * C
+HALVES = N // P
+SHIFT = 4
+CUT = 896
+PIECE = 768
+CHUNKS = (((0, 512), (512, 256), (768, 256)), ((0, 512), (512, 512)))
+ON_SCALAR = ((192, 192, 96), (512, 416))
+
+
+def tile_moe_tk_lin_relu_kernel(tc, xT, w_words, w_scales, b, gate, offs, pos1, pos2, pos3, out):
+    nc = tc.nc
+    with ExitStack() as ctx:
+        lists = ctx.enter_context(tc.tile_pool(name="lists", bufs=1))
+        keep = ctx.enter_context(tc.tile_pool(name="keep", bufs=1))
+        late = ctx.enter_context(tc.tile_pool(name="late", bufs=1))
+        gathered = [ctx.enter_context(tc.tile_pool(name=f"gathered{a}", bufs=3 + a)) for a in range(PASSES)]
+        work = ctx.enter_context(tc.tile_pool(name="work", bufs=2))
+        psum = ctx.enter_context(tc.psum_pool(name="psum", bufs=8))
+
+        offs_t = lists.tile([P, SLOTS // 16], U16, name="offs_t")
+        pos_t = [lists.tile([P, T // 16], U16, name=f"pos{r}_t") for r in range(TOP)]
+
+        raw = [[keep.tile([P, 4, n], F32, name=f"raw{a}_{lo}") for lo, n in CHUNKS[a]] for a in range(PASSES)]
+        grouped = [
+            [keep.tile([P, n, 4], BF16, align_bytes=64, name=f"grouped0_{lo}") for lo, n in CHUNKS[0]],
+            [keep.tile([P, n, 4], BF16, align_bytes=64, name=f"grouped1_{lo}") for lo, n in CHUNKS[1]],
+        ]
+        codes = [keep.tile([P, T], U32, align_bytes=64, name=f"codes{a}") for a in range(PASSES)]
+        scales = late.tile([P, T], U8, align_bytes=64, name="scales")
+        g_codes = [{}, {}]
+        g_scales = [keep.tile([P, PIECE], U8, align_bytes=64, name=f"g_scales_{c}") for c in range(SLOTS // PIECE)]
+        g_scales1 = [keep.tile([P, PIECE], U8, align_bytes=64, name=f"g_scales1_{c}") for c in range(SLOTS // PIECE)]
+        w_t = keep.tile([P, E * PASSES, 2 * N], U8, align_bytes=64, name="w_t")
+        ws_t = keep.tile([P, E * PASSES, N], U8, align_bytes=64, name="ws_t")
+        b_t = keep.tile([P, HALVES, E], F32, name="b_t")
+        y = [keep.tile([P, SLOTS], F32, name=f"y{h}") for h in range(HALVES)]
+
+        nc.gpsimd.memset(scales[:], 0)
+        nc.gpsimd.memset(ws_t[:].rearrange("p g n -> p (g n)").bitcast(I32), 0)
+        for c in range(SLOTS // PIECE):
+            nc.gpsimd.memset(g_scales1[c][:].bitcast(I32), 0)
+
+        def load_x(a, c):
+            lo, n = CHUNKS[a][c]
+            src = xT[512 * a : 512 * (a + 1), lo : lo + n].rearrange("(p j) w -> p j w", j=4)
+            nc.sync.dma_start(out=raw[a][c][:], in_=src)
+
+        load_x(0, 0)
+        nc.sync.dma_start(offs_t[:], offs)
+        load_x(0, 1)
+        load_x(0, 2)
+        load_x(1, 0)
+        load_x(1, 1)
+        w_src = w_words.bitcast(I32).rearrange("e a p n -> p (e a) n")
+        ws_src = w_scales.bitcast(I32)
+        for q in range(4):
+            nc.sync.dma_start(
+                out=ws_t[32 * q : 32 * q + 4].bitcast(I32),
+                in_=ws_src[:, :, 4 * q : 4 * q + 4, :].rearrange("e a r n -> r (e a) n"),
+            )
+        for s in range(3):
+            g = slice(8 * s, 8 * s + 8)
+            nc.sync.dma_start(out=w_t[:, g, :].bitcast(I32), in_=w_src[:, g, :])
+        nc.sync.dma_start(out=b_t[:], in_=b.rearrange("(h p) e -> p h e", p=P))
+        for r, src in enumerate((pos1, pos2, pos3)):
+            nc.sync.dma_start(pos_t[r][:], src)
+
+        def cast(engine, a, c, lo, hi):
+            dst = grouped[a][c][:, lo:hi, :].rearrange("p (c i) j -> p c j i", i=4)
+            src = raw[a][c][:, :, lo:hi].rearrange("p j (c i) -> p c j i", i=4)
+            if engine == "v":
+                nc.vector.tensor_copy(out=dst, in_=src)
+            else:
+                nc.scalar.activation(dst, src, COPY)
+
+        def quantize(a, c):
+            lo, n = CHUNKS[a][c]
+            nc.vector.quantize_mx(
+                out=codes[a][:, lo : lo + n].bitcast(FP8X4),
+                scales=scales[SHIFT * a : P, lo : lo + n],
+                in_=grouped[a][c][:].rearrange("p w j -> p (w j)"),
+            )
+
+        for a in range(PASSES):
+            for c in range(len(CHUNKS[a])):
+                n, cut = CHUNKS[a][c][1], ON_SCALAR[a][c]
+                cast("s", a, c, 0, cut)
+                if cut < n:
+                    cast("v", a, c, cut, n)
+                if a == 0:
+                    quantize(a, c)
+
+        def gather_codes(a, lo, hi):
+            c, o = divmod(lo, PIECE)
+            if o == 0:
+                if (a, c) == (0, 3):
+                    g_codes[a][c] = late.tile([P, PIECE], U32, align_bytes=64, name="scales")
+                else:
+                    g_codes[a][c] = gathered[a].tile([P, PIECE], U32, align_bytes=64, name=f"g_codes{a}")
+            nc.vector.tensor_copy(g_codes[a][c][:, o : o + hi - lo], codes[a][:].indirect(offs_t[:, lo // 16 : hi // 16]))
+
+        def gather_scales(c):
+            nc.vector.tensor_copy(g_scales[c][:], scales[:].indirect(offs_t[:, PIECE * c // 16 : PIECE * (c + 1) // 16]))
+            nc.sync.dma_start(out=g_scales1[c][0 : P - SHIFT, :].bitcast(I32), in_=g_scales[c][SHIFT:P, :].bitcast(I32))
+
+        def one_pass(ps, o, e, h, s, a, first=1):
+            g = e * PASSES + a
+            c, at = divmod(e * C + s * P, PIECE)
+            nc.tensor.matmul_mx(
+                out=ps[:, o : o + P],
+                lhsT=w_t[:, g, 2 * P * h : 2 * P * (h + 1)].bitcast(FP4X4),
+                lhsT_scale=ws_t[:, g, P * h : P * (h + 1)],
+                rhs=g_codes[a][c][:, at : at + P].bitcast(FP8X4),
+                rhs_scale=(g_scales, g_scales1)[a][c][:, at : at + P],
+                start=(a == first),
+                stop=(a != first),
+            )
+
+        def half(e, h):
+            ps = psum.tile([P, C], F32, name="ps")
+            for s in range(2):
+                for a in (1, 0):
+                    one_pass(ps, s * P, e, h, s, a)
+            nc.scalar.activation(y[h][:, e * C : (e + 1) * C], ps[:], RELU, bias=b_t[:, h, e : e + 1])
+
+        def expert(e):
+            for h in range(HALVES):
+                half(e, h)
+
+        def words(a, lo, n):
+            gather_codes(a, lo, lo + n)
+
+        for c in range(3):
+            words(0, PIECE * c, PIECE)
+        for c in range(len(CHUNKS[1])):
+            quantize(1, c)
+        gather_scales(0)
+        gather_scales(1)
+        words(1, 0, PIECE)
+        for e in range(3):
+            expert(e)
+        gather_scales(2)
+        words(1, PIECE, PIECE)
+        for e in range(3, 6):
+            expert(e)
+        gather_scales(3)
+        words(1, 2 * PIECE, PIECE)
+        for e in range(6, 9):
+            half(e, 0)
+        words(0, 3 * PIECE, PIECE)
+        ends = []
+        for s in range(2):
+            ps = psum.tile([P, C], F32, name="ps")
+            one_pass(ps, 0, E - 1, 0, s, 0, first=0)
+            ends.append(ps)
+        for e in range(9, E - 1):
+            words(1, e * C, C)
+            half(e, 0)
+        words(1, (E - 1) * C, C)
+        for s in range(2):
+            one_pass(ends[s], 0, E - 1, 0, s, 1, first=0)
+            at = (E - 1) * C + s * P
+            nc.scalar.activation(y[0][:, at : at + P], ends[s][:, 0:P], RELU, bias=b_t[:, 0, E - 1 : E])
+        for e in range(6, E):
+            half(e, 1)
+
+        gate_t = []
+        for r, a in enumerate((1, 1, 0)):
+            gate_t.append(gathered[a].tile([P, T], F32, align_bytes=64, name=f"g_codes{a}"))
+            nc.sync.dma_start(out=gate_t[r][:], in_=gate[r, 0:P, :])
+
+        def product(h, r, lo, hi):
+            prod = work.tile([P, hi - lo], F32, name=f"prod{r}_{hi - lo}")
+            nc.vector.tensor_tensor(prod[:], y[h][:].indirect(pos_t[r][:, lo // 16 : hi // 16]), gate_t[r][:, lo:hi], MULT)
+            return prod
+
+        def add(into, other):
+            nc.vector.tensor_tensor(into[:], into[:], other[:], ADD)
+
+        def store(h, lo, hi, total):
+            nc.sync.dma_start(out=out[h * P : (h + 1) * P, lo:hi], in_=total[:])
+
+        a0 = product(0, 0, 0, T)
+        a1 = product(0, 1, 0, T)
+        a2 = product(0, 2, 0, T)
+        add(a0, a1)
+        b0 = product(1, 0, 0, CUT)
+        add(a0, a2)
+        store(0, 0, T, a0)
+        b1 = product(1, 1, 0, CUT)
+        b2 = product(1, 2, 0, CUT)
+        add(b0, b1)
+        c0 = product(1, 0, CUT, T)
+        add(b0, b2)
+        store(1, 0, CUT, b0)
+        c1 = product(1, 1, CUT, T)
+        c2 = product(1, 2, CUT, T)
+        add(c0, c1)
+        add(c0, c2)
+        store(1, CUT, T, c0)

@@ -1,6 +1,7 @@
 from contextlib import ExitStack
 
 import concourse.mybir as mybir
+from concourse.masks import make_identity
 
 K, T, E, C, N = 1024, 1024, 12, 256, 256
 TOP = 3
@@ -23,7 +24,7 @@ PASSES = K // 512
 SLOTS = E * C
 HALVES = N // P
 SHIFT = 4
-CUT = 896
+CUT = 768
 PIECE = 768
 CHUNKS = (((0, 512), (512, 256), (768, 256)), ((0, 512), (512, 512)))
 ON_SCALAR = ((192, 192, 96), (512, 416))
@@ -36,8 +37,8 @@ def tile_moe_tk_lin_relu_kernel(tc, xT, w_words, w_scales, b, gate, offs, pos1, 
         keep = ctx.enter_context(tc.tile_pool(name="keep", bufs=1))
         late = ctx.enter_context(tc.tile_pool(name="late", bufs=1))
         gathered = [ctx.enter_context(tc.tile_pool(name=f"gathered{a}", bufs=3 + a)) for a in range(PASSES)]
-        work = ctx.enter_context(tc.tile_pool(name="work", bufs=2))
-        psum = ctx.enter_context(tc.psum_pool(name="psum", bufs=8))
+        psum = ctx.enter_context(tc.psum_pool(name="psum", bufs=6))
+        turns = ctx.enter_context(tc.psum_pool(name="turns", bufs=1))
 
         offs_t = lists.tile([P, SLOTS // 16], U16, name="offs_t")
         pos_t = [lists.tile([P, T // 16], U16, name=f"pos{r}_t") for r in range(TOP)]
@@ -56,6 +57,9 @@ def tile_moe_tk_lin_relu_kernel(tc, xT, w_words, w_scales, b, gate, offs, pos1, 
         ws_t = keep.tile([P, E * PASSES, N], U8, align_bytes=64, name="ws_t")
         b_t = keep.tile([P, HALVES, E], F32, name="b_t")
         y = [keep.tile([P, SLOTS], F32, name=f"y{h}") for h in range(HALVES)]
+
+        ident = keep.tile([P, P], F32, name="ident")
+        make_identity(nc, ident[:])
 
         nc.gpsimd.memset(scales[:], 0)
         nc.gpsimd.memset(ws_t[:].rearrange("p g n -> p (g n)").bitcast(I32), 0)
@@ -86,6 +90,9 @@ def tile_moe_tk_lin_relu_kernel(tc, xT, w_words, w_scales, b, gate, offs, pos1, 
         nc.sync.dma_start(out=b_t[:], in_=b.rearrange("(h p) e -> p h e", p=P))
         for r, src in enumerate((pos1, pos2, pos3)):
             nc.sync.dma_start(pos_t[r][:], src)
+        gate_t = [keep.tile([P, T], F32, name=f"gate{r}") for r in range(TOP)]
+        for r in range(TOP):
+            nc.sync.dma_start(out=gate_t[r][:], in_=gate[r, 0:P, :])
 
         def cast(engine, a, c, lo, hi):
             dst = grouped[a][c][:, lo:hi, :].rearrange("p (c i) j -> p c j i", i=4)
@@ -186,37 +193,41 @@ def tile_moe_tk_lin_relu_kernel(tc, xT, w_words, w_scales, b, gate, offs, pos1, 
         for e in range(6, E):
             half(e, 1)
 
-        gate_t = []
-        for r, a in enumerate((1, 1, 0)):
-            gate_t.append(gathered[a].tile([P, T], F32, align_bytes=64, name=f"g_codes{a}"))
-            nc.sync.dma_start(out=gate_t[r][:], in_=gate[r, 0:P, :])
-
         def product(h, r, lo, hi):
-            prod = work.tile([P, hi - lo], F32, name=f"prod{r}_{hi - lo}")
+            prod = keep.tile([P, hi - lo], F32, name=f"prod{r}_{h}_{lo}")
             nc.vector.tensor_tensor(prod[:], y[h][:].indirect(pos_t[r][:, lo // 16 : hi // 16]), gate_t[r][:, lo:hi], MULT)
             return prod
 
         def add(into, other):
             nc.vector.tensor_tensor(into[:], into[:], other[:], ADD)
 
-        def store(h, lo, hi, total):
-            nc.sync.dma_start(out=out[h * P : (h + 1) * P, lo:hi], in_=total[:])
+        def store(h, lo, hi, total, queue):
+            queue.dma_start(out=out[h * P : (h + 1) * P, lo:hi], in_=total[:])
 
-        a0 = product(0, 0, 0, T)
-        a1 = product(0, 1, 0, T)
-        a2 = product(0, 2, 0, T)
-        add(a0, a1)
-        b0 = product(1, 0, 0, CUT)
-        add(a0, a2)
-        store(0, 0, T, a0)
-        b1 = product(1, 1, 0, CUT)
-        b2 = product(1, 2, 0, CUT)
-        add(b0, b1)
+        def summed_on_tensor(h, lo, hi):
+            n = hi - lo
+            prods = [product(h, r, lo, hi) for r in range(TOP)]
+            turned = turns.tile([P, n], F32, name="turned")
+            for r in range(TOP):
+                for o in range(0, n, P):
+                    first, last = (r, o) == (0, 0), (r, o) == (TOP - 1, n - P)
+                    nc.tensor.matmul(turned[:, o : o + P], prods[r][:, o : o + P], ident[:], start=first, stop=last, is_transpose=True)
+            by_token = keep.tile([P, n], F32, name=f"by_token{h}_{lo}")
+            nc.scalar.copy(by_token[:], turned[:])
+            back = turns.tile([P, n], F32, name="back")
+            for o in range(0, n, P):
+                nc.tensor.transpose(back[:, o : o + P], by_token[:, o : o + P], ident[:])
+            total = keep.tile([P, n], F32, name=f"total{h}_{lo}")
+            nc.scalar.copy(total[:], back[:])
+            store(h, lo, hi, total, nc.scalar)
+
+        summed_on_tensor(0, 0, 512)
+        summed_on_tensor(0, 512, T)
+        summed_on_tensor(1, 0, 512)
+        summed_on_tensor(1, 512, CUT)
         c0 = product(1, 0, CUT, T)
-        add(b0, b2)
-        store(1, 0, CUT, b0)
         c1 = product(1, 1, CUT, T)
         c2 = product(1, 2, CUT, T)
         add(c0, c1)
         add(c0, c2)
-        store(1, CUT, T, c0)
+        store(1, CUT, T, c0, nc.sync)

@@ -26,8 +26,8 @@ HALVES = N // P
 SHIFT = 4
 CUT = 768
 PIECE = 768
-CHUNKS = (((0, 512), (512, 256), (768, 256)), ((0, 512), (512, 512)))
-ON_SCALAR = ((192, 192, 96), (512, 416))
+CHUNKS = (((0, 256), (256, 256), (512, 256), (768, 128), (896, 128)), ((0, 512), (512, 512)))
+ON_SCALAR = ((96, 96, 96, 48, 48), (512, 512))
 
 
 def tile_moe_tk_lin_relu_kernel(tc, xT, w_words, w_scales, b, gate, offs, pos1, pos2, pos3, out):
@@ -35,10 +35,15 @@ def tile_moe_tk_lin_relu_kernel(tc, xT, w_words, w_scales, b, gate, offs, pos1, 
     with ExitStack() as ctx:
         lists = ctx.enter_context(tc.tile_pool(name="lists", bufs=1))
         keep = ctx.enter_context(tc.tile_pool(name="keep", bufs=1))
-        late = ctx.enter_context(tc.tile_pool(name="late", bufs=1))
-        gathered = [ctx.enter_context(tc.tile_pool(name=f"gathered{a}", bufs=3 + a)) for a in range(PASSES)]
-        psum = ctx.enter_context(tc.psum_pool(name="psum", bufs=6))
-        turns = ctx.enter_context(tc.psum_pool(name="turns", bufs=1))
+        psum = ctx.enter_context(tc.psum_pool(name="psum", bufs=1))
+        taken = []
+
+        def bank(number, width):
+            return psum.tile([P, width], F32, name=f"bank{number}")
+
+        def next_bank():
+            taken.append(len(taken) % 8)
+            return bank(taken[-1], C)
 
         offs_t = lists.tile([P, SLOTS // 16], U16, name="offs_t")
         pos_t = [lists.tile([P, T // 16], U16, name=f"pos{r}_t") for r in range(TOP)]
@@ -49,7 +54,7 @@ def tile_moe_tk_lin_relu_kernel(tc, xT, w_words, w_scales, b, gate, offs, pos1, 
             [keep.tile([P, n, 4], BF16, align_bytes=64, name=f"grouped1_{lo}") for lo, n in CHUNKS[1]],
         ]
         codes = [keep.tile([P, T], U32, align_bytes=64, name=f"codes{a}") for a in range(PASSES)]
-        scales = late.tile([P, T], U8, align_bytes=64, name="scales")
+        scales = keep.tile([P, T], U8, align_bytes=64, name="scales")
         g_codes = [{}, {}]
         g_scales = [keep.tile([P, PIECE], U8, align_bytes=64, name=f"g_scales_{c}") for c in range(SLOTS // PIECE)]
         g_scales1 = [keep.tile([P, PIECE], U8, align_bytes=64, name=f"g_scales1_{c}") for c in range(SLOTS // PIECE)]
@@ -61,10 +66,10 @@ def tile_moe_tk_lin_relu_kernel(tc, xT, w_words, w_scales, b, gate, offs, pos1, 
         ident = keep.tile([P, P], F32, name="ident")
         make_identity(nc, ident[:])
 
-        nc.gpsimd.memset(scales[:], 0)
-        nc.gpsimd.memset(ws_t[:].rearrange("p g n -> p (g n)").bitcast(I32), 0)
+        nc.vector.memset(scales[:].bitcast(I32), 0)
+        nc.vector.memset(ws_t[:].rearrange("p g n -> p (g n)").bitcast(I32), 0)
         for c in range(SLOTS // PIECE):
-            nc.gpsimd.memset(g_scales1[c][:].bitcast(I32), 0)
+            nc.vector.memset(g_scales1[c][:].bitcast(I32), 0)
 
         def load_x(a, c):
             lo, n = CHUNKS[a][c]
@@ -73,8 +78,8 @@ def tile_moe_tk_lin_relu_kernel(tc, xT, w_words, w_scales, b, gate, offs, pos1, 
 
         load_x(0, 0)
         nc.sync.dma_start(offs_t[:], offs)
-        load_x(0, 1)
-        load_x(0, 2)
+        for c in range(1, len(CHUNKS[0])):
+            load_x(0, c)
         load_x(1, 0)
         load_x(1, 1)
         w_src = w_words.bitcast(I32).rearrange("e a p n -> p (e a) n")
@@ -122,10 +127,7 @@ def tile_moe_tk_lin_relu_kernel(tc, xT, w_words, w_scales, b, gate, offs, pos1, 
         def gather_codes(a, lo, hi):
             c, o = divmod(lo, PIECE)
             if o == 0:
-                if (a, c) == (0, 3):
-                    g_codes[a][c] = late.tile([P, PIECE], U32, align_bytes=64, name="scales")
-                else:
-                    g_codes[a][c] = gathered[a].tile([P, PIECE], U32, align_bytes=64, name=f"g_codes{a}")
+                g_codes[a][c] = keep.tile([P, PIECE], U32, align_bytes=64, name=f"g_codes{a}_{c}")
             nc.vector.tensor_copy(g_codes[a][c][:, o : o + hi - lo], codes[a][:].indirect(offs_t[:, lo // 16 : hi // 16]))
 
         def gather_scales(c):
@@ -146,7 +148,7 @@ def tile_moe_tk_lin_relu_kernel(tc, xT, w_words, w_scales, b, gate, offs, pos1, 
             )
 
         def half(e, h):
-            ps = psum.tile([P, C], F32, name="ps")
+            ps = next_bank()
             for s in range(2):
                 for a in (1, 0):
                     one_pass(ps, s * P, e, h, s, a)
@@ -159,36 +161,34 @@ def tile_moe_tk_lin_relu_kernel(tc, xT, w_words, w_scales, b, gate, offs, pos1, 
         def words(a, lo, n):
             gather_codes(a, lo, lo + n)
 
-        for c in range(3):
+        for c in range(4):
             words(0, PIECE * c, PIECE)
         for c in range(len(CHUNKS[1])):
             quantize(1, c)
-        gather_scales(0)
-        gather_scales(1)
+        for c in range(3):
+            gather_scales(c)
         words(1, 0, PIECE)
         for e in range(3):
             expert(e)
-        gather_scales(2)
+        gather_scales(3)
         words(1, PIECE, PIECE)
         for e in range(3, 6):
             expert(e)
-        gather_scales(3)
         words(1, 2 * PIECE, PIECE)
         for e in range(6, 9):
             half(e, 0)
-        words(0, 3 * PIECE, PIECE)
         ends = []
         for s in range(2):
-            ps = psum.tile([P, C], F32, name="ps")
+            ps = next_bank()
             one_pass(ps, 0, E - 1, 0, s, 0, first=0)
             ends.append(ps)
         for e in range(9, E - 1):
             words(1, e * C, C)
             half(e, 0)
-        words(1, (E - 1) * C, C)
         for s in range(2):
-            one_pass(ends[s], 0, E - 1, 0, s, 1, first=0)
             at = (E - 1) * C + s * P
+            words(1, at, P)
+            one_pass(ends[s], 0, E - 1, 0, s, 1, first=0)
             nc.scalar.activation(y[0][:, at : at + P], ends[s][:, 0:P], RELU, bias=b_t[:, 0, E - 1 : E])
         for e in range(6, E):
             half(e, 1)
@@ -204,27 +204,25 @@ def tile_moe_tk_lin_relu_kernel(tc, xT, w_words, w_scales, b, gate, offs, pos1, 
         def store(h, lo, hi, total, queue):
             queue.dma_start(out=out[h * P : (h + 1) * P, lo:hi], in_=total[:])
 
-        def summed_on_tensor(h, lo, hi):
+        def summed_on_tensor(piece, h, lo, hi):
             n = hi - lo
             prods = [product(h, r, lo, hi) for r in range(TOP)]
-            turned = turns.tile([P, n], F32, name="turned")
+            turned = bank(1 + piece % 2, n)
             for r in range(TOP):
                 for o in range(0, n, P):
                     first, last = (r, o) == (0, 0), (r, o) == (TOP - 1, n - P)
                     nc.tensor.matmul(turned[:, o : o + P], prods[r][:, o : o + P], ident[:], start=first, stop=last, is_transpose=True)
             by_token = keep.tile([P, n], F32, name=f"by_token{h}_{lo}")
             nc.scalar.copy(by_token[:], turned[:])
-            back = turns.tile([P, n], F32, name="back")
+            back = bank(3 + piece % 2, n)
             for o in range(0, n, P):
                 nc.tensor.transpose(back[:, o : o + P], by_token[:, o : o + P], ident[:])
             total = keep.tile([P, n], F32, name=f"total{h}_{lo}")
             nc.scalar.copy(total[:], back[:])
             store(h, lo, hi, total, nc.scalar)
 
-        summed_on_tensor(0, 0, 512)
-        summed_on_tensor(0, 512, T)
-        summed_on_tensor(1, 0, 512)
-        summed_on_tensor(1, 512, CUT)
+        for piece, (h, lo, hi) in enumerate(((0, 0, 512), (0, 512, T), (1, 0, 384), (1, 384, 640), (1, 640, CUT))):
+            summed_on_tensor(piece, h, lo, hi)
         c0 = product(1, 0, CUT, T)
         c1 = product(1, 1, CUT, T)
         c2 = product(1, 2, CUT, T)

@@ -125,14 +125,16 @@ def tile_moe_tk_lin_relu_kernel(tc, xT, w_words, w_scales, b, gate, offs, pos1, 
                     quantize(a, c)
 
         def gather_codes(a, lo, hi):
-            c, o = divmod(lo, PIECE)
-            if o == 0:
-                g_codes[a][c] = keep.tile([P, PIECE], U32, align_bytes=64, name=f"g_codes{a}_{c}")
-            nc.vector.tensor_copy(g_codes[a][c][:, o : o + hi - lo], codes[a][:].indirect(offs_t[:, lo // 16 : hi // 16]))
+            held = (a, lo) == (0, SLOTS - C)
+            dst = keep.tile([P, hi - lo], U32, align_bytes=64, name="grouped1_512" if held else f"g_codes{a}_{lo}")
+            nc.vector.tensor_copy(dst[:], codes[a][:].indirect(offs_t[:, lo // 16 : hi // 16]))
+            for at in range(lo, hi, P):
+                g_codes[a][at] = dst[:, at - lo : at - lo + P]
 
         def gather_scales(c):
             nc.vector.tensor_copy(g_scales[c][:], scales[:].indirect(offs_t[:, PIECE * c // 16 : PIECE * (c + 1) // 16]))
-            nc.sync.dma_start(out=g_scales1[c][0 : P - SHIFT, :].bitcast(I32), in_=g_scales[c][SHIFT:P, :].bitcast(I32))
+            for q in range(0, P, 32):
+                nc.sync.dma_start(out=g_scales1[c][q : q + 4, :].bitcast(I32), in_=g_scales[c][q + SHIFT : q + SHIFT + 4, :].bitcast(I32))
 
         def one_pass(ps, o, e, h, s, a, first=1):
             g = e * PASSES + a
@@ -141,14 +143,13 @@ def tile_moe_tk_lin_relu_kernel(tc, xT, w_words, w_scales, b, gate, offs, pos1, 
                 out=ps[:, o : o + P],
                 lhsT=w_t[:, g, 2 * P * h : 2 * P * (h + 1)].bitcast(FP4X4),
                 lhsT_scale=ws_t[:, g, P * h : P * (h + 1)],
-                rhs=g_codes[a][c][:, at : at + P].bitcast(FP8X4),
+                rhs=g_codes[a][e * C + s * P].bitcast(FP8X4),
                 rhs_scale=(g_scales, g_scales1)[a][c][:, at : at + P],
                 start=(a == first),
                 stop=(a != first),
             )
 
-        def half(e, h):
-            ps = next_bank()
+        def half(e, h, ps):
             for s in range(2):
                 for a in (1, 0):
                     one_pass(ps, s * P, e, h, s, a)
@@ -156,15 +157,17 @@ def tile_moe_tk_lin_relu_kernel(tc, xT, w_words, w_scales, b, gate, offs, pos1, 
 
         def expert(e):
             for h in range(HALVES):
-                half(e, h)
+                half(e, h, next_bank())
 
         def words(a, lo, n):
             gather_codes(a, lo, lo + n)
 
-        for c in range(4):
+        for c in range(3):
             words(0, PIECE * c, PIECE)
+        words(0, 3 * PIECE, PIECE - C)
         for c in range(len(CHUNKS[1])):
             quantize(1, c)
+        words(0, SLOTS - C, C)
         for c in range(3):
             gather_scales(c)
         words(1, 0, PIECE)
@@ -174,9 +177,9 @@ def tile_moe_tk_lin_relu_kernel(tc, xT, w_words, w_scales, b, gate, offs, pos1, 
         words(1, PIECE, PIECE)
         for e in range(3, 6):
             expert(e)
-        words(1, 2 * PIECE, PIECE)
         for e in range(6, 9):
-            half(e, 0)
+            words(1, e * C, C)
+            half(e, 0, next_bank())
         ends = []
         for s in range(2):
             ps = next_bank()
@@ -184,22 +187,20 @@ def tile_moe_tk_lin_relu_kernel(tc, xT, w_words, w_scales, b, gate, offs, pos1, 
             ends.append(ps)
         for e in range(9, E - 1):
             words(1, e * C, C)
-            half(e, 0)
+            half(e, 0, next_bank())
         for s in range(2):
             at = (E - 1) * C + s * P
             words(1, at, P)
             one_pass(ends[s], 0, E - 1, 0, s, 1, first=0)
             nc.scalar.activation(y[0][:, at : at + P], ends[s][:, 0:P], RELU, bias=b_t[:, 0, E - 1 : E])
+        last_four = taken[-2:] + taken[-4:-2]
         for e in range(6, E):
-            half(e, 1)
+            half(e, 1, bank(last_four[(e - 6) % 4], C))
 
         def product(h, r, lo, hi):
             prod = keep.tile([P, hi - lo], F32, name=f"prod{r}_{h}_{lo}")
             nc.vector.tensor_tensor(prod[:], y[h][:].indirect(pos_t[r][:, lo // 16 : hi // 16]), gate_t[r][:, lo:hi], MULT)
             return prod
-
-        def add(into, other):
-            nc.vector.tensor_tensor(into[:], into[:], other[:], ADD)
 
         def store(h, lo, hi, total, queue):
             queue.dma_start(out=out[h * P : (h + 1) * P, lo:hi], in_=total[:])
@@ -207,14 +208,14 @@ def tile_moe_tk_lin_relu_kernel(tc, xT, w_words, w_scales, b, gate, offs, pos1, 
         def summed_on_tensor(piece, h, lo, hi):
             n = hi - lo
             prods = [product(h, r, lo, hi) for r in range(TOP)]
-            turned = bank(1 + piece % 2, n)
+            turned = bank(last_four[1 - max(piece - 1, 0) % 2], n)
             for r in range(TOP):
                 for o in range(0, n, P):
                     first, last = (r, o) == (0, 0), (r, o) == (TOP - 1, n - P)
                     nc.tensor.matmul(turned[:, o : o + P], prods[r][:, o : o + P], ident[:], start=first, stop=last, is_transpose=True)
             by_token = keep.tile([P, n], F32, name=f"by_token{h}_{lo}")
             nc.scalar.copy(by_token[:], turned[:])
-            back = bank(3 + piece % 2, n)
+            back = bank(last_four[0 if piece == 0 else 2 + piece % 2], n)
             for o in range(0, n, P):
                 nc.tensor.transpose(back[:, o : o + P], by_token[:, o : o + P], ident[:])
             total = keep.tile([P, n], F32, name=f"total{h}_{lo}")
@@ -223,9 +224,12 @@ def tile_moe_tk_lin_relu_kernel(tc, xT, w_words, w_scales, b, gate, offs, pos1, 
 
         for piece, (h, lo, hi) in enumerate(((0, 0, 512), (0, 512, T), (1, 0, 384), (1, 384, 640), (1, 640, CUT))):
             summed_on_tensor(piece, h, lo, hi)
+        mid = (CUT + T) // 2
         c0 = product(1, 0, CUT, T)
         c1 = product(1, 1, CUT, T)
-        c2 = product(1, 2, CUT, T)
-        add(c0, c1)
-        add(c0, c2)
-        store(1, CUT, T, c0, nc.sync)
+        left = product(1, 2, CUT, mid)
+        nc.vector.tensor_tensor(c0[:], c0[:], c1[:], ADD)
+        right = product(1, 2, mid, T)
+        nc.vector.tensor_tensor(c1[:, : mid - CUT], c0[:, : mid - CUT], left[:], ADD)
+        nc.vector.tensor_tensor(c1[:, mid - CUT :], c0[:, mid - CUT :], right[:], ADD)
+        store(1, CUT, T, c1, nc.sync)

@@ -27,7 +27,7 @@ SHIFT = 4
 CUT = 768
 PIECE = 768
 CHUNKS = (((0, 256), (256, 256), (512, 256), (768, 128), (896, 128)), ((0, 512), (512, 512)))
-ON_SCALAR = ((96, 96, 96, 48, 48), (512, 512))
+ON_SCALAR = ((96, 96, 112, 64, 48), (512, 512))
 
 
 def tile_moe_tk_lin_relu_kernel(tc, xT, w_words, w_scales, b, gate, offs, pos1, pos2, pos3, out):
@@ -77,9 +77,9 @@ def tile_moe_tk_lin_relu_kernel(tc, xT, w_words, w_scales, b, gate, offs, pos1, 
             nc.sync.dma_start(out=raw[a][c][:], in_=src)
 
         load_x(0, 0)
-        nc.sync.dma_start(offs_t[:], offs)
         for c in range(1, len(CHUNKS[0])):
             load_x(0, c)
+        nc.sync.dma_start(offs_t[:], offs)
         load_x(1, 0)
         load_x(1, 1)
         w_src = w_words.bitcast(I32).rearrange("e a p n -> p (e a) n")

@@ -25,7 +25,7 @@ SLOTS = E * C
 HALVES = N // P
 SHIFT = 4
 CUT = 768
-PIECE = 768
+PIECE = 1024
 CHUNKS = (((0, 256), (256, 256), (512, 256), (768, 128), (896, 128)), ((0, 512), (512, 512)))
 ON_SCALAR = ((96, 96, 112, 64, 48), (512, 512))
 
@@ -36,14 +36,9 @@ def tile_moe_tk_lin_relu_kernel(tc, xT, w_words, w_scales, b, gate, offs, pos1, 
         lists = ctx.enter_context(tc.tile_pool(name="lists", bufs=1))
         keep = ctx.enter_context(tc.tile_pool(name="keep", bufs=1))
         psum = ctx.enter_context(tc.psum_pool(name="psum", bufs=1))
-        taken = []
 
         def bank(number, width):
             return psum.tile([P, width], F32, name=f"bank{number}")
-
-        def next_bank():
-            taken.append(len(taken) % 8)
-            return bank(taken[-1], C)
 
         offs_t = lists.tile([P, SLOTS // 16], U16, name="offs_t")
         pos_t = [lists.tile([P, T // 16], U16, name=f"pos{r}_t") for r in range(TOP)]
@@ -53,8 +48,9 @@ def tile_moe_tk_lin_relu_kernel(tc, xT, w_words, w_scales, b, gate, offs, pos1, 
             [keep.tile([P, n, 4], BF16, align_bytes=64, name=f"grouped0_{lo}") for lo, n in CHUNKS[0]],
             [keep.tile([P, n, 4], BF16, align_bytes=64, name=f"grouped1_{lo}") for lo, n in CHUNKS[1]],
         ]
-        codes = [keep.tile([P, T], U32, align_bytes=64, name=f"codes{a}") for a in range(PASSES)]
-        scales = keep.tile([P, T], U8, align_bytes=64, name="scales")
+        codes = keep.tile([P, 3 * T], U32, align_bytes=64, name="codes")
+        first_word = (T, 0)
+        scales = keep.tile([P, 2 * T], U8, align_bytes=64, name="scales")
         g_codes = [{}, {}]
         g_scales = [keep.tile([P, PIECE], U8, align_bytes=64, name=f"g_scales_{c}") for c in range(SLOTS // PIECE)]
         g_scales1 = [keep.tile([P, PIECE], U8, align_bytes=64, name=f"g_scales1_{c}") for c in range(SLOTS // PIECE)]
@@ -67,7 +63,8 @@ def tile_moe_tk_lin_relu_kernel(tc, xT, w_words, w_scales, b, gate, offs, pos1, 
         make_identity(nc, ident[:])
 
         nc.vector.memset(scales[:].bitcast(I32), 0)
-        nc.vector.memset(ws_t[:].rearrange("p g n -> p (g n)").bitcast(I32), 0)
+        nc.vector.memset(codes[:, 2 * T :].bitcast(I32), 0)
+        nc.gpsimd.memset(ws_t[:].rearrange("p g n -> p (g n)").bitcast(I32), 0)
         for c in range(SLOTS // PIECE):
             nc.vector.memset(g_scales1[c][:].bitcast(I32), 0)
 
@@ -110,7 +107,7 @@ def tile_moe_tk_lin_relu_kernel(tc, xT, w_words, w_scales, b, gate, offs, pos1, 
         def quantize(a, c):
             lo, n = CHUNKS[a][c]
             nc.vector.quantize_mx(
-                out=codes[a][:, lo : lo + n].bitcast(FP8X4),
+                out=codes[:, first_word[a] + lo : first_word[a] + lo + n].bitcast(FP8X4),
                 scales=scales[SHIFT * a : P, lo : lo + n],
                 in_=grouped[a][c][:].rearrange("p w j -> p (w j)"),
             )
@@ -127,7 +124,9 @@ def tile_moe_tk_lin_relu_kernel(tc, xT, w_words, w_scales, b, gate, offs, pos1, 
         def gather_codes(a, lo, hi):
             held = (a, lo) == (0, SLOTS - C)
             dst = keep.tile([P, hi - lo], U32, align_bytes=64, name="grouped1_512" if held else f"g_codes{a}_{lo}")
-            nc.vector.tensor_copy(dst[:], codes[a][:].indirect(offs_t[:, lo // 16 : hi // 16]))
+            wide = 2 * T if hi - lo >= T else T
+            window = codes[:, first_word[a] : first_word[a] + wide]
+            nc.vector.tensor_copy(dst[:], window.indirect(offs_t[:, lo // 16 : hi // 16]))
             for at in range(lo, hi, P):
                 g_codes[a][at] = dst[:, at - lo : at - lo + P]
 
@@ -136,66 +135,59 @@ def tile_moe_tk_lin_relu_kernel(tc, xT, w_words, w_scales, b, gate, offs, pos1, 
             for q in range(0, P, 32):
                 nc.sync.dma_start(out=g_scales1[c][q : q + 4, :].bitcast(I32), in_=g_scales[c][q + SHIFT : q + SHIFT + 4, :].bitcast(I32))
 
-        def one_pass(ps, o, e, h, s, a, first=1):
-            g = e * PASSES + a
-            c, at = divmod(e * C + s * P, PIECE)
+        def one_pass(ps, o, at, h, a, start, stop):
+            g = at // C * PASSES + a
+            c, col = divmod(at, PIECE)
             nc.tensor.matmul_mx(
                 out=ps[:, o : o + P],
                 lhsT=w_t[:, g, 2 * P * h : 2 * P * (h + 1)].bitcast(FP4X4),
                 lhsT_scale=ws_t[:, g, P * h : P * (h + 1)],
-                rhs=g_codes[a][e * C + s * P].bitcast(FP8X4),
-                rhs_scale=(g_scales, g_scales1)[a][c][:, at : at + P],
-                start=(a == first),
-                stop=(a != first),
+                rhs=g_codes[a][at].bitcast(FP8X4),
+                rhs_scale=(g_scales, g_scales1)[a][c][:, col : col + P],
+                start=start,
+                stop=stop,
             )
 
-        def half(e, h, ps):
-            for s in range(2):
-                for a in (1, 0):
-                    one_pass(ps, s * P, e, h, s, a)
-            nc.scalar.activation(y[h][:, e * C : (e + 1) * C], ps[:], RELU, bias=b_t[:, h, e : e + 1])
+        def open_group(number, h, lo, hi, a):
+            ps = bank(number, hi - lo)
+            for at in range(lo, hi, P):
+                one_pass(ps, at - lo, at, h, a, at == lo, False)
+            return ps, h, lo, hi, 1 - a
 
-        def expert(e):
-            for h in range(HALVES):
-                half(e, h, next_bank())
+        def close_group(ps, h, lo, hi, a):
+            for at in range(lo, hi, P):
+                one_pass(ps, at - lo, at, h, a, False, at == hi - P)
+            for at in range(lo, hi, C):
+                n, e = min(C, hi - at), at // C
+                nc.scalar.activation(y[h][:, at : at + n], ps[:, at - lo : at - lo + n], RELU, bias=b_t[:, h, e : e + 1])
 
         def words(a, lo, n):
             gather_codes(a, lo, lo + n)
 
-        for c in range(3):
-            words(0, PIECE * c, PIECE)
-        words(0, 3 * PIECE, PIECE - C)
+        words(0, 0, SLOTS // 2)
+        words(0, SLOTS // 2, SLOTS // 2 - C)
         for c in range(len(CHUNKS[1])):
             quantize(1, c)
         words(0, SLOTS - C, C)
-        for c in range(3):
-            gather_scales(c)
+        gather_scales(0)
+        early = [open_group(2 * e + h, h, e * C, (e + 1) * C, 0) for e in range(4) for h in range(HALVES)]
         words(1, 0, PIECE)
-        for e in range(3):
-            expert(e)
-        gather_scales(3)
-        words(1, PIECE, PIECE)
-        for e in range(3, 6):
-            expert(e)
-        for e in range(6, 9):
-            words(1, e * C, C)
-            half(e, 0, next_bank())
-        ends = []
-        for s in range(2):
-            ps = next_bank()
-            one_pass(ps, 0, E - 1, 0, s, 0, first=0)
-            ends.append(ps)
-        for e in range(9, E - 1):
-            words(1, e * C, C)
-            half(e, 0, next_bank())
-        for s in range(2):
-            at = (E - 1) * C + s * P
-            words(1, at, P)
-            one_pass(ends[s], 0, E - 1, 0, s, 1, first=0)
-            nc.scalar.activation(y[0][:, at : at + P], ends[s][:, 0:P], RELU, bias=b_t[:, 0, E - 1 : E])
-        last_four = taken[-2:] + taken[-4:-2]
-        for e in range(6, E):
-            half(e, 1, bank(last_four[(e - 6) % 4], C))
+        for group in early:
+            close_group(*group)
+        gather_scales(1)
+        late = [open_group(e - 4, 0, e * C, (e + 1) * C, 0) for e in range(4, 7)]
+        gather_scales(2)
+        ends = ((7 * C, 2 * C), (9 * C, C), (10 * C, C), (SLOTS - C, P), (SLOTS - P, P))
+        last = [open_group(3 + k, 0, lo, lo + n, 0) for k, (lo, n) in enumerate(ends)]
+        words(1, PIECE, 3 * C)
+        for group in late:
+            close_group(*group)
+        for (lo, n), group in zip(ends, last):
+            words(1, lo, n)
+            close_group(*group)
+        for e in range(4, E):
+            close_group(*open_group(7 - e % 4, 1, e * C, (e + 1) * C, 1))
+        last_four = [5, 4, 7, 6]
 
         def product(h, r, lo, hi):
             prod = keep.tile([P, hi - lo], F32, name=f"prod{r}_{h}_{lo}")

@@ -26,8 +26,8 @@ HALVES = N // P
 SHIFT = 4
 CUT = 768
 PIECE = 1024
-CHUNKS = (((0, 256), (256, 256), (512, 256), (768, 128), (896, 128)), ((0, 512), (512, 512)))
-ON_SCALAR = ((96, 96, 112, 64, 48), (512, 512))
+CHUNKS = (((0, 256), (256, 256), (512, 256), (768, 128), (896, 128)), ((0, 256), (256, 256), (512, 256), (768, 256)))
+ON_SCALAR = ((96, 96, 112, 64, 48), (256, 256, 256, 256))
 
 
 def tile_moe_tk_lin_relu_kernel(tc, xT, w_words, w_scales, b, gate, offs, pos1, pos2, pos3, out):
@@ -43,14 +43,15 @@ def tile_moe_tk_lin_relu_kernel(tc, xT, w_words, w_scales, b, gate, offs, pos1, 
         offs_t = lists.tile([P, SLOTS // 16], U16, name="offs_t")
         pos_t = [lists.tile([P, T // 16], U16, name=f"pos{r}_t") for r in range(TOP)]
 
-        raw = [[keep.tile([P, 4, n], F32, name=f"raw{a}_{lo}") for lo, n in CHUNKS[a]] for a in range(PASSES)]
+        raw = [[keep.tile([P, 4, n], F32, align_bytes=64, name=f"raw{a}_{lo}") for lo, n in CHUNKS[a]] for a in range(PASSES)]
         grouped = [
             [keep.tile([P, n, 4], BF16, align_bytes=64, name=f"grouped0_{lo}") for lo, n in CHUNKS[0]],
-            [keep.tile([P, n, 4], BF16, align_bytes=64, name=f"grouped1_{lo}") for lo, n in CHUNKS[1]],
         ]
-        codes = keep.tile([P, 3 * T], U32, align_bytes=64, name="codes")
+        pairs = [keep.tile([P, 512, 4], BF16, align_bytes=64, name=f"grouped1_{lo}") for lo in (0, 512)]
+        grouped.append([pairs[lo // 512][:, lo % 512 : lo % 512 + n, :] for lo, n in CHUNKS[1]])
+        codes = keep.tile([P, 2 * T], U32, align_bytes=64, name="codes")
         first_word = (T, 0)
-        scales = keep.tile([P, 2 * T], U8, align_bytes=64, name="scales")
+        scales = keep.tile([P, T + 384], U8, align_bytes=64, name="scales")
         g_codes = [{}, {}]
         g_scales = [keep.tile([P, PIECE], U8, align_bytes=64, name=f"g_scales_{c}") for c in range(SLOTS // PIECE)]
         g_scales1 = [keep.tile([P, PIECE], U8, align_bytes=64, name=f"g_scales1_{c}") for c in range(SLOTS // PIECE)]
@@ -63,8 +64,7 @@ def tile_moe_tk_lin_relu_kernel(tc, xT, w_words, w_scales, b, gate, offs, pos1, 
         make_identity(nc, ident[:])
 
         nc.vector.memset(scales[:].bitcast(I32), 0)
-        nc.vector.memset(codes[:, 2 * T :].bitcast(I32), 0)
-        nc.gpsimd.memset(ws_t[:].rearrange("p g n -> p (g n)").bitcast(I32), 0)
+        nc.vector.memset(ws_t[:].rearrange("p g n -> p (g n)").bitcast(I32), 0)
         for c in range(SLOTS // PIECE):
             nc.vector.memset(g_scales1[c][:].bitcast(I32), 0)
 
@@ -77,8 +77,8 @@ def tile_moe_tk_lin_relu_kernel(tc, xT, w_words, w_scales, b, gate, offs, pos1, 
         for c in range(1, len(CHUNKS[0])):
             load_x(0, c)
         nc.sync.dma_start(offs_t[:], offs)
-        load_x(1, 0)
-        load_x(1, 1)
+        for c in range(len(CHUNKS[1])):
+            load_x(1, c)
         w_src = w_words.bitcast(I32).rearrange("e a p n -> p (e a) n")
         ws_src = w_scales.bitcast(I32)
         for q in range(4):
@@ -104,12 +104,11 @@ def tile_moe_tk_lin_relu_kernel(tc, xT, w_words, w_scales, b, gate, offs, pos1, 
             else:
                 nc.scalar.activation(dst, src, COPY)
 
-        def quantize(a, c):
-            lo, n = CHUNKS[a][c]
+        def quantize(a, lo, n, src):
             nc.vector.quantize_mx(
                 out=codes[:, first_word[a] + lo : first_word[a] + lo + n].bitcast(FP8X4),
                 scales=scales[SHIFT * a : P, lo : lo + n],
-                in_=grouped[a][c][:].rearrange("p w j -> p (w j)"),
+                in_=src[:].rearrange("p w j -> p (w j)"),
             )
 
         for a in range(PASSES):
@@ -119,11 +118,11 @@ def tile_moe_tk_lin_relu_kernel(tc, xT, w_words, w_scales, b, gate, offs, pos1, 
                 if cut < n:
                     cast("v", a, c, cut, n)
                 if a == 0:
-                    quantize(a, c)
+                    quantize(a, CHUNKS[a][c][0], n, grouped[a][c])
 
         def gather_codes(a, lo, hi):
             held = (a, lo) == (0, SLOTS - C)
-            dst = keep.tile([P, hi - lo], U32, align_bytes=64, name="grouped1_512" if held else f"g_codes{a}_{lo}")
+            dst = keep.tile([P, hi - lo], U32, align_bytes=64, name="raw1_768" if held else f"g_codes{a}_{lo}")
             wide = 2 * T if hi - lo >= T else T
             window = codes[:, first_word[a] : first_word[a] + wide]
             nc.vector.tensor_copy(dst[:], window.indirect(offs_t[:, lo // 16 : hi // 16]))
@@ -164,10 +163,10 @@ def tile_moe_tk_lin_relu_kernel(tc, xT, w_words, w_scales, b, gate, offs, pos1, 
         def words(a, lo, n):
             gather_codes(a, lo, lo + n)
 
-        words(0, 0, SLOTS // 2)
-        words(0, SLOTS // 2, SLOTS // 2 - C)
-        for c in range(len(CHUNKS[1])):
-            quantize(1, c)
+        for lo in range(0, SLOTS - C, 3 * C):
+            words(0, lo, min(3 * C, SLOTS - C - lo))
+        for c in range(2):
+            quantize(1, 512 * c, 512, pairs[c])
         words(0, SLOTS - C, C)
         gather_scales(0)
         early = [open_group(2 * e + h, h, e * C, (e + 1) * C, 0) for e in range(4) for h in range(HALVES)]
@@ -175,19 +174,20 @@ def tile_moe_tk_lin_relu_kernel(tc, xT, w_words, w_scales, b, gate, offs, pos1, 
         for group in early:
             close_group(*group)
         gather_scales(1)
-        late = [open_group(e - 4, 0, e * C, (e + 1) * C, 0) for e in range(4, 7)]
+        both = [open_group(h, h, 4 * C, 6 * C, 0) for h in range(HALVES)]
+        ends = ((6 * C, 2 * C), (8 * C, 2 * C), (10 * C, C), (SLOTS - C, P), (SLOTS - P, P))
+        last = [open_group(2, 0, 6 * C, 8 * C, 0)]
         gather_scales(2)
-        ends = ((7 * C, 2 * C), (9 * C, C), (10 * C, C), (SLOTS - C, P), (SLOTS - P, P))
-        last = [open_group(3 + k, 0, lo, lo + n, 0) for k, (lo, n) in enumerate(ends)]
-        words(1, PIECE, 3 * C)
-        for group in late:
+        last.extend(open_group(3 + k, 0, lo, lo + n, 0) for k, (lo, n) in enumerate(ends[1:]))
+        words(1, 4 * C, 2 * C)
+        for group in both:
             close_group(*group)
         for (lo, n), group in zip(ends, last):
             words(1, lo, n)
             close_group(*group)
-        for e in range(4, E):
-            close_group(*open_group(7 - e % 4, 1, e * C, (e + 1) * C, 1))
-        last_four = [5, 4, 7, 6]
+        last_four = [6, 5, 4, 3]
+        for e in range(6, E):
+            close_group(*open_group(last_four[(e - 6) % 4], 1, e * C, (e + 1) * C, 1))
 
         def product(h, r, lo, hi):
             prod = keep.tile([P, hi - lo], F32, name=f"prod{r}_{h}_{lo}")

@@ -24,7 +24,7 @@ PASSES = K // 512
 SLOTS = E * C
 HALVES = N // P
 SHIFT = 4
-CUT = 768
+CUT = 640
 PIECE = 1024
 CHUNKS = (((0, 256), (256, 256), (512, 256), (768, 128), (896, 128)), ((0, 256), (256, 256), (512, 256), (768, 256)))
 ON_SCALAR = ((96, 96, 112, 64, 48), (256, 256, 256, 256))
@@ -154,8 +154,14 @@ def tile_moe_tk_lin_relu_kernel(tc, xT, w_words, w_scales, b, gate, offs, pos1, 
             return ps, h, lo, hi, 1 - a
 
         def close_group(ps, h, lo, hi, a):
+            second_pass(ps, h, lo, hi, a)
+            empty(ps, h, lo, hi)
+
+        def second_pass(ps, h, lo, hi, a):
             for at in range(lo, hi, P):
                 one_pass(ps, at - lo, at, h, a, False, at == hi - P)
+
+        def empty(ps, h, lo, hi):
             for at in range(lo, hi, C):
                 n, e = min(C, hi - at), at // C
                 nc.scalar.activation(y[h][:, at : at + n], ps[:, at - lo : at - lo + n], RELU, bias=b_t[:, h, e : e + 1])
@@ -179,14 +185,18 @@ def tile_moe_tk_lin_relu_kernel(tc, xT, w_words, w_scales, b, gate, offs, pos1, 
         last = [open_group(2, 0, 6 * C, 8 * C, 0)]
         gather_scales(2)
         last.extend(open_group(3 + k, 0, lo, lo + n, 0) for k, (lo, n) in enumerate(ends[1:]))
+        spare = open_group(7, 1, 6 * C, 8 * C, 0)
         words(1, 4 * C, 2 * C)
         for group in both:
             close_group(*group)
         for (lo, n), group in zip(ends, last):
             words(1, lo, n)
             close_group(*group)
-        last_four = [6, 5, 4, 3]
-        for e in range(6, E):
+            if lo == 6 * C:
+                second_pass(*spare)
+        empty(*spare[:4])
+        last_four = [4, 3, 6, 5]
+        for e in range(8, E):
             close_group(*open_group(last_four[(e - 6) % 4], 1, e * C, (e + 1) * C, 1))
 
         def product(h, r, lo, hi):
@@ -214,14 +224,15 @@ def tile_moe_tk_lin_relu_kernel(tc, xT, w_words, w_scales, b, gate, offs, pos1, 
             nc.scalar.copy(total[:], back[:])
             store(h, lo, hi, total, nc.scalar)
 
-        for piece, (h, lo, hi) in enumerate(((0, 0, 512), (0, 512, T), (1, 0, 384), (1, 384, 640), (1, 640, CUT))):
+        for piece, (h, lo, hi) in enumerate(((0, 0, 512), (0, 512, T), (1, 0, 384), (1, 384, CUT))):
             summed_on_tensor(piece, h, lo, hi)
-        mid = (CUT + T) // 2
+        mid = T - P
         c0 = product(1, 0, CUT, T)
         c1 = product(1, 1, CUT, T)
         left = product(1, 2, CUT, mid)
         nc.vector.tensor_tensor(c0[:], c0[:], c1[:], ADD)
         right = product(1, 2, mid, T)
-        nc.vector.tensor_tensor(c1[:, : mid - CUT], c0[:, : mid - CUT], left[:], ADD)
-        nc.vector.tensor_tensor(c1[:, mid - CUT :], c0[:, mid - CUT :], right[:], ADD)
-        store(1, CUT, T, c1, nc.sync)
+        nc.vector.tensor_tensor(left[:], c0[:, : mid - CUT], left[:], ADD)
+        store(1, CUT, mid, left, nc.sync)
+        nc.vector.tensor_tensor(right[:], c0[:, mid - CUT :], right[:], ADD)
+        store(1, mid, T, right, nc.sync)

@@ -92,9 +92,10 @@ def tile_moe_tk_lin_relu_kernel(tc, xT, w_words, w_scales, b, gate, offs, pos1, 
         nc.sync.dma_start(out=b_t[:], in_=b.rearrange("(h p) e -> p h e", p=P))
         for r, src in enumerate((pos1, pos2, pos3)):
             nc.sync.dma_start(pos_t[r][:], src)
-        gate_t = [keep.tile([P, T], F32, name=f"gate{r}") for r in range(TOP)]
-        for r in range(TOP):
-            nc.sync.dma_start(out=gate_t[r][:], in_=gate[r, 0:P, :])
+
+        first_gate = keep.tile([P, T], F32, name="first_gate")
+        nc.sync.dma_start(out=first_gate[:], in_=gate[0, 0:P, :])
+        gate_t = [first_gate]
 
         def cast(engine, a, c, lo, hi):
             dst = grouped[a][c][:, lo:hi, :].rearrange("p (c i) j -> p c j i", i=4)
@@ -177,6 +178,10 @@ def tile_moe_tk_lin_relu_kernel(tc, xT, w_words, w_scales, b, gate, offs, pos1, 
         gather_scales(0)
         early = [open_group(2 * e + h, h, e * C, (e + 1) * C, 0) for e in range(4) for h in range(HALVES)]
         words(1, 0, PIECE)
+        late_gates = keep.tile([P, TOP - 1, T], F32, align_bytes=64, name="g_codes0_0")
+        for r in range(1, TOP):
+            nc.sync.dma_start(out=late_gates[:, r - 1, :], in_=gate[r, 0:P, :])
+            gate_t.append(late_gates[:, r - 1, :])
         for group in early:
             close_group(*group)
         gather_scales(1)

@@ -23,11 +23,14 @@ P = 128
 PASSES = K // 512
 SLOTS = E * C
 HALVES = N // P
+BANKS = 8
 SHIFT = 4
-CUT = 640
 PIECE = 1024
 CHUNKS = (((0, 256), (256, 256), (512, 256), (768, 128), (896, 128)), ((0, 256), (256, 256), (512, 256), (768, 256)))
 ON_SCALAR = ((96, 96, 112, 64, 48), (256, 256, 256, 256))
+CUT = 640
+TURNED = ((0, 0, 256), (0, 256, 640), (0, 640, T), (1, 0, 384), (1, 384, CUT))
+H1_ON_VECTOR = 9 * C
 
 
 def tile_moe_tk_lin_relu_kernel(tc, xT, w_words, w_scales, b, gate, offs, pos1, pos2, pos3, out):
@@ -38,7 +41,7 @@ def tile_moe_tk_lin_relu_kernel(tc, xT, w_words, w_scales, b, gate, offs, pos1, 
         psum = ctx.enter_context(tc.psum_pool(name="psum", bufs=1))
 
         def bank(number, width):
-            return psum.tile([P, width], F32, name=f"bank{number}")
+            return psum.tile([P, width], F32, name=f"bank{number % BANKS}")
 
         offs_t = lists.tile([P, SLOTS // 16], U16, name="offs_t")
         pos_t = [lists.tile([P, T // 16], U16, name=f"pos{r}_t") for r in range(TOP)]
@@ -59,10 +62,13 @@ def tile_moe_tk_lin_relu_kernel(tc, xT, w_words, w_scales, b, gate, offs, pos1, 
         ws_t = keep.tile([P, E * PASSES, N], U8, align_bytes=64, name="ws_t")
         b_t = keep.tile([P, HALVES, E], F32, name="b_t")
         y = [keep.tile([P, SLOTS], F32, name=f"y{h}") for h in range(HALVES)]
+        gate_rows = keep.tile([P, P], F32, name="gate_rows")
+        gate_by_token = keep.tile([P, T // P], F32, name="gate_by_token")
 
         ident = keep.tile([P, P], F32, name="ident")
         make_identity(nc, ident[:])
 
+        nc.gpsimd.memset(gate_rows[:], 0.0)
         nc.vector.memset(scales[:].bitcast(I32), 0)
         nc.vector.memset(ws_t[:].rearrange("p g n -> p (g n)").bitcast(I32), 0)
         for c in range(SLOTS // PIECE):
@@ -73,8 +79,7 @@ def tile_moe_tk_lin_relu_kernel(tc, xT, w_words, w_scales, b, gate, offs, pos1, 
             src = xT[512 * a : 512 * (a + 1), lo : lo + n].rearrange("(p j) w -> p j w", j=4)
             nc.sync.dma_start(out=raw[a][c][:], in_=src)
 
-        load_x(0, 0)
-        for c in range(1, len(CHUNKS[0])):
+        for c in range(len(CHUNKS[0])):
             load_x(0, c)
         nc.sync.dma_start(offs_t[:], offs)
         for c in range(len(CHUNKS[1])):
@@ -86,16 +91,16 @@ def tile_moe_tk_lin_relu_kernel(tc, xT, w_words, w_scales, b, gate, offs, pos1, 
                 out=ws_t[32 * q : 32 * q + 4].bitcast(I32),
                 in_=ws_src[:, :, 4 * q : 4 * q + 4, :].rearrange("e a r n -> r (e a) n"),
             )
-        for s in range(3):
-            g = slice(8 * s, 8 * s + 8)
-            nc.sync.dma_start(out=w_t[:, g, :].bitcast(I32), in_=w_src[:, g, :])
+        nc.sync.dma_start(out=gate_rows[0 : T // P, :], in_=gate[TOP - 1, 0, :].rearrange("(c p) -> c p", p=P))
         nc.sync.dma_start(out=b_t[:], in_=b.rearrange("(h p) e -> p h e", p=P))
+        for g in (slice(0, 8), slice(8, E * PASSES)):
+            nc.sync.dma_start(out=w_t[:, g, :].bitcast(I32), in_=w_src[:, g, :])
         for r, src in enumerate((pos1, pos2, pos3)):
             nc.sync.dma_start(pos_t[r][:], src)
 
-        first_gate = keep.tile([P, T], F32, name="first_gate")
-        nc.sync.dma_start(out=first_gate[:], in_=gate[0, 0:P, :])
-        gate_t = [first_gate]
+        ps = bank(BANKS - 1, P)
+        nc.tensor.transpose(ps[:], gate_rows[:], ident[:])
+        nc.scalar.copy(gate_by_token[:], ps[:, 0 : T // P])
 
         def cast(engine, a, c, lo, hi):
             dst = grouped[a][c][:, lo:hi, :].rearrange("p (c i) j -> p c j i", i=4)
@@ -121,123 +126,148 @@ def tile_moe_tk_lin_relu_kernel(tc, xT, w_words, w_scales, b, gate, offs, pos1, 
                 if a == 0:
                     quantize(a, CHUNKS[a][c][0], n, grouped[a][c])
 
-        def gather_codes(a, lo, hi):
+        def words(a, lo, n):
             held = (a, lo) == (0, SLOTS - C)
-            dst = keep.tile([P, hi - lo], U32, align_bytes=64, name="raw1_768" if held else f"g_codes{a}_{lo}")
-            wide = 2 * T if hi - lo >= T else T
+            dst = keep.tile([P, n], U32, align_bytes=64, name="raw1_768" if held else f"g_codes{a}_{lo}")
+            wide = 2 * T if n >= T else T
             window = codes[:, first_word[a] : first_word[a] + wide]
-            nc.vector.tensor_copy(dst[:], window.indirect(offs_t[:, lo // 16 : hi // 16]))
-            for at in range(lo, hi, P):
-                g_codes[a][at] = dst[:, at - lo : at - lo + P]
+            nc.vector.tensor_copy(dst[:], window.indirect(offs_t[:, lo // 16 : (lo + n) // 16]))
+            for at in range(lo, lo + n, P):
+                g_codes[a][at] = (dst, at - lo)
 
-        def gather_scales(c):
+        def gather_scales(c, queue):
             nc.vector.tensor_copy(g_scales[c][:], scales[:].indirect(offs_t[:, PIECE * c // 16 : PIECE * (c + 1) // 16]))
             for q in range(0, P, 32):
-                nc.sync.dma_start(out=g_scales1[c][q : q + 4, :].bitcast(I32), in_=g_scales[c][q + SHIFT : q + SHIFT + 4, :].bitcast(I32))
+                queue.dma_start(out=g_scales1[c][q : q + 4, :].bitcast(I32), in_=g_scales[c][q + SHIFT : q + SHIFT + 4, :].bitcast(I32))
 
-        def one_pass(ps, o, at, h, a, start, stop):
-            g = at // C * PASSES + a
-            c, col = divmod(at, PIECE)
-            nc.tensor.matmul_mx(
-                out=ps[:, o : o + P],
-                lhsT=w_t[:, g, 2 * P * h : 2 * P * (h + 1)].bitcast(FP4X4),
-                lhsT_scale=ws_t[:, g, P * h : P * (h + 1)],
-                rhs=g_codes[a][at].bitcast(FP8X4),
-                rhs_scale=(g_scales, g_scales1)[a][c][:, col : col + P],
-                start=start,
-                stop=stop,
-            )
+        def one_pass(ps, lo, n, a):
+            g = lo // C * PASSES + a
+            c, col = divmod(lo, PIECE)
+            src, at = g_codes[a][lo]
+            for h in range(HALVES):
+                nc.tensor.matmul_mx(
+                    out=ps[:, h * n : (h + 1) * n],
+                    lhsT=w_t[:, g, 2 * P * h : 2 * P * (h + 1)].bitcast(FP4X4),
+                    lhsT_scale=ws_t[:, g, P * h : P * (h + 1)],
+                    rhs=src[:, at : at + n].bitcast(FP8X4),
+                    rhs_scale=(g_scales, g_scales1)[a][c][:, col : col + n],
+                    start=(a, h) == (0, 0),
+                    stop=(a, h) == (PASSES - 1, HALVES - 1),
+                )
 
-        def open_group(number, h, lo, hi, a):
-            ps = bank(number, hi - lo)
-            for at in range(lo, hi, P):
-                one_pass(ps, at - lo, at, h, a, at == lo, False)
-            return ps, h, lo, hi, 1 - a
+        def open_group(number, lo, n):
+            ps = bank(number, HALVES * n)
+            one_pass(ps, lo, n, 0)
+            return ps, lo, n
 
-        def close_group(ps, h, lo, hi, a):
-            second_pass(ps, h, lo, hi, a)
-            empty(ps, h, lo, hi)
+        left_over = []
 
-        def second_pass(ps, h, lo, hi, a):
-            for at in range(lo, hi, P):
-                one_pass(ps, at - lo, at, h, a, False, at == hi - P)
-
-        def empty(ps, h, lo, hi):
-            for at in range(lo, hi, C):
-                n, e = min(C, hi - at), at // C
-                nc.scalar.activation(y[h][:, at : at + n], ps[:, at - lo : at - lo + n], RELU, bias=b_t[:, h, e : e + 1])
-
-        def words(a, lo, n):
-            gather_codes(a, lo, lo + n)
+        def close_group(ps, lo, n):
+            one_pass(ps, lo, n, 1)
+            e = lo // C
+            for h in range(HALVES):
+                dst, src, bias = y[h][:, lo : lo + n], ps[:, h * n : (h + 1) * n], b_t[:, h, e : e + 1]
+                if h == 1 and lo >= H1_ON_VECTOR:
+                    left_over.append((dst, src, bias))
+                else:
+                    nc.scalar.activation(dst, src, RELU, bias=bias)
 
         for lo in range(0, SLOTS - C, 3 * C):
             words(0, lo, min(3 * C, SLOTS - C - lo))
         for c in range(2):
             quantize(1, 512 * c, 512, pairs[c])
         words(0, SLOTS - C, C)
-        gather_scales(0)
-        early = [open_group(2 * e + h, h, e * C, (e + 1) * C, 0) for e in range(4) for h in range(HALVES)]
+        gather_scales(0, nc.sync)
+        groups = [open_group(e, e * C, C) for e in range(4)]
+        gather_scales(1, nc.sync)
+        groups.extend(open_group(e, e * C, C) for e in range(4, 8))
+        last_gate = keep.tile([P, T - CUT], F32, align_bytes=64, name="g_codes0_0")
+        nc.sync.dma_start(out=last_gate[:], in_=gate[TOP - 1, 0:P, CUT:T])
+        gates = keep.tile([P, TOP - 1, T], F32, align_bytes=64, name="g_codes0_768")
+        nc.sync.dma_start(out=gates[:], in_=gate[0 : TOP - 1, 0:P, :].rearrange("r p t -> p r t"))
         words(1, 0, PIECE)
-        late_gates = keep.tile([P, TOP - 1, T], F32, align_bytes=64, name="g_codes0_0")
-        for r in range(1, TOP):
-            nc.sync.dma_start(out=late_gates[:, r - 1, :], in_=gate[r, 0:P, :])
-            gate_t.append(late_gates[:, r - 1, :])
-        for group in early:
+        for group in groups[:4]:
             close_group(*group)
-        gather_scales(1)
-        both = [open_group(h, h, 4 * C, 6 * C, 0) for h in range(HALVES)]
-        ends = ((6 * C, 2 * C), (8 * C, 2 * C), (10 * C, C), (SLOTS - C, P), (SLOTS - P, P))
-        last = [open_group(2, 0, 6 * C, 8 * C, 0)]
-        gather_scales(2)
-        last.extend(open_group(3 + k, 0, lo, lo + n, 0) for k, (lo, n) in enumerate(ends[1:]))
-        spare = open_group(7, 1, 6 * C, 8 * C, 0)
-        words(1, 4 * C, 2 * C)
-        for group in both:
-            close_group(*group)
-        for (lo, n), group in zip(ends, last):
+        gather_scales(2, nc.sync)
+        ends = ((8 * C, C), (9 * C, C), (10 * C, C), (SLOTS - C, P), (SLOTS - P, P))
+        groups.extend(open_group(8 + k, lo, n) for k, (lo, n) in enumerate(ends[:4]))
+        for e in range(4, 8):
+            words(1, e * C, C)
+            close_group(*groups[e])
+            if e == 4:
+                groups.append(open_group(12, *ends[4]))
+        for (lo, n), group in zip(ends, groups[8:]):
             words(1, lo, n)
             close_group(*group)
-            if lo == 6 * C:
-                second_pass(*spare)
-        empty(*spare[:4])
-        last_four = [4, 3, 6, 5]
-        for e in range(8, E):
-            close_group(*open_group(last_four[(e - 6) % 4], 1, e * C, (e + 1) * C, 1))
+        for dst, src, bias in left_over:
+            nc.vector.tensor_scalar(dst, src, bias, 0.0, ADD, MAX)
+
+        def picks(h, r, lo, hi):
+            return y[h][:].indirect(pos_t[r][:, lo // 16 : hi // 16])
 
         def product(h, r, lo, hi):
             prod = keep.tile([P, hi - lo], F32, name=f"prod{r}_{h}_{lo}")
-            nc.vector.tensor_tensor(prod[:], y[h][:].indirect(pos_t[r][:, lo // 16 : hi // 16]), gate_t[r][:, lo:hi], MULT)
+            nc.vector.tensor_tensor(prod[:], picks(h, r, lo, hi), gates[:, r, lo:hi], MULT)
             return prod
 
-        def store(h, lo, hi, total, queue):
-            queue.dma_start(out=out[h * P : (h + 1) * P, lo:hi], in_=total[:])
+        def plain(h, lo, hi):
+            picked = keep.tile([P, hi - lo], F32, name=f"picked_{h}_{lo}")
+            nc.scalar.activation(picked[:], picks(h, TOP - 1, lo, hi), COPY)
+            return picked
 
-        def summed_on_tensor(piece, h, lo, hi):
-            n = hi - lo
-            prods = [product(h, r, lo, hi) for r in range(TOP)]
-            turned = bank(last_four[1 - max(piece - 1, 0) % 2], n)
-            for r in range(TOP):
+        def turn(ps, parts):
+            n = ps.shape[1]
+            for r, part in enumerate(parts):
                 for o in range(0, n, P):
-                    first, last = (r, o) == (0, 0), (r, o) == (TOP - 1, n - P)
-                    nc.tensor.matmul(turned[:, o : o + P], prods[r][:, o : o + P], ident[:], start=first, stop=last, is_transpose=True)
-            by_token = keep.tile([P, n], F32, name=f"by_token{h}_{lo}")
-            nc.scalar.copy(by_token[:], turned[:])
-            back = bank(last_four[0 if piece == 0 else 2 + piece % 2], n)
-            for o in range(0, n, P):
-                nc.tensor.transpose(back[:, o : o + P], by_token[:, o : o + P], ident[:])
-            total = keep.tile([P, n], F32, name=f"total{h}_{lo}")
-            nc.scalar.copy(total[:], back[:])
-            store(h, lo, hi, total, nc.scalar)
+                    first, last = (r, o) == (0, 0), (r, o) == (len(parts) - 1, n - P)
+                    nc.tensor.matmul(ps[:, o : o + P], part[:, o : o + P], ident[:], start=first, stop=last, is_transpose=True)
+            return ps
 
-        for piece, (h, lo, hi) in enumerate(((0, 0, 512), (0, 512, T), (1, 0, 384), (1, 384, CUT))):
-            summed_on_tensor(piece, h, lo, hi)
+        def forward(i):
+            h, lo, hi = TURNED[i]
+            prods = [product(h, r, lo, hi) for r in range(TOP - 1)]
+            third = turn(bank(5 + 3 * i, hi - lo), [picked[i]])
+            both = turn(bank(6 + 3 * i, hi - lo), prods)
+            return third, both
+
+        def by_token(i):
+            h, lo, hi = TURNED[i]
+            third, both = turned[i]
+            parts = [keep.tile([P, hi - lo], F32, name=f"by_token{r}_{h}_{lo}") for r in range(2)]
+            for o in range(0, hi - lo, P):
+                block = (lo + o) // P
+                nc.scalar.activation(parts[0][:, o : o + P], third[:, o : o + P], COPY, scale=gate_by_token[:, block : block + 1])
+            nc.scalar.copy(parts[1][:], both[:])
+            return turn(bank(7 + 3 * i, hi - lo), parts)
+
+        def finish(i):
+            h, lo, hi = TURNED[i]
+            total = keep.tile([P, hi - lo], F32, name=f"total{h}_{lo}")
+            nc.scalar.copy(total[:], back[i][:])
+            nc.sync.dma_start(out=out[h * P : (h + 1) * P, lo:hi], in_=total[:])
+
+        picked, turned, back = [], [], []
+        count = len(TURNED)
+        picked.extend(plain(*piece) for piece in TURNED[:2])
+        for i in range(count + 1):
+            if i + 2 < count:
+                picked.append(plain(*TURNED[i + 2]))
+            if i < count:
+                turned.append(forward(i))
+                back.append(by_token(i))
+            if 1 <= i <= count:
+                finish(i - 1)
+
         mid = T - P
         c0 = product(1, 0, CUT, T)
         c1 = product(1, 1, CUT, T)
-        left = product(1, 2, CUT, mid)
+        left = keep.tile([P, mid - CUT], F32, name="left")
+        nc.vector.tensor_tensor(left[:], picks(1, 2, CUT, mid), last_gate[:, : mid - CUT], MULT)
         nc.vector.tensor_tensor(c0[:], c0[:], c1[:], ADD)
-        right = product(1, 2, mid, T)
-        nc.vector.tensor_tensor(left[:], c0[:, : mid - CUT], left[:], ADD)
-        store(1, CUT, mid, left, nc.sync)
-        nc.vector.tensor_tensor(right[:], c0[:, mid - CUT :], right[:], ADD)
-        store(1, mid, T, right, nc.sync)
+        right = keep.tile([P, T - mid], F32, name="right")
+        nc.vector.tensor_tensor(right[:], picks(1, 2, mid, T), last_gate[:, mid - CUT :], MULT)
+        last = keep.tile([P, T - CUT], F32, name="total0_256")
+        nc.vector.tensor_tensor(last[:, : mid - CUT], c0[:, : mid - CUT], left[:], ADD)
+        nc.sync.dma_start(out=out[P:N, CUT:mid], in_=last[:, : mid - CUT])
+        nc.vector.tensor_tensor(last[:, mid - CUT :], c0[:, mid - CUT :], right[:], ADD)
+        nc.sync.dma_start(out=out[P:N, mid:T], in_=last[:, mid - CUT :])

@@ -28,8 +28,9 @@ SHIFT = 4
 PIECE = 1024
 CHUNKS = (((0, 256), (256, 256), (512, 256), (768, 128), (896, 128)), ((0, 256), (256, 256), (512, 256), (768, 256)))
 ON_SCALAR = ((96, 96, 112, 64, 48), (256, 256, 256, 256))
-CUT = 640
-TURNED = ((0, 0, 256), (0, 256, 640), (0, 640, T), (1, 0, 384), (1, 384, CUT))
+TURNED = ((0, 0, 256), (0, 256, 640), (1, 0, 384))
+ADDED = ((0, 640, T, 1), (1, 384, 768, 1), (1, 768, 896, 1), (1, 896, T, 1))
+CUT = 384
 H1_ON_VECTOR = 9 * C
 
 
@@ -181,10 +182,9 @@ def tile_moe_tk_lin_relu_kernel(tc, xT, w_words, w_scales, b, gate, offs, pos1, 
         groups = [open_group(e, e * C, C) for e in range(4)]
         gather_scales(1, nc.sync)
         groups.extend(open_group(e, e * C, C) for e in range(4, 8))
-        last_gate = keep.tile([P, T - CUT], F32, align_bytes=64, name="g_codes0_0")
-        nc.sync.dma_start(out=last_gate[:], in_=gate[TOP - 1, 0:P, CUT:T])
-        gates = keep.tile([P, TOP - 1, T], F32, align_bytes=64, name="g_codes0_768")
-        nc.sync.dma_start(out=gates[:], in_=gate[0 : TOP - 1, 0:P, :].rearrange("r p t -> p r t"))
+        gates = keep.tile([P, TOP, T], F32, align_bytes=64, name="g_codes0_768")
+        nc.sync.dma_start(out=gates[:, : TOP - 1, :], in_=gate[0 : TOP - 1, 0:P, :].rearrange("r p t -> p r t"))
+        nc.sync.dma_start(out=gates[:, TOP - 1, CUT:T], in_=gate[TOP - 1, 0:P, CUT:T])
         words(1, 0, PIECE)
         for group in groups[:4]:
             close_group(*group)
@@ -246,28 +246,54 @@ def tile_moe_tk_lin_relu_kernel(tc, xT, w_words, w_scales, b, gate, offs, pos1, 
             nc.scalar.copy(total[:], back[i][:])
             nc.sync.dma_start(out=out[h * P : (h + 1) * P, lo:hi], in_=total[:])
 
-        picked, turned, back = [], [], []
-        count = len(TURNED)
-        picked.extend(plain(*piece) for piece in TURNED[:2])
-        for i in range(count + 1):
-            if i + 2 < count:
-                picked.append(plain(*TURNED[i + 2]))
-            if i < count:
-                turned.append(forward(i))
-                back.append(by_token(i))
-            if 1 <= i <= count:
-                finish(i - 1)
+        three = [keep.tile([P, TOP, hi - lo], F32, name=f"three{h}_{lo}") for h, lo, hi, own in ADDED]
 
-        mid = T - P
-        c0 = product(1, 0, CUT, T)
-        c1 = product(1, 1, CUT, T)
-        left = keep.tile([P, mid - CUT], F32, name="left")
-        nc.vector.tensor_tensor(left[:], picks(1, 2, CUT, mid), last_gate[:, : mid - CUT], MULT)
-        nc.vector.tensor_tensor(c0[:], c0[:], c1[:], ADD)
-        right = keep.tile([P, T - mid], F32, name="right")
-        nc.vector.tensor_tensor(right[:], picks(1, 2, mid, T), last_gate[:, mid - CUT :], MULT)
-        last = keep.tile([P, T - CUT], F32, name="total0_256")
-        nc.vector.tensor_tensor(last[:, : mid - CUT], c0[:, : mid - CUT], left[:], ADD)
-        nc.sync.dma_start(out=out[P:N, CUT:mid], in_=last[:, : mid - CUT])
-        nc.vector.tensor_tensor(last[:, mid - CUT :], c0[:, mid - CUT :], right[:], ADD)
-        nc.sync.dma_start(out=out[P:N, mid:T], in_=last[:, mid - CUT :])
+        def on_scalar(j):
+            h, lo, hi, own = ADDED[j]
+            for r in range(own, TOP):
+                nc.scalar.activation(three[j][:, r, :], picks(h, r, lo, hi), COPY)
+
+        def on_vector(j):
+            h, lo, hi, own = ADDED[j]
+            for r in range(own):
+                nc.vector.tensor_tensor(three[j][:, r, :], picks(h, r, lo, hi), gates[:, r, lo:hi], MULT)
+
+        def weigh(j):
+            h, lo, hi, own = ADDED[j]
+            nc.vector.tensor_tensor(three[j][:, own:, :], three[j][:, own:, :], gates[:, own:, lo:hi], MULT)
+
+        def add(j, r, name=None):
+            h, lo, hi, own = ADDED[j]
+            dst = three[j][:, 0, :] if name is None else keep.tile([P, hi - lo], F32, name=name)[:]
+            nc.vector.tensor_tensor(dst, three[j][:, 0, :], three[j][:, r, :], ADD)
+            if r == TOP - 1:
+                nc.sync.dma_start(out=out[h * P : (h + 1) * P, lo:hi], in_=dst)
+
+        picked = [plain(*piece) for piece in TURNED]
+        turned = [forward(i) for i in range(len(TURNED))]
+        back = [by_token(0)]
+        on_scalar(0)
+        finish(0)
+        back.append(by_token(1))
+        on_scalar(1)
+        back.append(by_token(2))
+        on_scalar(2)
+        on_scalar(3)
+        finish(1)
+        finish(2)
+        on_vector(0)
+        weigh(0)
+        on_vector(1)
+        add(0, 1)
+        on_vector(2)
+        add(0, 2, "total0_0")
+        weigh(1)
+        on_vector(3)
+        add(1, 1)
+        weigh(2)
+        add(1, 2)
+        weigh(3)
+        add(2, 1)
+        add(3, 1)
+        add(2, 2)
+        add(3, 2)

@@ -28,9 +28,9 @@ SHIFT = 4
 PIECE = 1024
 CHUNKS = (((0, 256), (256, 256), (512, 256), (768, 128), (896, 128)), ((0, 256), (256, 256), (512, 256), (768, 256)))
 ON_SCALAR = ((96, 96, 112, 64, 48), (256, 256, 256, 256))
-TURNED = ((0, 0, 256), (0, 256, 640), (1, 0, 384))
-ADDED = ((0, 640, T, 1), (1, 384, 768, 1), (1, 768, 896, 1), (1, 896, T, 1))
-CUT = 384
+TURNED = ((0, 0, 256), (0, 256, 640), (1, 0, 384), (1, 384, 640))
+CUT = 640
+SPARE = 1024
 H1_ON_VECTOR = 9 * C
 
 
@@ -53,7 +53,7 @@ def tile_moe_tk_lin_relu_kernel(tc, xT, w_words, w_scales, b, gate, offs, pos1, 
         ]
         pairs = [keep.tile([P, 512, 4], BF16, align_bytes=64, name=f"grouped1_{lo}") for lo in (0, 512)]
         grouped.append([pairs[lo // 512][:, lo % 512 : lo % 512 + n, :] for lo, n in CHUNKS[1]])
-        codes = keep.tile([P, 2 * T], U32, align_bytes=64, name="codes")
+        codes = keep.tile([P, 2 * T + SPARE], U32, align_bytes=64, name="codes")
         first_word = (T, 0)
         scales = keep.tile([P, T + 384], U8, align_bytes=64, name="scales")
         g_codes = [{}, {}]
@@ -72,6 +72,7 @@ def tile_moe_tk_lin_relu_kernel(tc, xT, w_words, w_scales, b, gate, offs, pos1, 
         nc.gpsimd.memset(gate_rows[:], 0.0)
         nc.vector.memset(scales[:].bitcast(I32), 0)
         nc.vector.memset(ws_t[:].rearrange("p g n -> p (g n)").bitcast(I32), 0)
+        nc.vector.memset(codes[:, 2 * T :].bitcast(I32), 0)
         for c in range(SLOTS // PIECE):
             nc.vector.memset(g_scales1[c][:].bitcast(I32), 0)
 
@@ -130,7 +131,7 @@ def tile_moe_tk_lin_relu_kernel(tc, xT, w_words, w_scales, b, gate, offs, pos1, 
         def words(a, lo, n):
             held = (a, lo) == (0, SLOTS - C)
             dst = keep.tile([P, n], U32, align_bytes=64, name="raw1_768" if held else f"g_codes{a}_{lo}")
-            wide = 2 * T if n >= T else T
+            wide = T if n < T else (T + SPARE, 2 * T)[a]
             window = codes[:, first_word[a] : first_word[a] + wide]
             nc.vector.tensor_copy(dst[:], window.indirect(offs_t[:, lo // 16 : (lo + n) // 16]))
             for at in range(lo, lo + n, P):
@@ -141,79 +142,96 @@ def tile_moe_tk_lin_relu_kernel(tc, xT, w_words, w_scales, b, gate, offs, pos1, 
             for q in range(0, P, 32):
                 queue.dma_start(out=g_scales1[c][q : q + 4, :].bitcast(I32), in_=g_scales[c][q + SHIFT : q + SHIFT + 4, :].bitcast(I32))
 
-        def one_pass(ps, lo, n, a):
+        def one_pass(ps, h, lo, n, a, start, stop):
             g = lo // C * PASSES + a
             c, col = divmod(lo, PIECE)
             src, at = g_codes[a][lo]
-            for h in range(HALVES):
-                nc.tensor.matmul_mx(
-                    out=ps[:, h * n : (h + 1) * n],
-                    lhsT=w_t[:, g, 2 * P * h : 2 * P * (h + 1)].bitcast(FP4X4),
-                    lhsT_scale=ws_t[:, g, P * h : P * (h + 1)],
-                    rhs=src[:, at : at + n].bitcast(FP8X4),
-                    rhs_scale=(g_scales, g_scales1)[a][c][:, col : col + n],
-                    start=(a, h) == (0, 0),
-                    stop=(a, h) == (PASSES - 1, HALVES - 1),
-                )
+            nc.tensor.matmul_mx(
+                out=ps,
+                lhsT=w_t[:, g, 2 * P * h : 2 * P * (h + 1)].bitcast(FP4X4),
+                lhsT_scale=ws_t[:, g, P * h : P * (h + 1)],
+                rhs=src[:, at : at + n].bitcast(FP8X4),
+                rhs_scale=(g_scales, g_scales1)[a][c][:, col : col + n],
+                start=start,
+                stop=stop,
+            )
 
-        def open_group(number, lo, n):
-            ps = bank(number, HALVES * n)
-            one_pass(ps, lo, n, 0)
-            return ps, lo, n
+        def open_group(number, parts):
+            ps = bank(number, sum(n for h, lo, n in parts))
+            views, at = [], 0
+            for h, lo, n in parts:
+                views.append(ps[:, at : at + n])
+                one_pass(views[-1], h, lo, n, 0, at == 0, False)
+                at = at + n
+            return ps, views, parts
+
+        def second_pass(group, k):
+            ps, views, parts = group
+            one_pass(views[k], *parts[k], 1, False, k == len(parts) - 1)
 
         left_over = []
 
-        def close_group(ps, lo, n):
-            one_pass(ps, lo, n, 1)
+        def empty(src, h, lo, n):
             e = lo // C
-            for h in range(HALVES):
-                dst, src, bias = y[h][:, lo : lo + n], ps[:, h * n : (h + 1) * n], b_t[:, h, e : e + 1]
-                if h == 1 and lo >= H1_ON_VECTOR:
-                    left_over.append((dst, src, bias))
-                else:
-                    nc.scalar.activation(dst, src, RELU, bias=bias)
+            dst, bias = y[h][:, lo : lo + n], b_t[:, h, e : e + 1]
+            if h == 1 and lo >= H1_ON_VECTOR:
+                left_over.append((dst, src, bias))
+            else:
+                nc.scalar.activation(dst, src, RELU, bias=bias)
 
-        for lo in range(0, SLOTS - C, 3 * C):
-            words(0, lo, min(3 * C, SLOTS - C - lo))
+        def close_group(group):
+            ps, views, parts = group
+            for k in range(len(parts)):
+                second_pass(group, k)
+            for view, part in zip(views, parts):
+                empty(view, *part)
+
+        def expert(e):
+            return open_group(e, [(h, e * C, C) for h in range(HALVES)])
+
+        words(0, 0, 5 * C)
+        words(0, 5 * C, 6 * C)
         for c in range(2):
             quantize(1, 512 * c, 512, pairs[c])
         words(0, SLOTS - C, C)
         gather_scales(0, nc.sync)
-        groups = [open_group(e, e * C, C) for e in range(4)]
+        groups = [expert(e) for e in range(4)]
         gather_scales(1, nc.sync)
-        groups.extend(open_group(e, e * C, C) for e in range(4, 8))
-        gates = keep.tile([P, TOP, T], F32, align_bytes=64, name="g_codes0_768")
+        groups.extend(expert(e) for e in range(4, 8))
+        gates = keep.tile([P, TOP, T], F32, align_bytes=64, name="g_codes0_0")
         nc.sync.dma_start(out=gates[:, : TOP - 1, :], in_=gate[0 : TOP - 1, 0:P, :].rearrange("r p t -> p r t"))
         nc.sync.dma_start(out=gates[:, TOP - 1, CUT:T], in_=gate[TOP - 1, 0:P, CUT:T])
         words(1, 0, PIECE)
         for group in groups[:4]:
-            close_group(*group)
+            close_group(group)
         gather_scales(2, nc.sync)
-        ends = ((8 * C, C), (9 * C, C), (10 * C, C), (SLOTS - C, P), (SLOTS - P, P))
-        groups.extend(open_group(8 + k, lo, n) for k, (lo, n) in enumerate(ends[:4]))
-        for e in range(4, 8):
-            words(1, e * C, C)
-            close_group(*groups[e])
+        groups.extend(expert(e) for e in range(8, E - 1))
+        ends = (SLOTS - C, SLOTS - P)
+        upper = [open_group(E - 1, [(0, ends[0], P)])]
+        for e in range(4, E - 1):
+            if e % 2 == 0:
+                words(1, e * C, 2 * C if e < E - 2 else C)
+            close_group(groups[e])
             if e == 4:
-                groups.append(open_group(12, *ends[4]))
-        for (lo, n), group in zip(ends, groups[8:]):
-            words(1, lo, n)
-            close_group(*group)
+                upper.append(open_group(E, [(0, ends[1], P)]))
+            if e == 5:
+                lower = open_group(E + 1, [(1, lo, P) for lo in ends])
+        for k, lo in enumerate(ends):
+            words(1, lo, P)
+            close_group(upper[k])
+            second_pass(lower, k)
+        empty(lower[0][:], 1, ends[0], C)
         for dst, src, bias in left_over:
             nc.vector.tensor_scalar(dst, src, bias, 0.0, ADD, MAX)
 
         def picks(h, r, lo, hi):
             return y[h][:].indirect(pos_t[r][:, lo // 16 : hi // 16])
 
-        def product(h, r, lo, hi):
-            prod = keep.tile([P, hi - lo], F32, name=f"prod{r}_{h}_{lo}")
-            nc.vector.tensor_tensor(prod[:], picks(h, r, lo, hi), gates[:, r, lo:hi], MULT)
-            return prod
+        def product(dst, h, r, lo, hi):
+            nc.vector.tensor_tensor(dst, picks(h, r, lo, hi), gates[:, r, lo:hi], MULT)
 
-        def plain(h, lo, hi):
-            picked = keep.tile([P, hi - lo], F32, name=f"picked_{h}_{lo}")
-            nc.scalar.activation(picked[:], picks(h, TOP - 1, lo, hi), COPY)
-            return picked
+        def plain(dst, h, r, lo, hi):
+            nc.scalar.activation(dst, picks(h, r, lo, hi), COPY)
 
         def turn(ps, parts):
             n = ps.shape[1]
@@ -223,11 +241,12 @@ def tile_moe_tk_lin_relu_kernel(tc, xT, w_words, w_scales, b, gate, offs, pos1, 
                     nc.tensor.matmul(ps[:, o : o + P], part[:, o : o + P], ident[:], start=first, stop=last, is_transpose=True)
             return ps
 
+        choice = [[keep.tile([P, T], F32, name=f"choice{h}_{r}") for r in range(TOP)] for h in range(HALVES)]
+
         def forward(i):
             h, lo, hi = TURNED[i]
-            prods = [product(h, r, lo, hi) for r in range(TOP - 1)]
-            third = turn(bank(5 + 3 * i, hi - lo), [picked[i]])
-            both = turn(bank(6 + 3 * i, hi - lo), prods)
+            third = turn(bank(6 + 3 * i, hi - lo), [choice[h][2][:, lo:hi]])
+            both = turn(bank(7 + 3 * i, hi - lo), [choice[h][r][:, lo:hi] for r in range(2)])
             return third, both
 
         def by_token(i):
@@ -238,62 +257,72 @@ def tile_moe_tk_lin_relu_kernel(tc, xT, w_words, w_scales, b, gate, offs, pos1, 
                 block = (lo + o) // P
                 nc.scalar.activation(parts[0][:, o : o + P], third[:, o : o + P], COPY, scale=gate_by_token[:, block : block + 1])
             nc.scalar.copy(parts[1][:], both[:])
-            return turn(bank(7 + 3 * i, hi - lo), parts)
+            back.append(turn(bank(8 + 3 * i, hi - lo), [part[:] for part in parts]))
+
+        def store(h, lo, hi, total):
+            nc.sync.dma_start(out=out[h * P : (h + 1) * P, lo:hi], in_=total)
 
         def finish(i):
             h, lo, hi = TURNED[i]
             total = keep.tile([P, hi - lo], F32, name=f"total{h}_{lo}")
             nc.scalar.copy(total[:], back[i][:])
-            nc.sync.dma_start(out=out[h * P : (h + 1) * P, lo:hi], in_=total[:])
+            nc.scalar.dma_start(out=out[h * P : (h + 1) * P, lo:hi], in_=total[:])
 
-        three = [keep.tile([P, TOP, hi - lo], F32, name=f"three{h}_{lo}") for h, lo, hi, own in ADDED]
+        def third_choice(h, lo, hi):
+            plain(choice[h][2][:, lo:hi], h, 2, lo, hi)
 
-        def on_scalar(j):
-            h, lo, hi, own = ADDED[j]
-            for r in range(own, TOP):
-                nc.scalar.activation(three[j][:, r, :], picks(h, r, lo, hi), COPY)
+        def two_products(h, lo, hi):
+            for r in range(2):
+                product(choice[h][r][:, lo:hi], h, r, lo, hi)
 
-        def on_vector(j):
-            h, lo, hi, own = ADDED[j]
-            for r in range(own):
-                nc.vector.tensor_tensor(three[j][:, r, :], picks(h, r, lo, hi), gates[:, r, lo:hi], MULT)
+        rest = [keep.tile([P, TOP, T - CUT], F32, name=f"rest{h}") for h in range(HALVES)]
 
-        def weigh(j):
-            h, lo, hi, own = ADDED[j]
-            nc.vector.tensor_tensor(three[j][:, own:, :], three[j][:, own:, :], gates[:, own:, lo:hi], MULT)
+        def rest_on_scalar(h, r, lo, hi):
+            plain(rest[h][:, r, lo - CUT : hi - CUT], h, r, lo, hi)
 
-        def add(j, r, name=None):
-            h, lo, hi, own = ADDED[j]
-            dst = three[j][:, 0, :] if name is None else keep.tile([P, hi - lo], F32, name=name)[:]
-            nc.vector.tensor_tensor(dst, three[j][:, 0, :], three[j][:, r, :], ADD)
+        def rest_on_vector(h, hi):
+            product(rest[h][:, 0, : hi - CUT], h, 0, CUT, hi)
+
+        def weigh(h, r, lo, hi):
+            part = rest[h][:, r:, lo - CUT : hi - CUT]
+            nc.vector.tensor_tensor(part, part, gates[:, r:, lo:hi], MULT)
+
+        def add(h, r, lo, hi, name=None):
+            cols = slice(lo - CUT, hi - CUT)
+            dst = rest[h][:, 0, cols] if name is None else keep.tile([P, hi - lo], F32, name=name)[:]
+            nc.vector.tensor_tensor(dst, rest[h][:, 0, cols], rest[h][:, r, cols], ADD)
             if r == TOP - 1:
-                nc.sync.dma_start(out=out[h * P : (h + 1) * P, lo:hi], in_=dst)
+                store(h, lo, hi, dst)
 
-        picked = [plain(*piece) for piece in TURNED]
-        turned = [forward(i) for i in range(len(TURNED))]
-        back = [by_token(0)]
-        on_scalar(0)
+        turned, back = [], []
+        mid = T - P
+        for i in range(2):
+            third_choice(*TURNED[i])
+            two_products(*TURNED[i])
+            turned.append(forward(i))
+        third_choice(*TURNED[2])
+        by_token(0)
+        third_choice(*TURNED[3])
+        two_products(1, 0, CUT)
+        turned.extend(forward(i) for i in (2, 3))
+        rest_on_scalar(0, 1, CUT, T)
         finish(0)
-        back.append(by_token(1))
-        on_scalar(1)
-        back.append(by_token(2))
-        on_scalar(2)
-        on_scalar(3)
+        by_token(1)
+        rest_on_scalar(1, 1, CUT, T)
+        rest_on_scalar(0, 2, CUT, mid)
+        rest_on_scalar(1, 2, CUT, mid)
         finish(1)
+        by_token(2)
+        by_token(3)
+        for h in range(HALVES):
+            rest_on_scalar(h, 2, mid, T)
         finish(2)
-        on_vector(0)
-        weigh(0)
-        on_vector(1)
-        add(0, 1)
-        on_vector(2)
-        add(0, 2, "total0_0")
-        weigh(1)
-        on_vector(3)
-        add(1, 1)
-        weigh(2)
-        add(1, 2)
-        weigh(3)
-        add(2, 1)
-        add(3, 1)
-        add(2, 2)
-        add(3, 2)
+        finish(3)
+        for h in range(HALVES):
+            rest_on_vector(h, T)
+        for lo, hi in ((CUT, mid), (mid, T)):
+            for h in range(HALVES):
+                weigh(h, 1, lo, hi)
+            for r in (1, 2):
+                for h in range(HALVES):
+                    add(h, r, lo, hi)

@@ -174,7 +174,7 @@ def tile_moe_tk_lin_relu_kernel(tc, xT, w_words, w_scales, b, gate, offs, pos1, 
         def empty(src, h, lo, n):
             e = lo // C
             dst, bias = y[h][:, lo : lo + n], b_t[:, h, e : e + 1]
-            if h == 1 and lo >= H1_ON_VECTOR:
+            if (h == 1 and H1_ON_VECTOR <= lo < SLOTS - C) or (h, lo) == (0, SLOTS - P):
                 left_over.append((dst, src, bias))
             else:
                 nc.scalar.activation(dst, src, RELU, bias=bias)

@@ -28,9 +28,11 @@ SHIFT = 4
 PIECE = 1024
 CHUNKS = (((0, 256), (256, 256), (512, 256), (768, 128), (896, 128)), ((0, 256), (256, 256), (512, 256), (768, 256)))
 ON_SCALAR = ((96, 96, 112, 64, 48), (256, 256, 256, 256))
-TURNED = ((0, 0, 256), (0, 256, 640), (1, 0, 384), (1, 384, 640))
+TURNED = ((0, 256), (256, 512), (512, 640))
 CUT = 640
+LATE = 768
 SPARE = 1024
+BLOCKS = T // P
 H1_ON_VECTOR = 9 * C
 
 
@@ -64,7 +66,7 @@ def tile_moe_tk_lin_relu_kernel(tc, xT, w_words, w_scales, b, gate, offs, pos1, 
         b_t = keep.tile([P, HALVES, E], F32, name="b_t")
         y = [keep.tile([P, SLOTS], F32, name=f"y{h}") for h in range(HALVES)]
         gate_rows = keep.tile([P, P], F32, name="gate_rows")
-        gate_by_token = keep.tile([P, T // P], F32, name="gate_by_token")
+        gate_by_token = keep.tile([P, (TOP - 1) * BLOCKS], F32, name="gate_by_token")
 
         ident = keep.tile([P, P], F32, name="ident")
         make_identity(nc, ident[:])
@@ -93,7 +95,8 @@ def tile_moe_tk_lin_relu_kernel(tc, xT, w_words, w_scales, b, gate, offs, pos1, 
                 out=ws_t[32 * q : 32 * q + 4].bitcast(I32),
                 in_=ws_src[:, :, 4 * q : 4 * q + 4, :].rearrange("e a r n -> r (e a) n"),
             )
-        nc.sync.dma_start(out=gate_rows[0 : T // P, :], in_=gate[TOP - 1, 0, :].rearrange("(c p) -> c p", p=P))
+        for r in (1, 2):
+            nc.sync.dma_start(out=gate_rows[(r - 1) * BLOCKS : r * BLOCKS, :], in_=gate[r, 0, :].rearrange("(c p) -> c p", p=P))
         nc.sync.dma_start(out=b_t[:], in_=b.rearrange("(h p) e -> p h e", p=P))
         for g in (slice(0, 8), slice(8, E * PASSES)):
             nc.sync.dma_start(out=w_t[:, g, :].bitcast(I32), in_=w_src[:, g, :])
@@ -102,7 +105,7 @@ def tile_moe_tk_lin_relu_kernel(tc, xT, w_words, w_scales, b, gate, offs, pos1, 
 
         ps = bank(BANKS - 1, P)
         nc.tensor.transpose(ps[:], gate_rows[:], ident[:])
-        nc.scalar.copy(gate_by_token[:], ps[:, 0 : T // P])
+        nc.scalar.copy(gate_by_token[:], ps[:, 0 : (TOP - 1) * BLOCKS])
 
         def cast(engine, a, c, lo, hi):
             dst = grouped[a][c][:, lo:hi, :].rearrange("p (c i) j -> p c j i", i=4)
@@ -199,130 +202,114 @@ def tile_moe_tk_lin_relu_kernel(tc, xT, w_words, w_scales, b, gate, offs, pos1, 
         gather_scales(1, nc.sync)
         groups.extend(expert(e) for e in range(4, 8))
         gates = keep.tile([P, TOP, T], F32, align_bytes=64, name="g_codes0_0")
-        nc.sync.dma_start(out=gates[:, : TOP - 1, :], in_=gate[0 : TOP - 1, 0:P, :].rearrange("r p t -> p r t"))
-        nc.sync.dma_start(out=gates[:, TOP - 1, CUT:T], in_=gate[TOP - 1, 0:P, CUT:T])
+        nc.sync.dma_start(out=gates[:, 0, :], in_=gate[0, 0:P, :])
+        nc.sync.dma_start(out=gates[:, 1:, CUT:T], in_=gate[1:, 0:P, CUT:T].rearrange("r p t -> p r t"))
         words(1, 0, PIECE)
         for group in groups[:4]:
             close_group(group)
         gather_scales(2, nc.sync)
         groups.extend(expert(e) for e in range(8, E - 1))
         ends = (SLOTS - C, SLOTS - P)
-        upper = [open_group(E - 1, [(0, ends[0], P)])]
+        groups.append(open_group(E - 1, [(h, ends[0], P) for h in range(HALVES)]))
         for e in range(4, E - 1):
             if e % 2 == 0:
                 words(1, e * C, 2 * C if e < E - 2 else C)
             close_group(groups[e])
-            if e == 4:
-                upper.append(open_group(E, [(0, ends[1], P)]))
-            if e == 5:
-                lower = open_group(E + 1, [(1, lo, P) for lo in ends])
-        for k, lo in enumerate(ends):
-            words(1, lo, P)
-            close_group(upper[k])
-            second_pass(lower, k)
-        empty(lower[0][:], 1, ends[0], C)
+            if e in (4, 5):
+                groups.append(open_group(E + e - 4, [(e - 4, ends[1], P)]))
+        words(1, ends[0], P)
+        close_group(groups[E - 1])
+        words(1, ends[1], P)
+        close_group(groups[E])
+        close_group(groups[E + 1])
         for dst, src, bias in left_over:
             nc.vector.tensor_scalar(dst, src, bias, 0.0, ADD, MAX)
 
         def picks(h, r, lo, hi):
             return y[h][:].indirect(pos_t[r][:, lo // 16 : hi // 16])
 
-        def product(dst, h, r, lo, hi):
+        choice = [[keep.tile([P, T], F32, name=f"choice{h}_{r}") for r in (1, 2)] for h in range(HALVES)]
+        first = keep.tile([P, HALVES, T], F32, name="first")
+        out_by_half = out.rearrange("(h p) t -> p h t", p=P)
+
+        def product(h, r, lo, hi):
+            dst = first[:, h, lo:hi] if r == 0 else choice[h][r - 1][:, lo:hi]
             nc.vector.tensor_tensor(dst, picks(h, r, lo, hi), gates[:, r, lo:hi], MULT)
 
-        def plain(dst, h, r, lo, hi):
-            nc.scalar.activation(dst, picks(h, r, lo, hi), COPY)
+        def plain(h, r, lo, hi):
+            nc.scalar.activation(choice[h][r - 1][:, lo:hi], picks(h, r, lo, hi), COPY)
 
-        def turn(ps, parts):
-            n = ps.shape[1]
-            for r, part in enumerate(parts):
-                for o in range(0, n, P):
-                    first, last = (r, o) == (0, 0), (r, o) == (len(parts) - 1, n - P)
-                    nc.tensor.matmul(ps[:, o : o + P], part[:, o : o + P], ident[:], start=first, stop=last, is_transpose=True)
-            return ps
+        turned, back = {}, {}
 
-        choice = [[keep.tile([P, T], F32, name=f"choice{h}_{r}") for r in range(TOP)] for h in range(HALVES)]
+        def forward(i, r, number):
+            lo, hi = TURNED[i]
+            ps = bank(number, HALVES * (hi - lo))
+            for h in range(HALVES):
+                plain(h, r, lo, hi)
+                for at in range(lo, hi, P):
+                    col = HALVES * (at - lo) + h * P
+                    opens, closes = (h, at) == (0, lo), (h, at) == (HALVES - 1, hi - P)
+                    nc.tensor.matmul(ps[:, col : col + P], choice[h][r - 1][:, at : at + P], ident[:], start=opens, stop=closes, is_transpose=True)
+            turned[i, r] = ps
 
-        def forward(i):
-            h, lo, hi = TURNED[i]
-            third = turn(bank(6 + 3 * i, hi - lo), [choice[h][2][:, lo:hi]])
-            both = turn(bank(7 + 3 * i, hi - lo), [choice[h][r][:, lo:hi] for r in range(2)])
-            return third, both
-
-        def by_token(i):
-            h, lo, hi = TURNED[i]
-            third, both = turned[i]
-            parts = [keep.tile([P, hi - lo], F32, name=f"by_token{r}_{h}_{lo}") for r in range(2)]
-            for o in range(0, hi - lo, P):
-                block = (lo + o) // P
-                nc.scalar.activation(parts[0][:, o : o + P], third[:, o : o + P], COPY, scale=gate_by_token[:, block : block + 1])
-            nc.scalar.copy(parts[1][:], both[:])
-            back.append(turn(bank(8 + 3 * i, hi - lo), [part[:] for part in parts]))
-
-        def store(h, lo, hi, total):
-            nc.sync.dma_start(out=out[h * P : (h + 1) * P, lo:hi], in_=total)
+        def weigh_and_return(i, number, choices):
+            lo, hi = TURNED[i]
+            n = hi - lo
+            ps = back[i] if i in back else bank(number, HALVES * n)
+            for r in choices:
+                by_token = keep.tile([P, HALVES * n], F32, name=f"by_token{r}_{lo}")
+                for at in range(lo, hi, P):
+                    cols = slice(HALVES * (at - lo), HALVES * (at - lo + P))
+                    column = (r - 1) * BLOCKS + at // P
+                    nc.scalar.activation(by_token[:, cols], turned[i, r][:, cols], COPY, scale=gate_by_token[:, column : column + 1])
+                    for h in range(HALVES):
+                        col, to = HALVES * (at - lo) + h * P, h * n + at - lo
+                        opens, closes = (r, at, h) == (1, lo, 0), (r, at, h) == (2, hi - P, HALVES - 1)
+                        nc.tensor.matmul(ps[:, to : to + P], by_token[:, col : col + P], ident[:], start=opens, stop=closes, is_transpose=True)
+            back[i] = ps
 
         def finish(i):
-            h, lo, hi = TURNED[i]
-            total = keep.tile([P, hi - lo], F32, name=f"total{h}_{lo}")
-            nc.scalar.copy(total[:], back[i][:])
-            nc.scalar.dma_start(out=out[h * P : (h + 1) * P, lo:hi], in_=total[:])
+            lo, hi = TURNED[i]
+            total = keep.tile([P, HALVES, hi - lo], F32, name=f"total{lo}")
+            nc.vector.tensor_tensor(total[:], back[i][:].rearrange("p (h t) -> p h t", h=HALVES), first[:, :, lo:hi], ADD)
+            nc.sync.dma_start(out=out_by_half[:, :, lo:hi], in_=total[:])
 
-        def third_choice(h, lo, hi):
-            plain(choice[h][2][:, lo:hi], h, 2, lo, hi)
-
-        def two_products(h, lo, hi):
-            for r in range(2):
-                product(choice[h][r][:, lo:hi], h, r, lo, hi)
-
-        rest = [keep.tile([P, TOP, T - CUT], F32, name=f"rest{h}") for h in range(HALVES)]
-
-        def rest_on_scalar(h, r, lo, hi):
-            plain(rest[h][:, r, lo - CUT : hi - CUT], h, r, lo, hi)
-
-        def rest_on_vector(h, hi):
-            product(rest[h][:, 0, : hi - CUT], h, 0, CUT, hi)
-
-        def weigh(h, r, lo, hi):
-            part = rest[h][:, r:, lo - CUT : hi - CUT]
-            nc.vector.tensor_tensor(part, part, gates[:, r:, lo:hi], MULT)
-
-        def add(h, r, lo, hi, name=None):
-            cols = slice(lo - CUT, hi - CUT)
-            dst = rest[h][:, 0, cols] if name is None else keep.tile([P, hi - lo], F32, name=name)[:]
-            nc.vector.tensor_tensor(dst, rest[h][:, 0, cols], rest[h][:, r, cols], ADD)
+        def add(h, r, lo, hi):
+            src = first[:, h, lo:hi] if r == 1 else choice[h][0][:, lo:hi]
+            dst = choice[h][r - 1][:, lo:hi]
+            nc.vector.tensor_tensor(dst, src, dst, ADD)
             if r == TOP - 1:
-                store(h, lo, hi, dst)
+                nc.sync.dma_start(out=out[h * P : (h + 1) * P, lo:hi], in_=dst)
 
-        turned, back = [], []
         mid = T - P
-        for i in range(2):
-            third_choice(*TURNED[i])
-            two_products(*TURNED[i])
-            turned.append(forward(i))
-        third_choice(*TURNED[2])
-        by_token(0)
-        third_choice(*TURNED[3])
-        two_products(1, 0, CUT)
-        turned.extend(forward(i) for i in (2, 3))
-        rest_on_scalar(0, 1, CUT, T)
+        forward(0, 1, 6)
+        forward(0, 2, 7)
+        forward(1, 1, 0)
+        weigh_and_return(0, 1, (1, 2))
+        forward(1, 2, 2)
+        forward(2, 1, 3)
+        weigh_and_return(1, 4, (1,))
+        forward(2, 2, 5)
+        weigh_and_return(1, 4, (2,))
+        weigh_and_return(2, 6, (1, 2))
+        late = choice[1][1][:, CUT - (T - LATE) : CUT]
+        nc.scalar.activation(late, picks(1, 2, LATE, T), COPY)
+
+        product(0, 0, 0, T)
+        product(1, 0, 0, T)
+        product(0, 1, CUT, T)
+        product(0, 2, CUT, T)
+        add(0, 1, CUT, T)
         finish(0)
-        by_token(1)
-        rest_on_scalar(1, 1, CUT, T)
-        rest_on_scalar(0, 2, CUT, mid)
-        rest_on_scalar(1, 2, CUT, mid)
+        add(0, 2, CUT, T)
+        product(1, 1, CUT, T)
+        product(1, 2, CUT, LATE)
+        add(1, 1, CUT, T)
         finish(1)
-        by_token(2)
-        by_token(3)
-        for h in range(HALVES):
-            rest_on_scalar(h, 2, mid, T)
+        add(1, 2, CUT, LATE)
         finish(2)
-        finish(3)
-        for h in range(HALVES):
-            rest_on_vector(h, T)
-        for lo, hi in ((CUT, mid), (mid, T)):
-            for h in range(HALVES):
-                weigh(h, 1, lo, hi)
-            for r in (1, 2):
-                for h in range(HALVES):
-                    add(h, r, lo, hi)
+        nc.vector.tensor_tensor(late, late, gates[:, 2, LATE:T], MULT)
+        for lo, hi in ((LATE, mid), (mid, T)):
+            part = late[:, lo - LATE : hi - LATE]
+            nc.vector.tensor_tensor(part, part, choice[1][0][:, lo:hi], ADD)
+            nc.sync.dma_start(out=out[P:N, lo:hi], in_=part)

@@ -28,9 +28,8 @@ SHIFT = 4
 PIECE = 1024
 CHUNKS = (((0, 256), (256, 256), (512, 256), (768, 128), (896, 128)), ((0, 256), (256, 256), (512, 256), (768, 256)))
 ON_SCALAR = ((96, 96, 112, 64, 48), (256, 256, 256, 256))
-TURNED = ((0, 256), (256, 512), (512, 640))
+TURNED = ((2, 0, 256), (2, 256, 512), (2, 512, 640), (1, 640, 768))
 CUT = 640
-LATE = 768
 SPARE = 1024
 BLOCKS = T // P
 H1_ON_VECTOR = 9 * C
@@ -242,37 +241,37 @@ def tile_moe_tk_lin_relu_kernel(tc, xT, w_words, w_scales, b, gate, offs, pos1, 
         turned, back = {}, {}
 
         def forward(i, r, number):
-            lo, hi = TURNED[i]
-            ps = bank(number, HALVES * (hi - lo))
-            for h in range(HALVES):
+            halves, lo, hi = TURNED[i]
+            ps = bank(number, halves * (hi - lo))
+            for h in range(halves):
                 plain(h, r, lo, hi)
                 for at in range(lo, hi, P):
-                    col = HALVES * (at - lo) + h * P
-                    opens, closes = (h, at) == (0, lo), (h, at) == (HALVES - 1, hi - P)
+                    col = halves * (at - lo) + h * P
+                    opens, closes = (h, at) == (0, lo), (h, at) == (halves - 1, hi - P)
                     nc.tensor.matmul(ps[:, col : col + P], choice[h][r - 1][:, at : at + P], ident[:], start=opens, stop=closes, is_transpose=True)
             turned[i, r] = ps
 
         def weigh_and_return(i, number, choices):
-            lo, hi = TURNED[i]
+            halves, lo, hi = TURNED[i]
             n = hi - lo
-            ps = back[i] if i in back else bank(number, HALVES * n)
+            ps = back[i] if i in back else bank(number, halves * n)
             for r in choices:
-                by_token = keep.tile([P, HALVES * n], F32, name=f"by_token{r}_{lo}")
+                by_token = keep.tile([P, halves * n], F32, name=f"by_token{r}_{lo}")
                 for at in range(lo, hi, P):
-                    cols = slice(HALVES * (at - lo), HALVES * (at - lo + P))
+                    cols = slice(halves * (at - lo), halves * (at - lo + P))
                     column = (r - 1) * BLOCKS + at // P
                     nc.scalar.activation(by_token[:, cols], turned[i, r][:, cols], COPY, scale=gate_by_token[:, column : column + 1])
-                    for h in range(HALVES):
-                        col, to = HALVES * (at - lo) + h * P, h * n + at - lo
-                        opens, closes = (r, at, h) == (1, lo, 0), (r, at, h) == (2, hi - P, HALVES - 1)
+                    for h in range(halves):
+                        col, to = halves * (at - lo) + h * P, h * n + at - lo
+                        opens, closes = (r, at, h) == (1, lo, 0), (r, at, h) == (2, hi - P, halves - 1)
                         nc.tensor.matmul(ps[:, to : to + P], by_token[:, col : col + P], ident[:], start=opens, stop=closes, is_transpose=True)
             back[i] = ps
 
         def finish(i):
-            lo, hi = TURNED[i]
-            total = keep.tile([P, HALVES, hi - lo], F32, name=f"total{lo}")
-            nc.vector.tensor_tensor(total[:], back[i][:].rearrange("p (h t) -> p h t", h=HALVES), first[:, :, lo:hi], ADD)
-            nc.sync.dma_start(out=out_by_half[:, :, lo:hi], in_=total[:])
+            halves, lo, hi = TURNED[i]
+            total = keep.tile([P, halves, hi - lo], F32, name=f"total{lo}")
+            nc.vector.tensor_tensor(total[:], back[i][:].rearrange("p (h t) -> p h t", h=halves), first[:, :halves, lo:hi], ADD)
+            nc.sync.dma_start(out=out_by_half[:, :halves, lo:hi], in_=total[:])
 
         def add(h, r, lo, hi):
             src = first[:, h, lo:hi] if r == 1 else choice[h][0][:, lo:hi]
@@ -281,35 +280,32 @@ def tile_moe_tk_lin_relu_kernel(tc, xT, w_words, w_scales, b, gate, offs, pos1, 
             if r == TOP - 1:
                 nc.sync.dma_start(out=out[h * P : (h + 1) * P, lo:hi], in_=dst)
 
-        mid = T - P
         forward(0, 1, 6)
         forward(0, 2, 7)
         forward(1, 1, 0)
         weigh_and_return(0, 1, (1, 2))
         forward(1, 2, 2)
-        forward(2, 1, 3)
         weigh_and_return(1, 4, (1,))
-        forward(2, 2, 5)
+        forward(2, 1, 3)
         weigh_and_return(1, 4, (2,))
-        weigh_and_return(2, 6, (1, 2))
-        late = choice[1][1][:, CUT - (T - LATE) : CUT]
-        nc.scalar.activation(late, picks(1, 2, LATE, T), COPY)
+        forward(2, 2, 5)
+        forward(3, 1, 6)
+        forward(3, 2, 0)
+        weigh_and_return(2, 7, (1, 2))
+        weigh_and_return(3, 2, (1, 2))
 
+        rest = TURNED[3][2]
         product(0, 0, 0, T)
         product(1, 0, 0, T)
-        product(0, 1, CUT, T)
-        product(0, 2, CUT, T)
-        add(0, 1, CUT, T)
-        finish(0)
-        add(0, 2, CUT, T)
         product(1, 1, CUT, T)
-        product(1, 2, CUT, LATE)
+        product(1, 2, CUT, T)
         add(1, 1, CUT, T)
+        finish(0)
+        add(1, 2, CUT, T)
+        product(0, 1, rest, T)
+        product(0, 2, rest, T)
+        add(0, 1, rest, T)
         finish(1)
-        add(1, 2, CUT, LATE)
+        add(0, 2, rest, T)
         finish(2)
-        nc.vector.tensor_tensor(late, late, gates[:, 2, LATE:T], MULT)
-        for lo, hi in ((LATE, mid), (mid, T)):
-            part = late[:, lo - LATE : hi - LATE]
-            nc.vector.tensor_tensor(part, part, choice[1][0][:, lo:hi], ADD)
-            nc.sync.dma_start(out=out[P:N, lo:hi], in_=part)
+        finish(3)

@@ -231,12 +231,9 @@ def tile_moe_tk_lin_relu_kernel(tc, xT, w_words, w_scales, b, gate, offs, pos1, 
         first = keep.tile([P, HALVES, T], F32, name="first")
         out_by_half = out.rearrange("(h p) t -> p h t", p=P)
 
-        def product(h, r, lo, hi):
-            dst = first[:, h, lo:hi] if r == 0 else choice[h][r - 1][:, lo:hi]
+        def product(dst, h, r, lo, hi):
             nc.vector.tensor_tensor(dst, picks(h, r, lo, hi), gates[:, r, lo:hi], MULT)
 
-        def plain(h, r, lo, hi):
-            nc.scalar.activation(choice[h][r - 1][:, lo:hi], picks(h, r, lo, hi), COPY)
 
         turned, back = {}, {}
 
@@ -244,11 +241,12 @@ def tile_moe_tk_lin_relu_kernel(tc, xT, w_words, w_scales, b, gate, offs, pos1, 
             halves, lo, hi = TURNED[i]
             ps = bank(number, halves * (hi - lo))
             for h in range(halves):
-                plain(h, r, lo, hi)
+                picked = choice[h][r - 1][:, lo:hi]
+                nc.scalar.activation(picked, picks(h, r, lo, hi), COPY)
                 for at in range(lo, hi, P):
                     col = halves * (at - lo) + h * P
                     opens, closes = (h, at) == (0, lo), (h, at) == (halves - 1, hi - P)
-                    nc.tensor.matmul(ps[:, col : col + P], choice[h][r - 1][:, at : at + P], ident[:], start=opens, stop=closes, is_transpose=True)
+                    nc.tensor.matmul(ps[:, col : col + P], picked[:, at - lo : at - lo + P], ident[:], start=opens, stop=closes, is_transpose=True)
             turned[i, r] = ps
 
         def weigh_and_return(i, number, choices):
@@ -273,21 +271,19 @@ def tile_moe_tk_lin_relu_kernel(tc, xT, w_words, w_scales, b, gate, offs, pos1, 
             nc.vector.tensor_tensor(total[:], back[i][:].rearrange("p (h t) -> p h t", h=halves), first[:, :halves, lo:hi], ADD)
             nc.sync.dma_start(out=out_by_half[:, :halves, lo:hi], in_=total[:])
 
-        def add(h, r, lo, hi):
-            src = first[:, h, lo:hi] if r == 1 else choice[h][0][:, lo:hi]
-            dst = choice[h][r - 1][:, lo:hi]
-            nc.vector.tensor_tensor(dst, src, dst, ADD)
-            if r == TOP - 1:
-                nc.sync.dma_start(out=out[h * P : (h + 1) * P, lo:hi], in_=dst)
+        def add(dst, one, other):
+            nc.vector.tensor_tensor(dst, one, other, ADD)
+
+        def after(i, r, width):
+            return keep.tile([P, width], F32, name=f"by_token{r}_{TURNED[i][1]}")
 
         forward(0, 1, 6)
         forward(0, 2, 7)
         forward(1, 1, 0)
         weigh_and_return(0, 1, (1, 2))
         forward(1, 2, 2)
-        weigh_and_return(1, 4, (1,))
+        weigh_and_return(1, 4, (1, 2))
         forward(2, 1, 3)
-        weigh_and_return(1, 4, (2,))
         forward(2, 2, 5)
         forward(3, 1, 6)
         forward(3, 2, 0)
@@ -295,17 +291,24 @@ def tile_moe_tk_lin_relu_kernel(tc, xT, w_words, w_scales, b, gate, offs, pos1, 
         weigh_and_return(3, 2, (1, 2))
 
         rest = TURNED[3][2]
-        product(0, 0, 0, T)
-        product(1, 0, 0, T)
-        product(1, 1, CUT, T)
-        product(1, 2, CUT, T)
-        add(1, 1, CUT, T)
+        for h in range(HALVES):
+            product(first[:, h, :], h, 0, 0, T)
+        second, third = (choice[1][r][:, CUT:T] for r in range(2))
+        product(second, 1, 1, CUT, T)
+        product(third, 1, 2, CUT, T)
+        two = choice[0][0][:, rest:T]
+        product(two, 0, 1, rest, T)
         finish(0)
-        add(1, 2, CUT, T)
-        product(0, 1, rest, T)
-        product(0, 2, rest, T)
-        add(0, 1, rest, T)
+        lower = after(0, 1, T - CUT)
+        upper = after(0, 2, 2 * (T - rest))
+        add(lower[:], first[:, 1, CUT:T], second)
+        product(upper[:, : T - rest], 0, 2, rest, T)
+        add(lower[:], lower[:], third)
+        nc.sync.dma_start(out=out[P:N, CUT:T], in_=lower[:])
+        add(upper[:, T - rest :], two, first[:, 0, rest:T])
         finish(1)
-        add(0, 2, rest, T)
+        total = after(1, 2, T - rest)
+        add(total[:], upper[:, T - rest :], upper[:, : T - rest])
+        nc.sync.dma_start(out=out[0:P, rest:T], in_=total[:])
         finish(2)
         finish(3)

@@ -24,15 +24,19 @@ PASSES = K // 512
 SLOTS = E * C
 HALVES = N // P
 BANKS = 8
-SHIFT = 4
-PIECE = 1024
-CHUNKS = (((0, 256), (256, 256), (512, 256), (768, 128), (896, 128)), ((0, 256), (256, 256), (512, 256), (768, 256)))
-ON_SCALAR = ((96, 96, 112, 64, 48), (256, 256, 256, 256))
+QUADRANT = 32
+PACK = 4
+
+X_LOADS = (((0, 256), (256, 256), (512, 256), (768, 128), (896, 128)), ((0, 256), (256, 256), (512, 256), (768, 256)))
+CAST_ON_SCALAR = ((96, 96, 112, 64, 48), (256, 256, 256, 256))
+QUANTISE_RUN = 512
+BYTE_RUN = 1024
+SPARE_WORDS = 1024
+SPARE_BYTES = 384
+HALF_1_ON_VECTOR = (9, 10)
 TURNED = ((2, 0, 256), (2, 256, 512), (2, 512, 640), (1, 640, 768))
-CUT = 640
-SPARE = 1024
-BLOCKS = T // P
-H1_ON_VECTOR = 9 * C
+ALONE_FROM = (768, 640)
+TURNED_BLOCKS = ALONE_FROM[0] // P
 
 
 def tile_moe_tk_lin_relu_kernel(tc, xT, w_words, w_scales, b, gate, offs, pos1, pos2, pos3, out):
@@ -48,24 +52,24 @@ def tile_moe_tk_lin_relu_kernel(tc, xT, w_words, w_scales, b, gate, offs, pos1, 
         offs_t = lists.tile([P, SLOTS // 16], U16, name="offs_t")
         pos_t = [lists.tile([P, T // 16], U16, name=f"pos{r}_t") for r in range(TOP)]
 
-        raw = [[keep.tile([P, 4, n], F32, align_bytes=64, name=f"raw{a}_{lo}") for lo, n in CHUNKS[a]] for a in range(PASSES)]
+        raw = [[keep.tile([P, PACK, n], F32, align_bytes=64, name=f"raw{a}_{lo}") for lo, n in X_LOADS[a]] for a in range(PASSES)]
         grouped = [
-            [keep.tile([P, n, 4], BF16, align_bytes=64, name=f"grouped0_{lo}") for lo, n in CHUNKS[0]],
+            [keep.tile([P, n, PACK], BF16, align_bytes=64, name=f"grouped0_{lo}") for lo, n in X_LOADS[0]],
         ]
-        pairs = [keep.tile([P, 512, 4], BF16, align_bytes=64, name=f"grouped1_{lo}") for lo in (0, 512)]
-        grouped.append([pairs[lo // 512][:, lo % 512 : lo % 512 + n, :] for lo, n in CHUNKS[1]])
-        codes = keep.tile([P, 2 * T + SPARE], U32, align_bytes=64, name="codes")
+        runs = [keep.tile([P, QUANTISE_RUN, PACK], BF16, align_bytes=64, name=f"grouped1_{lo}") for lo in range(0, T, QUANTISE_RUN)]
+        grouped.append([runs[lo // QUANTISE_RUN][:, lo % QUANTISE_RUN : lo % QUANTISE_RUN + n, :] for lo, n in X_LOADS[1]])
+        codes = keep.tile([P, PASSES * T + SPARE_WORDS], U32, align_bytes=64, name="codes")
         first_word = (T, 0)
-        scales = keep.tile([P, T + 384], U8, align_bytes=64, name="scales")
-        g_codes = [{}, {}]
-        g_scales = [keep.tile([P, PIECE], U8, align_bytes=64, name=f"g_scales_{c}") for c in range(SLOTS // PIECE)]
-        g_scales1 = [keep.tile([P, PIECE], U8, align_bytes=64, name=f"g_scales1_{c}") for c in range(SLOTS // PIECE)]
+        scales = keep.tile([P, T + SPARE_BYTES], U8, align_bytes=64, name="scales")
+        slot_words = [{}, {}]
+        slot_scales = [keep.tile([P, BYTE_RUN], U8, align_bytes=64, name=f"slot_scales_{c}") for c in range(SLOTS // BYTE_RUN)]
+        slot_scales1 = [keep.tile([P, BYTE_RUN], U8, align_bytes=64, name=f"slot_scales1_{c}") for c in range(SLOTS // BYTE_RUN)]
         w_t = keep.tile([P, E * PASSES, 2 * N], U8, align_bytes=64, name="w_t")
         ws_t = keep.tile([P, E * PASSES, N], U8, align_bytes=64, name="ws_t")
         b_t = keep.tile([P, HALVES, E], F32, name="b_t")
         y = [keep.tile([P, SLOTS], F32, name=f"y{h}") for h in range(HALVES)]
         gate_rows = keep.tile([P, P], F32, name="gate_rows")
-        gate_by_token = keep.tile([P, (TOP - 1) * BLOCKS], F32, name="gate_by_token")
+        gate_by_token = keep.tile([P, (TOP - 1) * TURNED_BLOCKS], F32, name="gate_by_token")
 
         ident = keep.tile([P, P], F32, name="ident")
         make_identity(nc, ident[:])
@@ -73,87 +77,91 @@ def tile_moe_tk_lin_relu_kernel(tc, xT, w_words, w_scales, b, gate, offs, pos1, 
         nc.gpsimd.memset(gate_rows[:], 0.0)
         nc.vector.memset(scales[:].bitcast(I32), 0)
         nc.vector.memset(ws_t[:].rearrange("p g n -> p (g n)").bitcast(I32), 0)
-        nc.vector.memset(codes[:, 2 * T :].bitcast(I32), 0)
-        for c in range(SLOTS // PIECE):
-            nc.vector.memset(g_scales1[c][:].bitcast(I32), 0)
+        nc.vector.memset(codes[:, PASSES * T :].bitcast(I32), 0)
+        for c in range(SLOTS // BYTE_RUN):
+            nc.vector.memset(slot_scales1[c][:].bitcast(I32), 0)
 
         def load_x(a, c):
-            lo, n = CHUNKS[a][c]
-            src = xT[512 * a : 512 * (a + 1), lo : lo + n].rearrange("(p j) w -> p j w", j=4)
+            lo, n = X_LOADS[a][c]
+            src = xT[512 * a : 512 * (a + 1), lo : lo + n].rearrange("(p j) w -> p j w", j=PACK)
             nc.sync.dma_start(out=raw[a][c][:], in_=src)
 
-        for c in range(len(CHUNKS[0])):
+        for c in range(len(X_LOADS[0])):
             load_x(0, c)
         nc.sync.dma_start(offs_t[:], offs)
-        for c in range(len(CHUNKS[1])):
+        for c in range(len(X_LOADS[1])):
             load_x(1, c)
         w_src = w_words.bitcast(I32).rearrange("e a p n -> p (e a) n")
         ws_src = w_scales.bitcast(I32)
-        for q in range(4):
+        for q in range(P // QUADRANT):
             nc.sync.dma_start(
-                out=ws_t[32 * q : 32 * q + 4].bitcast(I32),
-                in_=ws_src[:, :, 4 * q : 4 * q + 4, :].rearrange("e a r n -> r (e a) n"),
+                out=ws_t[QUADRANT * q : QUADRANT * q + PACK].bitcast(I32),
+                in_=ws_src[:, :, PACK * q : PACK * (q + 1), :].rearrange("e a r n -> r (e a) n"),
             )
         for r in (1, 2):
-            nc.sync.dma_start(out=gate_rows[(r - 1) * BLOCKS : r * BLOCKS, :], in_=gate[r, 0, :].rearrange("(c p) -> c p", p=P))
+            rows = slice((r - 1) * TURNED_BLOCKS, r * TURNED_BLOCKS)
+            nc.sync.dma_start(out=gate_rows[rows, :], in_=gate[r, 0, : TURNED_BLOCKS * P].rearrange("(c p) -> c p", p=P))
         nc.sync.dma_start(out=b_t[:], in_=b.rearrange("(h p) e -> p h e", p=P))
-        for g in (slice(0, 8), slice(8, E * PASSES)):
+        first_run = BYTE_RUN // C * PASSES
+        for g in (slice(0, first_run), slice(first_run, E * PASSES)):
             nc.sync.dma_start(out=w_t[:, g, :].bitcast(I32), in_=w_src[:, g, :])
         for r, src in enumerate((pos1, pos2, pos3)):
             nc.sync.dma_start(pos_t[r][:], src)
 
-        ps = bank(BANKS - 1, P)
-        nc.tensor.transpose(ps[:], gate_rows[:], ident[:])
-        nc.scalar.copy(gate_by_token[:], ps[:, 0 : (TOP - 1) * BLOCKS])
+        gates_turned = bank(BANKS - 1, P)
+        nc.tensor.transpose(gates_turned[:], gate_rows[:], ident[:])
+        nc.scalar.copy(gate_by_token[:], gates_turned[:, 0 : (TOP - 1) * TURNED_BLOCKS])
 
-        def cast(engine, a, c, lo, hi):
+        def cast(on_scalar, a, c, lo, hi):
             dst = grouped[a][c][:, lo:hi, :].rearrange("p (c i) j -> p c j i", i=4)
             src = raw[a][c][:, :, lo:hi].rearrange("p j (c i) -> p c j i", i=4)
-            if engine == "v":
-                nc.vector.tensor_copy(out=dst, in_=src)
-            else:
+            if on_scalar:
                 nc.scalar.activation(dst, src, COPY)
+            else:
+                nc.vector.tensor_copy(out=dst, in_=src)
 
-        def quantize(a, lo, n, src):
+        def quantise(a, lo, n, src):
             nc.vector.quantize_mx(
                 out=codes[:, first_word[a] + lo : first_word[a] + lo + n].bitcast(FP8X4),
-                scales=scales[SHIFT * a : P, lo : lo + n],
+                scales=scales[PACK * a : P, lo : lo + n],
                 in_=src[:].rearrange("p w j -> p (w j)"),
             )
 
         for a in range(PASSES):
-            for c in range(len(CHUNKS[a])):
-                n, cut = CHUNKS[a][c][1], ON_SCALAR[a][c]
-                cast("s", a, c, 0, cut)
-                if cut < n:
-                    cast("v", a, c, cut, n)
+            for c, (lo, n) in enumerate(X_LOADS[a]):
+                share = CAST_ON_SCALAR[a][c]
+                cast(True, a, c, 0, share)
+                if share < n:
+                    cast(False, a, c, share, n)
                 if a == 0:
-                    quantize(a, CHUNKS[a][c][0], n, grouped[a][c])
+                    quantise(a, lo, n, grouped[a][c])
 
-        def words(a, lo, n):
-            held = (a, lo) == (0, SLOTS - C)
-            dst = keep.tile([P, n], U32, align_bytes=64, name="raw1_768" if held else f"g_codes{a}_{lo}")
-            wide = T if n < T else (T + SPARE, 2 * T)[a]
-            window = codes[:, first_word[a] : first_word[a] + wide]
+        def gather_words(a, lo, n, buffer=None):
+            dst = keep.tile([P, n], U32, align_bytes=64, name=buffer or f"slot_words{a}_{lo}")
+            width = T if n < T else (T + SPARE_WORDS, PASSES * T)[a]
+            window = codes[:, first_word[a] : first_word[a] + width]
             nc.vector.tensor_copy(dst[:], window.indirect(offs_t[:, lo // 16 : (lo + n) // 16]))
             for at in range(lo, lo + n, P):
-                g_codes[a][at] = (dst, at - lo)
+                slot_words[a][at] = (dst, at - lo)
 
-        def gather_scales(c, queue):
-            nc.vector.tensor_copy(g_scales[c][:], scales[:].indirect(offs_t[:, PIECE * c // 16 : PIECE * (c + 1) // 16]))
-            for q in range(0, P, 32):
-                queue.dma_start(out=g_scales1[c][q : q + 4, :].bitcast(I32), in_=g_scales[c][q + SHIFT : q + SHIFT + 4, :].bitcast(I32))
+        def gather_scales(c):
+            nc.vector.tensor_copy(slot_scales[c][:], scales[:].indirect(offs_t[:, BYTE_RUN * c // 16 : BYTE_RUN * (c + 1) // 16]))
+            for q in range(0, P, QUADRANT):
+                nc.sync.dma_start(
+                    out=slot_scales1[c][q : q + PACK, :].bitcast(I32),
+                    in_=slot_scales[c][q + PACK : q + 2 * PACK, :].bitcast(I32),
+                )
 
         def one_pass(ps, h, lo, n, a, start, stop):
             g = lo // C * PASSES + a
-            c, col = divmod(lo, PIECE)
-            src, at = g_codes[a][lo]
+            c, col = divmod(lo, BYTE_RUN)
+            src, at = slot_words[a][lo]
             nc.tensor.matmul_mx(
                 out=ps,
                 lhsT=w_t[:, g, 2 * P * h : 2 * P * (h + 1)].bitcast(FP4X4),
                 lhsT_scale=ws_t[:, g, P * h : P * (h + 1)],
                 rhs=src[:, at : at + n].bitcast(FP8X4),
-                rhs_scale=(g_scales, g_scales1)[a][c][:, col : col + n],
+                rhs_scale=(slot_scales, slot_scales1)[a][c][:, col : col + n],
                 start=start,
                 stop=stop,
             )
@@ -165,64 +173,60 @@ def tile_moe_tk_lin_relu_kernel(tc, xT, w_words, w_scales, b, gate, offs, pos1, 
                 views.append(ps[:, at : at + n])
                 one_pass(views[-1], h, lo, n, 0, at == 0, False)
                 at = at + n
-            return ps, views, parts
+            return views, parts
 
-        def second_pass(group, k):
-            ps, views, parts = group
-            one_pass(views[k], *parts[k], 1, False, k == len(parts) - 1)
+        for_vector = []
 
-        left_over = []
+        def close_group(views, parts):
+            for k, (view, part) in enumerate(zip(views, parts)):
+                one_pass(view, *part, 1, False, k == len(parts) - 1)
+            for view, (h, lo, n) in zip(views, parts):
+                e = lo // C
+                dst, bias = y[h][:, lo : lo + n], b_t[:, h, e : e + 1]
+                if (h == 1 and e in HALF_1_ON_VECTOR) or (h, lo) == (0, SLOTS - P):
+                    for_vector.append((dst, view, bias))
+                else:
+                    nc.scalar.activation(dst, view, RELU, bias=bias)
 
-        def empty(src, h, lo, n):
-            e = lo // C
-            dst, bias = y[h][:, lo : lo + n], b_t[:, h, e : e + 1]
-            if (h == 1 and H1_ON_VECTOR <= lo < SLOTS - C) or (h, lo) == (0, SLOTS - P):
-                left_over.append((dst, src, bias))
-            else:
-                nc.scalar.activation(dst, src, RELU, bias=bias)
-
-        def close_group(group):
-            ps, views, parts = group
-            for k in range(len(parts)):
-                second_pass(group, k)
-            for view, part in zip(views, parts):
-                empty(view, *part)
-
-        def expert(e):
+        def open_expert(e):
             return open_group(e, [(h, e * C, C) for h in range(HALVES)])
 
-        words(0, 0, 5 * C)
-        words(0, 5 * C, 6 * C)
-        for c in range(2):
-            quantize(1, 512 * c, 512, pairs[c])
-        words(0, SLOTS - C, C)
-        gather_scales(0, nc.sync)
-        groups = [expert(e) for e in range(4)]
-        gather_scales(1, nc.sync)
-        groups.extend(expert(e) for e in range(4, 8))
-        gates = keep.tile([P, TOP, T], F32, align_bytes=64, name="g_codes0_0")
+        gather_words(0, 0, 5 * C)
+        gather_words(0, 5 * C, 6 * C)
+        for c, run in enumerate(runs):
+            quantise(1, QUANTISE_RUN * c, QUANTISE_RUN, run)
+        gather_words(0, SLOTS - C, C, buffer=f"raw1_{X_LOADS[1][-1][0]}")
+
+        per_run = BYTE_RUN // C
+        gather_scales(0)
+        groups = [open_expert(e) for e in range(per_run)]
+        gather_scales(1)
+        groups.extend(open_expert(e) for e in range(per_run, 2 * per_run))
+        gates = keep.tile([P, TOP, T], F32, align_bytes=64, name="slot_words0_0")
+        alone = min(ALONE_FROM)
         nc.sync.dma_start(out=gates[:, 0, :], in_=gate[0, 0:P, :])
-        nc.sync.dma_start(out=gates[:, 1:, CUT:T], in_=gate[1:, 0:P, CUT:T].rearrange("r p t -> p r t"))
-        words(1, 0, PIECE)
-        for group in groups[:4]:
-            close_group(group)
-        gather_scales(2, nc.sync)
-        groups.extend(expert(e) for e in range(8, E - 1))
-        ends = (SLOTS - C, SLOTS - P)
-        groups.append(open_group(E - 1, [(h, ends[0], P) for h in range(HALVES)]))
-        for e in range(4, E - 1):
+        nc.sync.dma_start(out=gates[:, 1:, alone:T], in_=gate[1:, 0:P, alone:T].rearrange("r p t -> p r t"))
+        gather_words(1, 0, BYTE_RUN)
+        for group in groups[:per_run]:
+            close_group(*group)
+        gather_scales(2)
+        groups.extend(open_expert(e) for e in range(2 * per_run, E - 1))
+
+        last_but_one, last = SLOTS - C, SLOTS - P
+        groups.append(open_group(E - 1, [(h, last_but_one, P) for h in range(HALVES)]))
+        for e in range(per_run, E - 1):
             if e % 2 == 0:
-                words(1, e * C, 2 * C if e < E - 2 else C)
-            close_group(groups[e])
-            if e in (4, 5):
-                groups.append(open_group(E + e - 4, [(e - 4, ends[1], P)]))
-        words(1, ends[0], P)
-        close_group(groups[E - 1])
-        words(1, ends[1], P)
-        close_group(groups[E])
-        close_group(groups[E + 1])
-        for dst, src, bias in left_over:
-            nc.vector.tensor_scalar(dst, src, bias, 0.0, ADD, MAX)
+                gather_words(1, e * C, 2 * C if e < E - 2 else C)
+            close_group(*groups[e])
+            if e - per_run < HALVES:
+                groups.append(open_group(e, [(e - per_run, last, P)]))
+        gather_words(1, last_but_one, P)
+        close_group(*groups[E - 1])
+        gather_words(1, last, P)
+        for group in groups[E:]:
+            close_group(*group)
+        for dst, view, bias in for_vector:
+            nc.vector.tensor_scalar(dst, view, bias, 0.0, ADD, MAX)
 
         def picks(h, r, lo, hi):
             return y[h][:].indirect(pos_t[r][:, lo // 16 : hi // 16])
@@ -230,12 +234,13 @@ def tile_moe_tk_lin_relu_kernel(tc, xT, w_words, w_scales, b, gate, offs, pos1, 
         choice = [[keep.tile([P, T], F32, name=f"choice{h}_{r}") for r in (1, 2)] for h in range(HALVES)]
         first = keep.tile([P, HALVES, T], F32, name="first")
         out_by_half = out.rearrange("(h p) t -> p h t", p=P)
+        turned, back = {}, {}
 
         def product(dst, h, r, lo, hi):
             nc.vector.tensor_tensor(dst, picks(h, r, lo, hi), gates[:, r, lo:hi], MULT)
 
-
-        turned, back = {}, {}
+        def add(dst, one, other):
+            nc.vector.tensor_tensor(dst, one, other, ADD)
 
         def forward(i, r, number):
             halves, lo, hi = TURNED[i]
@@ -249,15 +254,18 @@ def tile_moe_tk_lin_relu_kernel(tc, xT, w_words, w_scales, b, gate, offs, pos1, 
                     nc.tensor.matmul(ps[:, col : col + P], picked[:, at - lo : at - lo + P], ident[:], start=opens, stop=closes, is_transpose=True)
             turned[i, r] = ps
 
-        def weigh_and_return(i, number, choices):
+        def by_token_buffer(i, r, width):
+            return keep.tile([P, width], F32, name=f"by_token{r}_{TURNED[i][1]}")
+
+        def weigh_and_return(i, number):
             halves, lo, hi = TURNED[i]
             n = hi - lo
-            ps = back[i] if i in back else bank(number, halves * n)
-            for r in choices:
-                by_token = keep.tile([P, halves * n], F32, name=f"by_token{r}_{lo}")
+            ps = bank(number, halves * n)
+            for r in (1, 2):
+                by_token = by_token_buffer(i, r, halves * n)
                 for at in range(lo, hi, P):
                     cols = slice(halves * (at - lo), halves * (at - lo + P))
-                    column = (r - 1) * BLOCKS + at // P
+                    column = (r - 1) * TURNED_BLOCKS + at // P
                     nc.scalar.activation(by_token[:, cols], turned[i, r][:, cols], COPY, scale=gate_by_token[:, column : column + 1])
                     for h in range(halves):
                         col, to = halves * (at - lo) + h * P, h * n + at - lo
@@ -268,47 +276,42 @@ def tile_moe_tk_lin_relu_kernel(tc, xT, w_words, w_scales, b, gate, offs, pos1, 
         def finish(i):
             halves, lo, hi = TURNED[i]
             total = keep.tile([P, halves, hi - lo], F32, name=f"total{lo}")
-            nc.vector.tensor_tensor(total[:], back[i][:].rearrange("p (h t) -> p h t", h=halves), first[:, :halves, lo:hi], ADD)
+            add(total[:], back[i][:].rearrange("p (h t) -> p h t", h=halves), first[:, :halves, lo:hi])
             nc.sync.dma_start(out=out_by_half[:, :halves, lo:hi], in_=total[:])
-
-        def add(dst, one, other):
-            nc.vector.tensor_tensor(dst, one, other, ADD)
-
-        def after(i, r, width):
-            return keep.tile([P, width], F32, name=f"by_token{r}_{TURNED[i][1]}")
 
         forward(0, 1, 6)
         forward(0, 2, 7)
         forward(1, 1, 0)
-        weigh_and_return(0, 1, (1, 2))
+        weigh_and_return(0, 1)
         forward(1, 2, 2)
-        weigh_and_return(1, 4, (1, 2))
+        weigh_and_return(1, 4)
         forward(2, 1, 3)
         forward(2, 2, 5)
         forward(3, 1, 6)
         forward(3, 2, 0)
-        weigh_and_return(2, 7, (1, 2))
-        weigh_and_return(3, 2, (1, 2))
+        weigh_and_return(2, 7)
+        weigh_and_return(3, 2)
 
-        rest = TURNED[3][2]
+        upper, lower = ALONE_FROM
         for h in range(HALVES):
             product(first[:, h, :], h, 0, 0, T)
-        second, third = (choice[1][r][:, CUT:T] for r in range(2))
-        product(second, 1, 1, CUT, T)
-        product(third, 1, 2, CUT, T)
-        two = choice[0][0][:, rest:T]
-        product(two, 0, 1, rest, T)
+        lower_1, lower_2 = (choice[1][r][:, lower:T] for r in range(2))
+        product(lower_1, 1, 1, lower, T)
+        product(lower_2, 1, 2, lower, T)
+        upper_1 = choice[0][0][:, upper:T]
+        product(upper_1, 0, 1, upper, T)
         finish(0)
-        lower = after(0, 1, T - CUT)
-        upper = after(0, 2, 2 * (T - rest))
-        add(lower[:], first[:, 1, CUT:T], second)
-        product(upper[:, : T - rest], 0, 2, rest, T)
-        add(lower[:], lower[:], third)
-        nc.sync.dma_start(out=out[P:N, CUT:T], in_=lower[:])
-        add(upper[:, T - rest :], two, first[:, 0, rest:T])
+        lower_sum = by_token_buffer(0, 1, T - lower)
+        upper_parts = by_token_buffer(0, 2, 2 * (T - upper))
+        upper_2, upper_01 = upper_parts[:, : T - upper], upper_parts[:, T - upper :]
+        add(lower_sum[:], first[:, 1, lower:T], lower_1)
+        product(upper_2, 0, 2, upper, T)
+        add(lower_sum[:], lower_sum[:], lower_2)
+        nc.sync.dma_start(out=out[P:N, lower:T], in_=lower_sum[:])
+        add(upper_01, upper_1, first[:, 0, upper:T])
         finish(1)
-        total = after(1, 2, T - rest)
-        add(total[:], upper[:, T - rest :], upper[:, : T - rest])
-        nc.sync.dma_start(out=out[0:P, rest:T], in_=total[:])
+        upper_sum = by_token_buffer(1, 2, T - upper)
+        add(upper_sum[:], upper_01, upper_2)
+        nc.sync.dma_start(out=out[0:P, upper:T], in_=upper_sum[:])
         finish(2)
         finish(3)

@@ -242,26 +242,28 @@ def tile_moe_tk_lin_relu_kernel(tc, xT, w_words, w_scales, b, gate, offs, pos1, 
         def add(dst, one, other):
             nc.vector.tensor_tensor(dst, one, other, ADD)
 
-        def forward(i, r, number):
+        def gather(h, r, lo, hi):
+            nc.scalar.activation(choice[h][r - 1][:, lo:hi], picks(h, r, lo, hi), COPY)
+
+        def turn(i, r, h, number=None):
             halves, lo, hi = TURNED[i]
-            ps = bank(number, halves * (hi - lo))
-            for h in range(halves):
-                picked = choice[h][r - 1][:, lo:hi]
-                nc.scalar.activation(picked, picks(h, r, lo, hi), COPY)
-                for at in range(lo, hi, P):
-                    col = halves * (at - lo) + h * P
-                    opens, closes = (h, at) == (0, lo), (h, at) == (halves - 1, hi - P)
-                    nc.tensor.matmul(ps[:, col : col + P], picked[:, at - lo : at - lo + P], ident[:], start=opens, stop=closes, is_transpose=True)
-            turned[i, r] = ps
+            if h == 0:
+                turned[i, r] = bank(number, halves * (hi - lo))
+            for at in range(lo, hi, P):
+                col = halves * (at - lo) + h * P
+                opens, closes = (h, at) == (0, lo), (h, at) == (halves - 1, hi - P)
+                nc.tensor.matmul(turned[i, r][:, col : col + P], choice[h][r - 1][:, at : at + P], ident[:], start=opens, stop=closes, is_transpose=True)
 
         def by_token_buffer(i, r, width):
             return keep.tile([P, width], F32, name=f"by_token{r}_{TURNED[i][1]}")
 
-        def weigh_and_return(i, number):
+        def weigh_and_return(i, choices, number=None):
             halves, lo, hi = TURNED[i]
             n = hi - lo
-            ps = bank(number, halves * n)
-            for r in (1, 2):
+            if number is not None:
+                back[i] = bank(number, halves * n)
+            ps = back[i]
+            for r in choices:
                 by_token = by_token_buffer(i, r, halves * n)
                 for at in range(lo, hi, P):
                     cols = slice(halves * (at - lo), halves * (at - lo + P))
@@ -271,7 +273,6 @@ def tile_moe_tk_lin_relu_kernel(tc, xT, w_words, w_scales, b, gate, offs, pos1, 
                         col, to = halves * (at - lo) + h * P, h * n + at - lo
                         opens, closes = (r, at, h) == (1, lo, 0), (r, at, h) == (2, hi - P, halves - 1)
                         nc.tensor.matmul(ps[:, to : to + P], by_token[:, col : col + P], ident[:], start=opens, stop=closes, is_transpose=True)
-            back[i] = ps
 
         def finish(i):
             halves, lo, hi = TURNED[i]
@@ -279,18 +280,35 @@ def tile_moe_tk_lin_relu_kernel(tc, xT, w_words, w_scales, b, gate, offs, pos1, 
             add(total[:], back[i][:].rearrange("p (h t) -> p h t", h=halves), first[:, :halves, lo:hi])
             nc.sync.dma_start(out=out_by_half[:, :halves, lo:hi], in_=total[:])
 
-        forward(0, 1, 6)
-        forward(0, 2, 7)
-        forward(1, 1, 0)
-        weigh_and_return(0, 1)
-        forward(1, 2, 2)
-        weigh_and_return(1, 4)
-        forward(2, 1, 3)
-        forward(2, 2, 5)
-        forward(3, 1, 6)
-        forward(3, 2, 0)
-        weigh_and_return(2, 7)
-        weigh_and_return(3, 2)
+        gather(0, 1, 0, 512)
+        turn(0, 1, 0, 6)
+        turn(1, 1, 0, 0)
+        gather(1, 1, 0, 512)
+        turn(0, 1, 1)
+        turn(1, 1, 1)
+        gather(0, 2, 0, 512)
+        turn(0, 2, 0, 7)
+        turn(1, 2, 0, 2)
+        gather(1, 2, 0, 256)
+        turn(0, 2, 1)
+        weigh_and_return(0, (1,), 1)
+        gather(1, 2, 256, 512)
+        turn(1, 2, 1)
+        weigh_and_return(0, (2,))
+        weigh_and_return(1, (1, 2), 4)
+        gather(0, 1, 512, 768)
+        turn(2, 1, 0, 3)
+        turn(3, 1, 0, 6)
+        gather(1, 1, 512, 640)
+        turn(2, 1, 1)
+        gather(0, 2, 512, 640)
+        turn(2, 2, 0, 5)
+        gather(1, 2, 512, 640)
+        turn(2, 2, 1)
+        gather(0, 2, 640, 768)
+        turn(3, 2, 0, 0)
+        weigh_and_return(2, (1, 2), 7)
+        weigh_and_return(3, (1, 2), 2)
 
         upper, lower = ALONE_FROM
         for h in range(HALVES):

@@ -33,8 +33,10 @@ QUANTISE_RUN = 512
 BYTE_RUN = 1024
 SPARE_WORDS = 1024
 SPARE_BYTES = 384
-HALF_1_ON_VECTOR = (9, 10)
-TURNED = ((2, 0, 256), (2, 256, 512), (2, 512, 640), (1, 640, 768))
+HALF_1_ON_VECTOR = (8, 9, 10)
+TURNED = (((0, 1), 0, 256), ((0, 1), 256, 512), ((0, 1), 512, 640), ((0,), 640, 768))
+TURN_BANK = ((6, 7), (0, 2), (3, 5), (6, 0))
+BACK_BANK = (1, 4, 7, 2)
 ALONE_FROM = (768, 640)
 TURNED_BLOCKS = ALONE_FROM[0] // P
 
@@ -183,7 +185,7 @@ def tile_moe_tk_lin_relu_kernel(tc, xT, w_words, w_scales, b, gate, offs, pos1, 
             for view, (h, lo, n) in zip(views, parts):
                 e = lo // C
                 dst, bias = y[h][:, lo : lo + n], b_t[:, h, e : e + 1]
-                if (h == 1 and e in HALF_1_ON_VECTOR) or (h, lo) == (0, SLOTS - P):
+                if h == 1 and e in HALF_1_ON_VECTOR:
                     for_vector.append((dst, view, bias))
                 else:
                     nc.scalar.activation(dst, view, RELU, bias=bias)
@@ -242,73 +244,62 @@ def tile_moe_tk_lin_relu_kernel(tc, xT, w_words, w_scales, b, gate, offs, pos1, 
         def add(dst, one, other):
             nc.vector.tensor_tensor(dst, one, other, ADD)
 
-        def gather(h, r, lo, hi):
-            nc.scalar.activation(choice[h][r - 1][:, lo:hi], picks(h, r, lo, hi), COPY)
-
-        def turn(i, r, h, number=None):
-            halves, lo, hi = TURNED[i]
-            if h == 0:
-                turned[i, r] = bank(number, halves * (hi - lo))
-            for at in range(lo, hi, P):
-                col = halves * (at - lo) + h * P
-                opens, closes = (h, at) == (0, lo), (h, at) == (halves - 1, hi - P)
-                nc.tensor.matmul(turned[i, r][:, col : col + P], choice[h][r - 1][:, at : at + P], ident[:], start=opens, stop=closes, is_transpose=True)
+        def forward(h, r, *pieces):
+            start, end = TURNED[pieces[0]][1], TURNED[pieces[-1]][2]
+            nc.scalar.activation(choice[h][r - 1][:, start:end], picks(h, r, start, end), COPY)
+            for i in pieces:
+                halves, lo, hi = TURNED[i]
+                if (i, r) not in turned:
+                    turned[i, r] = bank(TURN_BANK[i][r - 1], len(halves) * (hi - lo))
+                opened = done.setdefault((i, r), [])
+                for at in range(lo, hi, P):
+                    col = len(halves) * (at - lo) + halves.index(h) * P
+                    opens, closes = not opened and at == lo, len(opened) == len(halves) - 1 and at == hi - P
+                    nc.tensor.matmul(turned[i, r][:, col : col + P], choice[h][r - 1][:, at : at + P], ident[:], start=opens, stop=closes, is_transpose=True)
+                opened.append(h)
 
         def by_token_buffer(i, r, width):
-            return keep.tile([P, width], F32, name=f"by_token{r}_{TURNED[i][1]}")
+            return keep.tile([P, width], F32, name=f"by_token{r}_{i}")
 
-        def weigh_and_return(i, choices, number=None):
+        def weigh_and_return(i, r):
             halves, lo, hi = TURNED[i]
-            n = hi - lo
-            if number is not None:
-                back[i] = bank(number, halves * n)
-            ps = back[i]
-            for r in choices:
-                by_token = by_token_buffer(i, r, halves * n)
-                for at in range(lo, hi, P):
-                    cols = slice(halves * (at - lo), halves * (at - lo + P))
-                    column = (r - 1) * TURNED_BLOCKS + at // P
-                    nc.scalar.activation(by_token[:, cols], turned[i, r][:, cols], COPY, scale=gate_by_token[:, column : column + 1])
-                    for h in range(halves):
-                        col, to = halves * (at - lo) + h * P, h * n + at - lo
-                        opens, closes = (r, at, h) == (1, lo, 0), (r, at, h) == (2, hi - P, halves - 1)
-                        nc.tensor.matmul(ps[:, to : to + P], by_token[:, col : col + P], ident[:], start=opens, stop=closes, is_transpose=True)
+            n, count = hi - lo, len(halves)
+            opening = i not in back
+            if opening:
+                back[i] = bank(BACK_BANK[i], count * n)
+            by_token = by_token_buffer(i, r, count * n)
+            for at in range(lo, hi, P):
+                cols = slice(count * (at - lo), count * (at - lo + P))
+                column = (r - 1) * TURNED_BLOCKS + at // P
+                nc.scalar.activation(by_token[:, cols], turned[i, r][:, cols], COPY, scale=gate_by_token[:, column : column + 1])
+                for k in range(count):
+                    col, to = count * (at - lo) + k * P, k * n + at - lo
+                    opens, closes = opening and (at, k) == (lo, 0), not opening and (at, k) == (hi - P, count - 1)
+                    nc.tensor.matmul(back[i][:, to : to + P], by_token[:, col : col + P], ident[:], start=opens, stop=closes, is_transpose=True)
 
         def finish(i):
             halves, lo, hi = TURNED[i]
-            total = keep.tile([P, halves, hi - lo], F32, name=f"total{lo}")
-            add(total[:], back[i][:].rearrange("p (h t) -> p h t", h=halves), first[:, :halves, lo:hi])
-            nc.sync.dma_start(out=out_by_half[:, :halves, lo:hi], in_=total[:])
+            rows = slice(halves[0], halves[-1] + 1)
+            total = keep.tile([P, len(halves), hi - lo], F32, name=f"total{i}")
+            add(total[:], back[i][:].rearrange("p (h t) -> p h t", h=len(halves)), first[:, rows, lo:hi])
+            nc.sync.dma_start(out=out_by_half[:, rows, lo:hi], in_=total[:])
 
-        gather(0, 1, 0, 512)
-        turn(0, 1, 0, 6)
-        turn(1, 1, 0, 0)
-        gather(1, 1, 0, 512)
-        turn(0, 1, 1)
-        turn(1, 1, 1)
-        gather(0, 2, 0, 512)
-        turn(0, 2, 0, 7)
-        turn(1, 2, 0, 2)
-        gather(1, 2, 0, 256)
-        turn(0, 2, 1)
-        weigh_and_return(0, (1,), 1)
-        gather(1, 2, 256, 512)
-        turn(1, 2, 1)
-        weigh_and_return(0, (2,))
-        weigh_and_return(1, (1, 2), 4)
-        gather(0, 1, 512, 768)
-        turn(2, 1, 0, 3)
-        turn(3, 1, 0, 6)
-        gather(1, 1, 512, 640)
-        turn(2, 1, 1)
-        gather(0, 2, 512, 640)
-        turn(2, 2, 0, 5)
-        gather(1, 2, 512, 640)
-        turn(2, 2, 1)
-        gather(0, 2, 640, 768)
-        turn(3, 2, 0, 0)
-        weigh_and_return(2, (1, 2), 7)
-        weigh_and_return(3, (1, 2), 2)
+        done = {}
+        forward(0, 1, 0, 1)
+        forward(1, 1, 0, 1)
+        forward(0, 2, 0, 1)
+        forward(1, 2, 0)
+        weigh_and_return(0, 1)
+        forward(1, 2, 1, 2)
+        weigh_and_return(0, 2)
+        weigh_and_return(1, 1)
+        forward(0, 2, 2, 3)
+        forward(0, 1, 2, 3)
+        forward(1, 1, 2)
+        weigh_and_return(1, 2)
+        for r in (2, 1):
+            weigh_and_return(2, r)
+            weigh_and_return(3, r)
 
         upper, lower = ALONE_FROM
         for h in range(HALVES):

@@ -293,13 +293,12 @@ def tile_moe_tk_lin_relu_kernel(tc, xT, w_words, w_scales, b, gate, offs, pos1, 
         forward(1, 2, 1, 2)
         weigh_and_return(0, 2)
         weigh_and_return(1, 1)
+        weigh_and_return(1, 2)
         forward(0, 2, 2, 3)
         forward(0, 1, 2, 3)
         forward(1, 1, 2)
-        weigh_and_return(1, 2)
-        for r in (2, 1):
-            weigh_and_return(2, r)
-            weigh_and_return(3, r)
+        for i, r in ((2, 2), (3, 2), (3, 1), (2, 1)):
+            weigh_and_return(i, r)
 
         upper, lower = ALONE_FROM
         for h in range(HALVES):
@@ -307,20 +306,19 @@ def tile_moe_tk_lin_relu_kernel(tc, xT, w_words, w_scales, b, gate, offs, pos1, 
         lower_1, lower_2 = (choice[1][r][:, lower:T] for r in range(2))
         product(lower_1, 1, 1, lower, T)
         product(lower_2, 1, 2, lower, T)
+        add(lower_1, first[:, 1, lower:T], lower_1)
         upper_1 = choice[0][0][:, upper:T]
         product(upper_1, 0, 1, upper, T)
+        add(lower_1, lower_1, lower_2)
+        nc.sync.dma_start(out=out[P:N, lower:T], in_=lower_1)
         finish(0)
-        lower_sum = by_token_buffer(0, 1, T - lower)
-        upper_parts = by_token_buffer(0, 2, 2 * (T - upper))
-        upper_2, upper_01 = upper_parts[:, : T - upper], upper_parts[:, T - upper :]
-        add(lower_sum[:], first[:, 1, lower:T], lower_1)
-        product(upper_2, 0, 2, upper, T)
-        add(lower_sum[:], lower_sum[:], lower_2)
-        nc.sync.dma_start(out=out[P:N, lower:T], in_=lower_sum[:])
-        add(upper_01, upper_1, first[:, 0, upper:T])
         finish(1)
-        upper_sum = by_token_buffer(1, 2, T - upper)
+        upper_parts = by_token_buffer(1, 2, 2 * (T - upper))
+        upper_2, upper_01 = upper_parts[:, : T - upper], upper_parts[:, T - upper :]
+        product(upper_2, 0, 2, upper, T)
+        add(upper_01, upper_1, first[:, 0, upper:T])
+        finish(3)
+        upper_sum = by_token_buffer(3, 1, T - upper)
         add(upper_sum[:], upper_01, upper_2)
         nc.sync.dma_start(out=out[0:P, upper:T], in_=upper_sum[:])
         finish(2)
-        finish(3)

@@ -261,21 +261,25 @@ def tile_moe_tk_lin_relu_kernel(tc, xT, w_words, w_scales, b, gate, offs, pos1, 
         def by_token_buffer(i, r, width):
             return keep.tile([P, width], F32, name=f"by_token{r}_{i}")
 
-        def weigh_and_return(i, r):
+        def weigh_and_return(i, r, blocks=None):
             halves, lo, hi = TURNED[i]
             n, count = hi - lo, len(halves)
-            opening = i not in back
-            if opening:
+            if i not in back:
                 back[i] = bank(BACK_BANK[i], count * n)
-            by_token = by_token_buffer(i, r, count * n)
-            for at in range(lo, hi, P):
+            if (i, r) not in weighed:
+                weighed[i, r] = by_token_buffer(i, r, count * n)
+            for at in blocks or range(lo, hi, P):
                 cols = slice(count * (at - lo), count * (at - lo + P))
                 column = (r - 1) * TURNED_BLOCKS + at // P
-                nc.scalar.activation(by_token[:, cols], turned[i, r][:, cols], COPY, scale=gate_by_token[:, column : column + 1])
+                nc.scalar.activation(weighed[i, r][:, cols], turned[i, r][:, cols], COPY, scale=gate_by_token[:, column : column + 1])
                 for k in range(count):
                     col, to = count * (at - lo) + k * P, k * n + at - lo
-                    opens, closes = opening and (at, k) == (lo, 0), not opening and (at, k) == (hi - P, count - 1)
-                    nc.tensor.matmul(back[i][:, to : to + P], by_token[:, col : col + P], ident[:], start=opens, stop=closes, is_transpose=True)
+                    returned = passes.setdefault(i, [])
+                    returned.append(to)
+                    nc.tensor.matmul(
+                        back[i][:, to : to + P], weighed[i, r][:, col : col + P], ident[:],
+                        start=len(returned) == 1, stop=len(returned) == 2 * count * n // P, is_transpose=True,
+                    )
 
         def finish(i):
             halves, lo, hi = TURNED[i]
@@ -284,7 +288,7 @@ def tile_moe_tk_lin_relu_kernel(tc, xT, w_words, w_scales, b, gate, offs, pos1, 
             add(total[:], back[i][:].rearrange("p (h t) -> p h t", h=len(halves)), first[:, rows, lo:hi])
             nc.sync.dma_start(out=out_by_half[:, rows, lo:hi], in_=total[:])
 
-        done = {}
+        done, weighed, passes = {}, {}, {}
         forward(0, 1, 0, 1)
         forward(1, 1, 0, 1)
         forward(0, 2, 0, 1)
@@ -293,10 +297,11 @@ def tile_moe_tk_lin_relu_kernel(tc, xT, w_words, w_scales, b, gate, offs, pos1, 
         forward(1, 2, 1, 2)
         weigh_and_return(0, 2)
         weigh_and_return(1, 1)
-        weigh_and_return(1, 2)
+        weigh_and_return(1, 2, (256,))
         forward(0, 2, 2, 3)
         forward(0, 1, 2, 3)
         forward(1, 1, 2)
+        weigh_and_return(1, 2, (384,))
         for i, r in ((2, 2), (3, 2), (3, 1), (2, 1)):
             weigh_and_return(i, r)
 
@@ -307,18 +312,17 @@ def tile_moe_tk_lin_relu_kernel(tc, xT, w_words, w_scales, b, gate, offs, pos1, 
         product(lower_1, 1, 1, lower, T)
         product(lower_2, 1, 2, lower, T)
         add(lower_1, first[:, 1, lower:T], lower_1)
-        upper_1 = choice[0][0][:, upper:T]
-        product(upper_1, 0, 1, upper, T)
+        upper_1, upper_2 = (choice[0][r][:, upper:T] for r in range(2))
+        product(upper_2, 0, 2, upper, T)
         add(lower_1, lower_1, lower_2)
         nc.sync.dma_start(out=out[P:N, lower:T], in_=lower_1)
+        product(upper_1, 0, 1, upper, T)
+        upper_01 = keep.tile([P, T - upper], F32, name="upper_01")
+        nc.gpsimd.tensor_tensor(upper_01[:], upper_1, first[:, 0, upper:T], ADD)
         finish(0)
         finish(1)
-        upper_parts = by_token_buffer(1, 2, 2 * (T - upper))
-        upper_2, upper_01 = upper_parts[:, : T - upper], upper_parts[:, T - upper :]
-        product(upper_2, 0, 2, upper, T)
-        add(upper_01, upper_1, first[:, 0, upper:T])
         finish(3)
         upper_sum = by_token_buffer(3, 1, T - upper)
-        add(upper_sum[:], upper_01, upper_2)
+        add(upper_sum[:], upper_01[:], upper_2)
         nc.sync.dma_start(out=out[0:P, upper:T], in_=upper_sum[:])
         finish(2)

@@ -34,9 +34,13 @@ BYTE_RUN = 1024
 SPARE_WORDS = 1024
 SPARE_BYTES = 384
 HALF_1_ON_VECTOR = (8, 9, 10)
-TURNED = (((0, 1), 0, 256), ((0, 1), 256, 512), ((0, 1), 512, 640), ((0,), 640, 768))
-TURN_BANK = ((6, 7), (0, 2), (3, 5), (6, 0))
+TURNED = (((0, 1), 0, 256), ((0, 1), 256, 512), ((0,), 512, 768), ((1,), 512, 640))
 BACK_BANK = (1, 4, 7, 2)
+PAIRS = tuple(tuple((h, at) for at in (lo, lo + P) for h in range(HALVES)) for lo in (0, 256))
+TURN_GROUPS = (
+    ((6, PAIRS[0]), (0, PAIRS[1]), (6, ((0, 512), (0, 640))), (3, ((1, 512),))),
+    ((7, PAIRS[0]), (2, PAIRS[1]), (5, ((0, 512), (1, 512))), (0, ((0, 640),))),
+)
 ALONE_FROM = (768, 640)
 TURNED_BLOCKS = ALONE_FROM[0] // P
 
@@ -236,7 +240,7 @@ def tile_moe_tk_lin_relu_kernel(tc, xT, w_words, w_scales, b, gate, offs, pos1, 
         choice = [[keep.tile([P, T], F32, name=f"choice{h}_{r}") for r in (1, 2)] for h in range(HALVES)]
         first = keep.tile([P, HALVES, T], F32, name="first")
         out_by_half = out.rearrange("(h p) t -> p h t", p=P)
-        turned, back = {}, {}
+        turned, back, written, returned = {}, {}, {}, {}
 
         def product(dst, h, r, lo, hi):
             nc.vector.tensor_tensor(dst, picks(h, r, lo, hi), gates[:, r, lo:hi], MULT)
@@ -244,42 +248,44 @@ def tile_moe_tk_lin_relu_kernel(tc, xT, w_words, w_scales, b, gate, offs, pos1, 
         def add(dst, one, other):
             nc.vector.tensor_tensor(dst, one, other, ADD)
 
-        def forward(h, r, *pieces):
-            start, end = TURNED[pieces[0]][1], TURNED[pieces[-1]][2]
-            nc.scalar.activation(choice[h][r - 1][:, start:end], picks(h, r, start, end), COPY)
-            for i in pieces:
-                halves, lo, hi = TURNED[i]
-                if (i, r) not in turned:
-                    turned[i, r] = bank(TURN_BANK[i][r - 1], len(halves) * (hi - lo))
-                opened = done.setdefault((i, r), [])
-                for at in range(lo, hi, P):
-                    col = len(halves) * (at - lo) + halves.index(h) * P
-                    opens, closes = not opened and at == lo, len(opened) == len(halves) - 1 and at == hi - P
-                    nc.tensor.matmul(turned[i, r][:, col : col + P], choice[h][r - 1][:, at : at + P], ident[:], start=opens, stop=closes, is_transpose=True)
-                opened.append(h)
+        def forward(h, r, start, end, into=None):
+            if into is None:
+                into = choice[h][r - 1][:, start:end]
+            nc.scalar.activation(into, picks(h, r, start, end), COPY)
+            for at in range(start, end, P):
+                group = [g for g in TURN_GROUPS[r - 1] if (h, at) in g[1]][0]
+                number, cells = group
+                if (r, cells) not in turned:
+                    turned[r, cells] = bank(number, len(cells) * P)
+                count = written.setdefault((r, cells), [])
+                count.append(at)
+                col = cells.index((h, at)) * P
+                nc.tensor.matmul(
+                    turned[r, cells][:, col : col + P], into[:, at - start : at - start + P], ident[:],
+                    start=len(count) == 1, stop=len(count) == len(cells), is_transpose=True,
+                )
 
-        def by_token_buffer(i, r, width):
-            return keep.tile([P, width], F32, name=f"by_token{r}_{i}")
+        def by_token_buffer(r, h, at, width):
+            return keep.tile([P, width], F32, name=f"by_token{r}_{h}_{at}")
 
-        def weigh_and_return(i, r, blocks=None):
-            halves, lo, hi = TURNED[i]
-            n, count = hi - lo, len(halves)
-            if i not in back:
-                back[i] = bank(BACK_BANK[i], count * n)
-            if (i, r) not in weighed:
-                weighed[i, r] = by_token_buffer(i, r, count * n)
-            for at in blocks or range(lo, hi, P):
-                cols = slice(count * (at - lo), count * (at - lo + P))
-                column = (r - 1) * TURNED_BLOCKS + at // P
-                nc.scalar.activation(weighed[i, r][:, cols], turned[i, r][:, cols], COPY, scale=gate_by_token[:, column : column + 1])
-                for k in range(count):
-                    col, to = count * (at - lo) + k * P, k * n + at - lo
-                    returned = passes.setdefault(i, [])
-                    returned.append(to)
-                    nc.tensor.matmul(
-                        back[i][:, to : to + P], weighed[i, r][:, col : col + P], ident[:],
-                        start=len(returned) == 1, stop=len(returned) == 2 * count * n // P, is_transpose=True,
-                    )
+        def weigh_and_return(r, at, halves):
+            cells = [g[1] for g in TURN_GROUPS[r - 1] if (halves[0], at) in g[1]][0]
+            col = cells.index((halves[0], at)) * P
+            weighed = by_token_buffer(r, halves[0], at, len(halves) * P)
+            column = (r - 1) * TURNED_BLOCKS + at // P
+            nc.scalar.activation(weighed[:], turned[r, cells][:, col : col + len(halves) * P], COPY, scale=gate_by_token[:, column : column + 1])
+            for k, h in enumerate(halves):
+                i = [n for n, (rows, lo, hi) in enumerate(TURNED) if h in rows and lo <= at < hi][0]
+                rows, lo, hi = TURNED[i]
+                if i not in back:
+                    back[i] = bank(BACK_BANK[i], len(rows) * (hi - lo))
+                count = returned.setdefault(i, [])
+                count.append(at)
+                to = rows.index(h) * (hi - lo) + at - lo
+                nc.tensor.matmul(
+                    back[i][:, to : to + P], weighed[:, k * P : (k + 1) * P], ident[:],
+                    start=len(count) == 1, stop=len(count) == 2 * len(rows) * (hi - lo) // P, is_transpose=True,
+                )
 
         def finish(i):
             halves, lo, hi = TURNED[i]
@@ -288,22 +294,28 @@ def tile_moe_tk_lin_relu_kernel(tc, xT, w_words, w_scales, b, gate, offs, pos1, 
             add(total[:], back[i][:].rearrange("p (h t) -> p h t", h=len(halves)), first[:, rows, lo:hi])
             nc.sync.dma_start(out=out_by_half[:, rows, lo:hi], in_=total[:])
 
-        done, weighed, passes = {}, {}, {}
-        forward(0, 1, 0, 1)
-        forward(1, 1, 0, 1)
-        forward(0, 2, 0, 1)
-        forward(1, 2, 0)
-        weigh_and_return(0, 1)
-        forward(1, 2, 1, 2)
-        weigh_and_return(0, 2)
-        weigh_and_return(1, 1)
-        weigh_and_return(1, 2, (256,))
-        forward(0, 2, 2, 3)
-        forward(0, 1, 2, 3)
-        forward(1, 1, 2)
-        weigh_and_return(1, 2, (384,))
-        for i, r in ((2, 2), (3, 2), (3, 1), (2, 1)):
-            weigh_and_return(i, r)
+        both = (0, 1)
+        forward(0, 1, 0, 512)
+        forward(1, 1, 0, 512)
+        forward(0, 2, 0, 512)
+        weigh_and_return(1, 0, both)
+        weigh_and_return(1, 128, both)
+        forward(1, 2, 0, 256, into=choice[1][0][:, 0:256])
+        weigh_and_return(1, 256, both)
+        weigh_and_return(1, 384, both)
+        forward(1, 2, 256, 640, into=choice[1][0][:, 256:640])
+        weigh_and_return(2, 0, both)
+        weigh_and_return(2, 128, both)
+        forward(0, 2, 512, 768, into=choice[0][1][:, 0:256])
+        weigh_and_return(2, 256, both)
+        forward(0, 1, 512, 768, into=choice[0][1][:, 256:512])
+        weigh_and_return(2, 384, both)
+        forward(1, 1, 512, 640)
+        weigh_and_return(2, 512, both)
+        weigh_and_return(2, 640, (0,))
+        weigh_and_return(1, 640, (0,))
+        weigh_and_return(1, 512, (0,))
+        weigh_and_return(1, 512, (1,))
 
         upper, lower = ALONE_FROM
         for h in range(HALVES):
@@ -321,8 +333,8 @@ def tile_moe_tk_lin_relu_kernel(tc, xT, w_words, w_scales, b, gate, offs, pos1, 
         nc.gpsimd.tensor_tensor(upper_01[:], upper_1, first[:, 0, upper:T], ADD)
         finish(0)
         finish(1)
-        finish(3)
-        upper_sum = by_token_buffer(3, 1, T - upper)
+        upper_sum = by_token_buffer(2, 0, 384, T - upper)
         add(upper_sum[:], upper_01[:], upper_2)
         nc.sync.dma_start(out=out[0:P, upper:T], in_=upper_sum[:])
         finish(2)
+        finish(3)

@@ -42,6 +42,7 @@ TURN_GROUPS = (
     ((7, PAIRS[0]), (2, PAIRS[1]), (5, ((0, 512), (1, 512))), (0, ((0, 640),))),
 )
 ALONE_FROM = (768, 640)
+ON_GPSIMD = 160
 TURNED_BLOCKS = ALONE_FROM[0] // P
 
 
@@ -311,10 +312,11 @@ def tile_moe_tk_lin_relu_kernel(tc, xT, w_words, w_scales, b, gate, offs, pos1, 
         forward(0, 1, 512, 768, into=choice[0][1][:, 256:512])
         weigh_and_return(2, 384, both)
         forward(1, 1, 512, 640)
-        weigh_and_return(2, 512, both)
+        weigh_and_return(2, 512, (0,))
         weigh_and_return(2, 640, (0,))
         weigh_and_return(1, 640, (0,))
         weigh_and_return(1, 512, (0,))
+        weigh_and_return(2, 512, (1,))
         weigh_and_return(1, 512, (1,))
 
         upper, lower = ALONE_FROM
@@ -325,16 +327,17 @@ def tile_moe_tk_lin_relu_kernel(tc, xT, w_words, w_scales, b, gate, offs, pos1, 
         product(lower_2, 1, 2, lower, T)
         add(lower_1, first[:, 1, lower:T], lower_1)
         upper_1, upper_2 = (choice[0][r][:, upper:T] for r in range(2))
-        product(upper_2, 0, 2, upper, T)
+        product(upper_1, 0, 1, upper, T)
         add(lower_1, lower_1, lower_2)
         nc.sync.dma_start(out=out[P:N, lower:T], in_=lower_1)
-        product(upper_1, 0, 1, upper, T)
-        upper_01 = keep.tile([P, T - upper], F32, name="upper_01")
-        nc.gpsimd.tensor_tensor(upper_01[:], upper_1, first[:, 0, upper:T], ADD)
+        split = upper + ON_GPSIMD
+        add(upper_1[:, ON_GPSIMD:], first[:, 0, split:T], upper_1[:, ON_GPSIMD:])
+        product(upper_2, 0, 2, upper, T)
+        nc.gpsimd.tensor_tensor(upper_2[:, :ON_GPSIMD], upper_2[:, :ON_GPSIMD], first[:, 0, upper:split], ADD)
         finish(0)
         finish(1)
         upper_sum = by_token_buffer(2, 0, 384, T - upper)
-        add(upper_sum[:], upper_01[:], upper_2)
+        add(upper_sum[:], upper_1, upper_2)
         nc.sync.dma_start(out=out[0:P, upper:T], in_=upper_sum[:])
         finish(2)
         finish(3)

@@ -35,14 +35,13 @@ SPARE_WORDS = 1024
 SPARE_BYTES = 384
 HALF_1_ON_VECTOR = (8, 9, 10)
 TURNED = (((0, 1), 0, 256), ((0, 1), 256, 512), ((0,), 512, 768), ((1,), 512, 640))
-BACK_BANK = (1, 4, 7, 2)
+BACK_BANK = (1, 4, 7, 1)
 PAIRS = tuple(tuple((h, at) for at in (lo, lo + P) for h in range(HALVES)) for lo in (0, 256))
 TURN_GROUPS = (
-    ((6, PAIRS[0]), (0, PAIRS[1]), (6, ((0, 512), (0, 640))), (3, ((1, 512),))),
+    ((6, PAIRS[0]), (0, PAIRS[1]), (6, ((0, 512),)), (2, ((0, 640),)), (3, ((1, 512),))),
     ((7, PAIRS[0]), (2, PAIRS[1]), (5, ((0, 512), (1, 512))), (0, ((0, 640),))),
 )
 ALONE_FROM = (768, 640)
-ON_GPSIMD = 160
 TURNED_BLOCKS = ALONE_FROM[0] // P
 
 
@@ -309,14 +308,13 @@ def tile_moe_tk_lin_relu_kernel(tc, xT, w_words, w_scales, b, gate, offs, pos1, 
         weigh_and_return(2, 128, both)
         forward(0, 2, 512, 768, into=choice[0][1][:, 0:256])
         weigh_and_return(2, 256, both)
-        forward(0, 1, 512, 768, into=choice[0][1][:, 256:512])
         weigh_and_return(2, 384, both)
+        forward(0, 1, 512, 768, into=choice[1][0][:, 256:512])
         forward(1, 1, 512, 640)
-        weigh_and_return(2, 512, (0,))
+        weigh_and_return(2, 512, both)
         weigh_and_return(2, 640, (0,))
-        weigh_and_return(1, 640, (0,))
         weigh_and_return(1, 512, (0,))
-        weigh_and_return(2, 512, (1,))
+        weigh_and_return(1, 640, (0,))
         weigh_and_return(1, 512, (1,))
 
         upper, lower = ALONE_FROM
@@ -328,16 +326,15 @@ def tile_moe_tk_lin_relu_kernel(tc, xT, w_words, w_scales, b, gate, offs, pos1, 
         add(lower_1, first[:, 1, lower:T], lower_1)
         upper_1, upper_2 = (choice[0][r][:, upper:T] for r in range(2))
         product(upper_1, 0, 1, upper, T)
-        add(lower_1, lower_1, lower_2)
-        nc.sync.dma_start(out=out[P:N, lower:T], in_=lower_1)
-        split = upper + ON_GPSIMD
-        add(upper_1[:, ON_GPSIMD:], first[:, 0, split:T], upper_1[:, ON_GPSIMD:])
         product(upper_2, 0, 2, upper, T)
-        nc.gpsimd.tensor_tensor(upper_2[:, :ON_GPSIMD], upper_2[:, :ON_GPSIMD], first[:, 0, upper:split], ADD)
+        nc.gpsimd.tensor_tensor(upper_2, upper_2, first[:, 0, upper:T], ADD)
         finish(0)
         finish(1)
-        upper_sum = by_token_buffer(2, 0, 384, T - upper)
-        add(upper_sum[:], upper_1, upper_2)
-        nc.sync.dma_start(out=out[0:P, upper:T], in_=upper_sum[:])
+        sums = by_token_buffer(2, 0, 384, 2 * T - lower - upper)
+        lower_sum, upper_sum = sums[:, : T - lower], sums[:, T - lower :]
+        add(lower_sum, lower_1, lower_2)
+        nc.sync.dma_start(out=out[P:N, lower:T], in_=lower_sum)
+        add(upper_sum, upper_1, upper_2)
+        nc.sync.dma_start(out=out[0:P, upper:T], in_=upper_sum)
         finish(2)
         finish(3)

@@ -300,13 +300,12 @@ def tile_moe_tk_lin_relu_kernel(tc, xT, w_words, w_scales, b, gate, offs, pos1, 
         forward(0, 2, 0, 512)
         weigh_and_return(1, 0, both)
         weigh_and_return(1, 128, both)
-        forward(1, 2, 0, 256, into=choice[1][0][:, 0:256])
+        forward(1, 2, 0, 640, into=choice[1][0][:, 0:640])
         weigh_and_return(1, 256, both)
         weigh_and_return(1, 384, both)
-        forward(1, 2, 256, 640, into=choice[1][0][:, 256:640])
+        forward(0, 2, 512, 768, into=choice[0][1][:, 0:256])
         weigh_and_return(2, 0, both)
         weigh_and_return(2, 128, both)
-        forward(0, 2, 512, 768, into=choice[0][1][:, 0:256])
         weigh_and_return(2, 256, both)
         weigh_and_return(2, 384, both)
         forward(0, 1, 512, 768, into=choice[1][0][:, 256:512])

from contextlib import ExitStack

import concourse.mybir as mybir
from concourse.masks import make_identity

K, T, E, C, N = 1024, 1024, 12, 256, 256
TOP = 3
FLOPS = 2 * K * N * E * C

F32 = mybir.dt.float32
BF16 = mybir.dt.bfloat16
I32 = mybir.dt.int32
U32 = mybir.dt.uint32
U16 = mybir.dt.uint16
U8 = mybir.dt.uint8
FP8X4 = mybir.dt.float8_e4m3fn_x4
FP4X4 = mybir.dt.float4_e2m1fn_x4
MULT, ADD, MAX = mybir.AluOpType.mult, mybir.AluOpType.add, mybir.AluOpType.max
COPY = mybir.ActivationFunctionType.Copy
RELU = mybir.ActivationFunctionType.Relu

P = 128
PASSES = K // 512
SLOTS = E * C
HALVES = N // P
BANKS = 8
QUADRANT = 32
PACK = 4

X_LOADS = (((0, 256), (256, 256), (512, 256), (768, 128), (896, 128)), ((0, 256), (256, 256), (512, 256), (768, 256)))
CAST_ON_SCALAR = ((96, 96, 112, 64, 48), (256, 256, 256, 256))
QUANTISE_RUN = 512
BYTE_RUN = 1024
SPARE_WORDS = 1024
SPARE_BYTES = 384
HALF_1_ON_VECTOR = (8, 9, 10)
TURNED = (((0, 1), 0, 256), ((0, 1), 256, 512), ((0,), 512, 768), ((1,), 512, 640))
BACK_BANK = (1, 4, 7, 1)
PAIRS = tuple(tuple((h, at) for at in (lo, lo + P) for h in range(HALVES)) for lo in (0, 256))
TURN_GROUPS = (
    ((6, PAIRS[0]), (0, PAIRS[1]), (6, ((0, 512),)), (2, ((0, 640),)), (3, ((1, 512),))),
    ((7, PAIRS[0]), (2, PAIRS[1]), (5, ((0, 512), (1, 512))), (0, ((0, 640),))),
)
ALONE_FROM = (768, 640)
TURNED_BLOCKS = ALONE_FROM[0] // P


def tile_moe_tk_lin_relu_kernel(tc, xT, w_words, w_scales, b, gate, offs, pos1, pos2, pos3, out):
    nc = tc.nc
    with ExitStack() as ctx:
        lists = ctx.enter_context(tc.tile_pool(name="lists", bufs=1))
        keep = ctx.enter_context(tc.tile_pool(name="keep", bufs=1))
        psum = ctx.enter_context(tc.psum_pool(name="psum", bufs=1))

        def bank(number, width):
            return psum.tile([P, width], F32, name=f"bank{number % BANKS}")

        offs_t = lists.tile([P, SLOTS // 16], U16, name="offs_t")
        pos_t = [lists.tile([P, T // 16], U16, name=f"pos{r}_t") for r in range(TOP)]

        raw = [[keep.tile([P, PACK, n], F32, align_bytes=64, name=f"raw{a}_{lo}") for lo, n in X_LOADS[a]] for a in range(PASSES)]
        grouped = [
            [keep.tile([P, n, PACK], BF16, align_bytes=64, name=f"grouped0_{lo}") for lo, n in X_LOADS[0]],
        ]
        runs = [keep.tile([P, QUANTISE_RUN, PACK], BF16, align_bytes=64, name=f"grouped1_{lo}") for lo in range(0, T, QUANTISE_RUN)]
        grouped.append([runs[lo // QUANTISE_RUN][:, lo % QUANTISE_RUN : lo % QUANTISE_RUN + n, :] for lo, n in X_LOADS[1]])
        codes = keep.tile([P, PASSES * T + SPARE_WORDS], U32, align_bytes=64, name="codes")
        first_word = (T, 0)
        scales = keep.tile([P, T + SPARE_BYTES], U8, align_bytes=64, name="scales")
        slot_words = [{}, {}]
        slot_scales = [keep.tile([P, BYTE_RUN], U8, align_bytes=64, name=f"slot_scales_{c}") for c in range(SLOTS // BYTE_RUN)]
        slot_scales1 = [keep.tile([P, BYTE_RUN], U8, align_bytes=64, name=f"slot_scales1_{c}") for c in range(SLOTS // BYTE_RUN)]
        w_t = keep.tile([P, E * PASSES, 2 * N], U8, align_bytes=64, name="w_t")
        ws_t = keep.tile([P, E * PASSES, N], U8, align_bytes=64, name="ws_t")
        b_t = keep.tile([P, HALVES, E], F32, name="b_t")
        y = [keep.tile([P, SLOTS], F32, name=f"y{h}") for h in range(HALVES)]
        gate_rows = keep.tile([P, P], F32, name="gate_rows")
        gate_by_token = keep.tile([P, (TOP - 1) * TURNED_BLOCKS], F32, name="gate_by_token")

        ident = keep.tile([P, P], F32, name="ident")
        make_identity(nc, ident[:])

        nc.gpsimd.memset(gate_rows[:], 0.0)
        nc.vector.memset(scales[:].bitcast(I32), 0)
        nc.vector.memset(ws_t[:].rearrange("p g n -> p (g n)").bitcast(I32), 0)
        nc.vector.memset(codes[:, PASSES * T :].bitcast(I32), 0)
        for c in range(SLOTS // BYTE_RUN):
            nc.vector.memset(slot_scales1[c][:].bitcast(I32), 0)

        def load_x(a, c):
            lo, n = X_LOADS[a][c]
            src = xT[512 * a : 512 * (a + 1), lo : lo + n].rearrange("(p j) w -> p j w", j=PACK)
            nc.sync.dma_start(out=raw[a][c][:], in_=src)

        for c in range(len(X_LOADS[0])):
            load_x(0, c)
        nc.sync.dma_start(offs_t[:], offs)
        for c in range(len(X_LOADS[1])):
            load_x(1, c)
        w_src = w_words.bitcast(I32).rearrange("e a p n -> p (e a) n")
        ws_src = w_scales.bitcast(I32)
        for q in range(P // QUADRANT):
            nc.sync.dma_start(
                out=ws_t[QUADRANT * q : QUADRANT * q + PACK].bitcast(I32),
                in_=ws_src[:, :, PACK * q : PACK * (q + 1), :].rearrange("e a r n -> r (e a) n"),
            )
        for r in (1, 2):
            rows = slice((r - 1) * TURNED_BLOCKS, r * TURNED_BLOCKS)
            nc.sync.dma_start(out=gate_rows[rows, :], in_=gate[r, 0, : TURNED_BLOCKS * P].rearrange("(c p) -> c p", p=P))
        nc.sync.dma_start(out=b_t[:], in_=b.rearrange("(h p) e -> p h e", p=P))
        first_run = BYTE_RUN // C * PASSES
        for g in (slice(0, first_run), slice(first_run, E * PASSES)):
            nc.sync.dma_start(out=w_t[:, g, :].bitcast(I32), in_=w_src[:, g, :])
        for r, src in enumerate((pos1, pos2, pos3)):
            nc.sync.dma_start(pos_t[r][:], src)

        gates_turned = bank(BANKS - 1, P)
        nc.tensor.transpose(gates_turned[:], gate_rows[:], ident[:])
        nc.scalar.copy(gate_by_token[:], gates_turned[:, 0 : (TOP - 1) * TURNED_BLOCKS])

        def cast(on_scalar, a, c, lo, hi):
            dst = grouped[a][c][:, lo:hi, :].rearrange("p (c i) j -> p c j i", i=4)
            src = raw[a][c][:, :, lo:hi].rearrange("p j (c i) -> p c j i", i=4)
            if on_scalar:
                nc.scalar.activation(dst, src, COPY)
            else:
                nc.vector.tensor_copy(out=dst, in_=src)

        def quantise(a, lo, n, src):
            nc.vector.quantize_mx(
                out=codes[:, first_word[a] + lo : first_word[a] + lo + n].bitcast(FP8X4),
                scales=scales[PACK * a : P, lo : lo + n],
                in_=src[:].rearrange("p w j -> p (w j)"),
            )

        for a in range(PASSES):
            for c, (lo, n) in enumerate(X_LOADS[a]):
                share = CAST_ON_SCALAR[a][c]
                cast(True, a, c, 0, share)
                if share < n:
                    cast(False, a, c, share, n)
                if a == 0:
                    quantise(a, lo, n, grouped[a][c])

        def gather_words(a, lo, n, buffer=None):
            dst = keep.tile([P, n], U32, align_bytes=64, name=buffer or f"slot_words{a}_{lo}")
            width = T if n < T else (T + SPARE_WORDS, PASSES * T)[a]
            window = codes[:, first_word[a] : first_word[a] + width]
            nc.vector.tensor_copy(dst[:], window.indirect(offs_t[:, lo // 16 : (lo + n) // 16]))
            for at in range(lo, lo + n, P):
                slot_words[a][at] = (dst, at - lo)

        def gather_scales(c):
            nc.vector.tensor_copy(slot_scales[c][:], scales[:].indirect(offs_t[:, BYTE_RUN * c // 16 : BYTE_RUN * (c + 1) // 16]))
            for q in range(0, P, QUADRANT):
                nc.sync.dma_start(
                    out=slot_scales1[c][q : q + PACK, :].bitcast(I32),
                    in_=slot_scales[c][q + PACK : q + 2 * PACK, :].bitcast(I32),
                )

        def one_pass(ps, h, lo, n, a, start, stop):
            g = lo // C * PASSES + a
            c, col = divmod(lo, BYTE_RUN)
            src, at = slot_words[a][lo]
            nc.tensor.matmul_mx(
                out=ps,
                lhsT=w_t[:, g, 2 * P * h : 2 * P * (h + 1)].bitcast(FP4X4),
                lhsT_scale=ws_t[:, g, P * h : P * (h + 1)],
                rhs=src[:, at : at + n].bitcast(FP8X4),
                rhs_scale=(slot_scales, slot_scales1)[a][c][:, col : col + n],
                start=start,
                stop=stop,
            )

        def open_group(number, parts):
            ps = bank(number, sum(n for h, lo, n in parts))
            views, at = [], 0
            for h, lo, n in parts:
                views.append(ps[:, at : at + n])
                one_pass(views[-1], h, lo, n, 0, at == 0, False)
                at = at + n
            return views, parts

        for_vector = []

        def close_group(views, parts):
            for k, (view, part) in enumerate(zip(views, parts)):
                one_pass(view, *part, 1, False, k == len(parts) - 1)
            for view, (h, lo, n) in zip(views, parts):
                e = lo // C
                dst, bias = y[h][:, lo : lo + n], b_t[:, h, e : e + 1]
                if h == 1 and e in HALF_1_ON_VECTOR:
                    for_vector.append((dst, view, bias))
                else:
                    nc.scalar.activation(dst, view, RELU, bias=bias)

        def open_expert(e):
            return open_group(e, [(h, e * C, C) for h in range(HALVES)])

        gather_words(0, 0, 5 * C)
        gather_words(0, 5 * C, 6 * C)
        for c, run in enumerate(runs):
            quantise(1, QUANTISE_RUN * c, QUANTISE_RUN, run)
        gather_words(0, SLOTS - C, C, buffer=f"raw1_{X_LOADS[1][-1][0]}")

        per_run = BYTE_RUN // C
        gather_scales(0)
        groups = [open_expert(e) for e in range(per_run)]
        gather_scales(1)
        groups.extend(open_expert(e) for e in range(per_run, 2 * per_run))
        gates = keep.tile([P, TOP, T], F32, align_bytes=64, name="slot_words0_0")
        alone = min(ALONE_FROM)
        nc.sync.dma_start(out=gates[:, 0, :], in_=gate[0, 0:P, :])
        nc.sync.dma_start(out=gates[:, 1:, alone:T], in_=gate[1:, 0:P, alone:T].rearrange("r p t -> p r t"))
        gather_words(1, 0, BYTE_RUN)
        for group in groups[:per_run]:
            close_group(*group)
        gather_scales(2)
        groups.extend(open_expert(e) for e in range(2 * per_run, E - 1))

        last_but_one, last = SLOTS - C, SLOTS - P
        groups.append(open_group(E - 1, [(h, last_but_one, P) for h in range(HALVES)]))
        for e in range(per_run, E - 1):
            if e % 2 == 0:
                gather_words(1, e * C, 2 * C if e < E - 2 else C)
            close_group(*groups[e])
            if e - per_run < HALVES:
                groups.append(open_group(e, [(e - per_run, last, P)]))
        gather_words(1, last_but_one, P)
        close_group(*groups[E - 1])
        gather_words(1, last, P)
        for group in groups[E:]:
            close_group(*group)
        for dst, view, bias in for_vector:
            nc.vector.tensor_scalar(dst, view, bias, 0.0, ADD, MAX)

        def picks(h, r, lo, hi):
            return y[h][:].indirect(pos_t[r][:, lo // 16 : hi // 16])

        choice = [[keep.tile([P, T], F32, name=f"choice{h}_{r}") for r in (1, 2)] for h in range(HALVES)]
        first = keep.tile([P, HALVES, T], F32, name="first")
        out_by_half = out.rearrange("(h p) t -> p h t", p=P)
        turned, back, written, returned = {}, {}, {}, {}

        def product(dst, h, r, lo, hi):
            nc.vector.tensor_tensor(dst, picks(h, r, lo, hi), gates[:, r, lo:hi], MULT)

        def add(dst, one, other):
            nc.vector.tensor_tensor(dst, one, other, ADD)

        def forward(h, r, start, end, into=None):
            if into is None:
                into = choice[h][r - 1][:, start:end]
            nc.scalar.activation(into, picks(h, r, start, end), COPY)
            for at in range(start, end, P):
                group = [g for g in TURN_GROUPS[r - 1] if (h, at) in g[1]][0]
                number, cells = group
                if (r, cells) not in turned:
                    turned[r, cells] = bank(number, len(cells) * P)
                count = written.setdefault((r, cells), [])
                count.append(at)
                col = cells.index((h, at)) * P
                nc.tensor.matmul(
                    turned[r, cells][:, col : col + P], into[:, at - start : at - start + P], ident[:],
                    start=len(count) == 1, stop=len(count) == len(cells), is_transpose=True,
                )

        def by_token_buffer(r, h, at, width):
            return keep.tile([P, width], F32, name=f"by_token{r}_{h}_{at}")

        def weigh_and_return(r, at, halves):
            cells = [g[1] for g in TURN_GROUPS[r - 1] if (halves[0], at) in g[1]][0]
            col = cells.index((halves[0], at)) * P
            weighed = by_token_buffer(r, halves[0], at, len(halves) * P)
            column = (r - 1) * TURNED_BLOCKS + at // P
            nc.scalar.activation(weighed[:], turned[r, cells][:, col : col + len(halves) * P], COPY, scale=gate_by_token[:, column : column + 1])
            for k, h in enumerate(halves):
                i = [n for n, (rows, lo, hi) in enumerate(TURNED) if h in rows and lo <= at < hi][0]
                rows, lo, hi = TURNED[i]
                if i not in back:
                    back[i] = bank(BACK_BANK[i], len(rows) * (hi - lo))
                count = returned.setdefault(i, [])
                count.append(at)
                to = rows.index(h) * (hi - lo) + at - lo
                nc.tensor.matmul(
                    back[i][:, to : to + P], weighed[:, k * P : (k + 1) * P], ident[:],
                    start=len(count) == 1, stop=len(count) == 2 * len(rows) * (hi - lo) // P, is_transpose=True,
                )

        def finish(i):
            halves, lo, hi = TURNED[i]
            rows = slice(halves[0], halves[-1] + 1)
            total = keep.tile([P, len(halves), hi - lo], F32, name=f"total{i}")
            add(total[:], back[i][:].rearrange("p (h t) -> p h t", h=len(halves)), first[:, rows, lo:hi])
            nc.sync.dma_start(out=out_by_half[:, rows, lo:hi], in_=total[:])

        both = (0, 1)
        forward(0, 1, 0, 512)
        forward(1, 1, 0, 512)
        forward(0, 2, 0, 512)
        weigh_and_return(1, 0, both)
        weigh_and_return(1, 128, both)
        forward(1, 2, 0, 640, into=choice[1][0][:, 0:640])
        weigh_and_return(1, 256, both)
        weigh_and_return(1, 384, both)
        forward(0, 2, 512, 768, into=choice[0][1][:, 0:256])
        weigh_and_return(2, 0, both)
        weigh_and_return(2, 128, both)
        weigh_and_return(2, 256, both)
        weigh_and_return(2, 384, both)
        forward(0, 1, 512, 768, into=choice[1][0][:, 256:512])
        forward(1, 1, 512, 640)
        weigh_and_return(2, 512, both)
        weigh_and_return(2, 640, (0,))
        weigh_and_return(1, 512, (0,))
        weigh_and_return(1, 640, (0,))
        weigh_and_return(1, 512, (1,))

        upper, lower = ALONE_FROM
        for h in range(HALVES):
            product(first[:, h, :], h, 0, 0, T)
        lower_1, lower_2 = (choice[1][r][:, lower:T] for r in range(2))
        product(lower_1, 1, 1, lower, T)
        product(lower_2, 1, 2, lower, T)
        add(lower_1, first[:, 1, lower:T], lower_1)
        upper_1, upper_2 = (choice[0][r][:, upper:T] for r in range(2))
        product(upper_1, 0, 1, upper, T)
        product(upper_2, 0, 2, upper, T)
        nc.gpsimd.tensor_tensor(upper_2, upper_2, first[:, 0, upper:T], ADD)
        finish(0)
        finish(1)
        sums = by_token_buffer(2, 0, 384, 2 * T - lower - upper)
        lower_sum, upper_sum = sums[:, : T - lower], sums[:, T - lower :]
        add(lower_sum, lower_1, lower_2)
        nc.sync.dma_start(out=out[P:N, lower:T], in_=lower_sum)
        add(upper_sum, upper_1, upper_2)
        nc.sync.dma_start(out=out[0:P, upper:T], in_=upper_sum)
        finish(2)
        finish(3)
